import numpy as np
import ml_dtypes


def mxq(x, axis, fmt="e4m3"):
    dtype, down = {"e4m3": (ml_dtypes.float8_e4m3fn, 7), "e5m2": (ml_dtypes.float8_e5m2, 14)}[fmt]
    v = np.moveaxis(np.asarray(x, np.float32).astype(ml_dtypes.bfloat16).astype(np.float64), axis, -1)
    blocks = v.reshape(v.shape[:-1] + (-1, 32))
    amax = np.abs(blocks).max(-1, keepdims=True)
    byte = np.maximum(np.where(amax > 0, np.frexp(amax)[1] - 1 + 127, 0) - down, 1)
    scale = np.exp2(byte - 127.0)
    codes = (blocks / scale).astype(np.float32).astype(dtype).astype(np.float64)
    return np.moveaxis((codes * scale).reshape(v.shape), -1, axis)


WIDE = False


def mx_kscale(k):
    if not WIDE:
        return np.ones(k)
    levels = np.array([10, -10, 5, -5, 0])
    if k % 512:
        return np.exp2(np.random.permutation(np.resize(levels, k // 32))).repeat(32)
    a = np.empty((k // 512, 16))
    for p in range(k // 512):
        a[p, :8] = np.random.permutation(np.resize(levels, 8))
        for g in range(8):
            far = levels[np.abs(levels - a[p, g]) >= 10]
            a[p, g + 8] = far[np.random.randint(len(far))]
    return np.exp2(a.ravel()).repeat(32)


BF16 = ml_dtypes.bfloat16


def bf(x):
    return np.asarray(x, np.float32).astype(BF16)


def f64(x):
    return np.asarray(x).astype(np.float64)


B, S, R, D, E, T = 16, 512, 256, 512, 256, 2


def draw0():
    s, t = mx_kscale(S), mx_kscale(D)
    return {
        "x": bf(np.random.standard_normal((B, S, D)) * s[:, None]),
        "mp": bf(np.random.standard_normal((R, S)) / np.sqrt(S) / s[None, :]),
        "mq": bf(np.random.standard_normal((R, S)) / np.sqrt(S) / s[None, :]),
        "mr": bf(np.random.standard_normal((R, S)) / np.sqrt(S) / s[None, :]),
        "coef": bf(np.random.uniform(0.4, 1.0, (T, D))),
        "gain": bf((1.0 + 0.1 * np.random.standard_normal(D)) * t),
        "wo": bf(np.random.standard_normal((D, E)) / np.sqrt(D) / t[:, None]),
    }


def mix_time(m, xq):
    return mxq(f64(m), 1, "e4m3") @ xq


def core(x, mp, mq, mr, coef, gain, wo):
    c = f64(coef)
    xq = mxq(f64(x), 1, "e4m3")
    p = mix_time(mp, xq)
    q = mix_time(mq, xq)
    r = mix_time(mr, xq)
    h = c[0] + c[1] * r
    y = p * (1.0 + q * h)
    z = y * f64(gain)
    return mxq(z, 2, "e4m3") @ mxq(f64(wo), 0, "e4m3")


def e4m3fn_bytes(y):
    return np.clip(np.asarray(y, np.float64), -448.0, 448.0).astype(np.float32).astype(ml_dtypes.float8_e4m3fn).view(np.uint8)


def e4m3fn_values(b):
    return np.asarray(b, np.uint8).view(ml_dtypes.float8_e4m3fn).astype(np.float64)


def setup_inputs():
    d = draw0()
    x0 = np.asarray(d['x']).astype(np.float64)
    s = (np.max(np.abs(x0), axis=(0, 2), keepdims=True) / 448.0).astype(np.float32)
    out = {}
    for k, v in d.items():
        if k == 'x':
            out['x_bytes'] = e4m3fn_bytes(x0 / s.astype(np.float64))
            out['x_scale'] = s
        else:
            out[k] = v
    return out


def reference(x_bytes, x_scale, mp, mq, mr, coef, gain, wo):
    return core(e4m3fn_values(x_bytes) * x_scale.astype(np.float64), mp, mq, mr, coef, gain, wo)

@@ -1,0 +1,359 @@
+from contextlib import ExitStack
+
+import concourse.mybir as mybir
+from concourse.masks import make_identity
+
+NB, S, D, T, E = 16, 512, 512, 256, 256
+P = 128
+FLOPS = NB * (2 * 3 * T * S * D + 2 * T * D * E)
+
+F32 = mybir.dt.float32
+BF16 = mybir.dt.bfloat16
+U32 = mybir.dt.uint32
+U8 = mybir.dt.uint8
+FP8 = mybir.dt.float8_e4m3fn
+X4 = mybir.dt.float8_e4m3fn_x4
+COPY = mybir.ActivationFunctionType.Copy
+IDENTITY = mybir.ActivationFunctionType.Identity
+ADD = mybir.AluOpType.add
+MULT = mybir.AluOpType.mult
+
+STEPS = 2 * NB
+SINGLE = 4
+LAST = NB - 1
+DIRECT = NB - 3
+
+
+def tile_volterrathirdordermixer_t_kernel(tc, x_bytes, x_scale, mp, mq, mr, coef, gain, wo, out):
+    nc = tc.nc
+    with ExitStack() as ctx:
+        const = ctx.enter_context(tc.tile_pool(name="const", bufs=1))
+        bytes_pool = ctx.enter_context(tc.tile_pool(name="bytes_pool", bufs=8))
+        wide_pool = ctx.enter_context(tc.tile_pool(name="wide_pool", bufs=3))
+        x_pool = ctx.enter_context(tc.tile_pool(name="x_pool", bufs=3))
+        xq_pool = ctx.enter_context(tc.tile_pool(name="xq_pool", bufs=5))
+        poly = ctx.enter_context(tc.tile_pool(name="poly", bufs=3))
+        z_pool = ctx.enter_context(tc.tile_pool(name="z_pool", bufs=3))
+        zq_pool = ctx.enter_context(tc.tile_pool(name="zq_pool", bufs=4))
+        out_pool = ctx.enter_context(tc.tile_pool(name="out_pool", bufs=4))
+        psum = ctx.enter_context(tc.psum_pool(name="psum", bufs=2))
+        ctx.enter_context(tc.manual_schedule())
+
+        x_raw = {}
+
+        def load_x(b, width):
+            codes = bytes_pool.tile([P, 4, width, D], U8, name="codes%d" % width, align_bytes=64)
+            for k in range(width):
+                nc.sync.dma_start(out=codes[:, :, k, :], in_=x_bytes[b + k].rearrange("(p t) d -> p t d", t=4))
+            x_raw[b] = codes
+
+        load_x(0, 1)
+        scale = const.tile([P, 4], F32, name="scale", align_bytes=64)
+        nc.sync.dma_start(out=scale[:], in_=x_scale.rearrange("o (p t) z -> p (o t z)", t=4))
+
+        vec_rows = const.tile([P, P], BF16, name="vec_rows", align_bytes=64)
+        first_act = const.tile([P, 1], F32, name="first_act")
+        nc.vector.memset(vec_rows[:], 0.0)
+        nc.vector.memset(first_act[:], 0.0)
+        for v, vec in enumerate((coef[0], coef[1], gain)):
+            nc.sync.dma_start(
+                out=vec_rows[4 * v : 4 * v + 4, :].rearrange("p (g i) -> p g i", i=8),
+                in_=vec.rearrange("(g j i) -> j g i", j=4, i=8),
+            )
+        m_raw = []
+        for i, m in enumerate((mr, mq, mp)):
+            m_rows = const.tile([P, 2, S], BF16, name="m_rows%d" % i, align_bytes=64)
+            nc.sync.dma_start(out=m_rows[:], in_=m.rearrange("(p c) k -> p c k", c=2))
+            m_raw.append(m_rows)
+        for b in range(1, SINGLE):
+            load_x(b, 1)
+
+        nc.scalar.activation(out=first_act[:], in_=first_act[:], func=IDENTITY)
+        ident_f32 = const.tile([P, P], F32, name="ident_f32", align_bytes=64)
+        make_identity(nc, ident_f32[:])
+        ident_bf16 = const.tile([P, P], BF16, name="ident_bf16", align_bytes=64)
+
+        wo_rows = const.tile([P, 4, E], BF16, name="wo_rows", align_bytes=64)
+        for g in range(16):
+            nc.sync.dma_start(
+                out=wo_rows[8 * g : 8 * g + 8, :, :],
+                in_=wo[32 * g : 32 * g + 32, :].rearrange("(j i) e -> i j e", i=8),
+            )
+        for b in range(SINGLE, NB, 2):
+            load_x(b, 2)
+
+        x_wide, x_rows, x_words, x_codes, x_scales = {}, {}, {}, {}, {}
+
+        def widen(engine, b, t):
+            width = 1 if b < SINGLE else 2
+            if b not in x_wide:
+                wide = wide_pool.tile([P, 4, width, D], BF16, name="wide%d" % width, align_bytes=64)
+                x_wide[b] = wide
+                for k in range(width):
+                    x_rows[b + k] = wide[:, :, k, :]
+            dst = x_wide[b][:, t, :, :].rearrange("p b d -> p (b d)")
+            src = x_raw[b][:, t, :, :].rearrange("p b d -> p (b d)").bitcast(FP8)
+            if engine == "scalar":
+                nc.scalar.activation(out=dst, in_=src, func=COPY, scale=scale[:, t : t + 1])
+            else:
+                nc.vector.tensor_scalar(out=dst, in0=src, scalar1=scale[:, t : t + 1], scalar2=None, op0=MULT)
+
+        def interleave_x(b):
+            words = x_pool.tile([P, 4 * D], BF16, name="words", align_bytes=64)
+            nc.vector.tensor_copy(
+                out=words[:].rearrange("p (j g i t) -> p g j t i", j=4, g=16, i=8, t=4),
+                in_=x_rows[b].rearrange("p t (g j i) -> p g j t i", g=16, j=4, i=8),
+            )
+            x_words[b] = words
+
+        def quantize_x(b):
+            codes = xq_pool.tile([P, D], U32, name="x_q", align_bytes=64)
+            scales = xq_pool.tile([P, D], U8, name="x_qs", align_bytes=64)
+            nc.vector.quantize_mx(out=codes[:].bitcast(X4), scales=scales[:], in_=x_words[b][:])
+            x_codes[b], x_scales[b] = codes, scales
+
+        m_words, m_codes, m_scales = [], [], []
+
+        def turn_m(i):
+            turned = psum.tile([P, 2, 2, P], F32, name="turned", tag="RQP"[i])
+            for c in range(2):
+                words = m_raw[i][:, c, :].bitcast(F32)
+                for u in range(2):
+                    nc.tensor.transpose(turned[:, c, u, :], words[:, u : S // 2 : 2], ident_f32[:])
+            grouped = const.tile([P, T, 4], BF16, name="m_words%d" % i, align_bytes=64)
+            dst = grouped[:].rearrange("p n t -> p (n t)").bitcast(F32)
+            nc.scalar.copy(
+                out=dst.rearrange("p (c n u) -> p c n u", c=2, u=2), in_=turned[:].rearrange("p c u n -> p c n u")
+            )
+            m_words.append(grouped)
+
+        def quantize_m(i):
+            codes = const.tile([P, T], U32, name="m_q%d" % i, align_bytes=64)
+            scales = const.tile([P, T], U8, name="m_qs%d" % i, align_bytes=64)
+            nc.vector.quantize_mx(
+                out=codes[:].bitcast(X4), scales=scales[:], in_=m_words[i][:].rearrange("p n t -> p (n t)")
+            )
+            m_codes.append(codes)
+            m_scales.append(scales)
+
+        r_sum, q_sum, p_sum, h_val, u_val, z_tile = {}, {}, {}, {}, {}, {}
+
+        def products(n):
+            b, j0 = n // 2, 2 * (n % 2)
+            r_ps = psum.tile([P, 2, T], F32, name="r_ps", tag="R")
+            q_ps = psum.tile([P, 2, T], F32, name="q_ps", tag="Q")
+            p_ps = psum.tile([P, 2, T], F32, name="p_ps", tag="P")
+            for i, ps in enumerate((r_ps, q_ps, p_ps)):
+                for k in range(2):
+                    cols = slice((j0 + k) * P, (j0 + k + 1) * P)
+                    nc.tensor.matmul_mx(
+                        out=ps[:, k, :],
+                        lhsT=x_codes[b][:, cols].bitcast(X4),
+                        lhsT_scale=x_scales[b][:, cols],
+                        rhs=m_codes[i][:].bitcast(X4),
+                        rhs_scale=m_scales[i][:],
+                        start=True,
+                        stop=True,
+                    )
+            r_sum[n], q_sum[n], p_sum[n] = r_ps, q_ps, p_ps
+
+        def third_order(n):
+            h = poly.tile([P, 2, T], F32, name="h", align_bytes=64)
+            for k in range(2):
+                j = 2 * (n % 2) + k
+                nc.scalar.activation(
+                    out=h[:, k, :],
+                    in_=r_sum[n][:, k, :],
+                    func=IDENTITY,
+                    bias=gain_coef[:, j : j + 1],
+                    scale=gain_coef[:, 4 + j : 5 + j],
+                )
+            h_val[n] = h
+
+        def times_q(n):
+            u = poly.tile([P, 2, T], F32, name="u", align_bytes=64)
+            nc.vector.tensor_tensor(out=u[:], in0=h_val[n][:], in1=q_sum[n][:], op=MULT)
+            u_val[n] = u
+
+        def times_p(n):
+            b = n // 2
+            if n % 2 == 0:
+                z_rows = z_pool.tile([P, 4, T], BF16, name="z_rows", align_bytes=64)
+                z_tile[b] = z_rows
+            for k in range(2):
+                j = 2 * (n % 2) + k
+                nc.vector.scalar_tensor_tensor(
+                    out=z_tile[b][:, j, :],
+                    in0=u_val[n][:, k, :],
+                    scalar=vec_cols[:, 8 + j : 9 + j],
+                    in1=p_sum[n][:, k, :],
+                    op0=ADD,
+                    op1=MULT,
+                )
+
+        z_turned, z_words, z_codes, z_scales, out_sum = {}, {}, {}, {}, {}
+
+        def turn_z(b):
+            turned = psum.tile([P, T, 4], BF16, name="z_turned", tag="O")
+            for c in range(2):
+                t = slice(c * P, (c + 1) * P)
+                nc.tensor.matmul(
+                    turned[:, t, :].rearrange("p t j -> p j t"),
+                    lhsT=ident_bf16[:],
+                    rhs=z_tile[b][:, :, t],
+                    start=True,
+                    stop=True,
+                )
+            z_turned[b] = turned
+
+        def fetch_z(b):
+            words = zq_pool.tile([P, T, 4], BF16, name="z_words", align_bytes=64)
+            if b == DIRECT:
+                nc.scalar.copy(out=words[:], in_=z_tile[b][:].rearrange("p j t -> p t j"))
+            else:
+                nc.scalar.copy(
+                    out=words[:].rearrange("p t j -> p (t j)"), in_=z_turned[b][:].rearrange("p t j -> p (t j)")
+                )
+            z_words[b] = words
+
+        def quantize_z(b):
+            codes = zq_pool.tile([P, T], U32, name="z_q", align_bytes=64)
+            scales = zq_pool.tile([P, T], U8, name="z_qs", align_bytes=64)
+            nc.vector.quantize_mx(
+                out=codes[:].bitcast(X4), scales=scales[:], in_=z_words[b][:].rearrange("p t j -> p (t j)")
+            )
+            z_codes[b], z_scales[b] = codes, scales
+
+        def project(b):
+            o_ps = psum.tile([P, 2, E], F32, name="o_ps", tag="O")
+            for c in range(2):
+                cols = slice(c * P, (c + 1) * P)
+                nc.tensor.matmul_mx(
+                    out=o_ps[:, c, :],
+                    lhsT=z_codes[b][:, cols].bitcast(X4),
+                    lhsT_scale=z_scales[b][:, cols],
+                    rhs=wo_codes[:].bitcast(X4),
+                    rhs_scale=wo_scales[:],
+                    start=True,
+                    stop=True,
+                )
+            out_sum[b] = o_ps
+
+        def store(b):
+            o_sb = out_pool.tile([P, 2, E], F32, name="o_sb", align_bytes=64)
+            nc.scalar.copy(out=o_sb[:], in_=out_sum[b][:])
+            nc.sync.dma_start(out=out[b].rearrange("(p c) e -> p c e", c=2), in_=o_sb[:])
+
+        vec_cols = const.tile([P, 12], F32, name="vec_cols", align_bytes=64)
+        gain_coef = const.tile([P, 8], F32, name="gain_coef", align_bytes=64)
+        vec_ps = psum.tile([P, P], BF16, name="vec_ps", tag="O")
+        nc.vector.tensor_copy(out=ident_bf16[:], in_=ident_f32[:])
+        for t in (1, 2, 3):
+            widen("vector", 0, t)
+        widen("scalar", 0, 0)
+        turn_m(0)
+        interleave_x(0)
+        nc.tensor.transpose(vec_ps[:], vec_rows[:], ident_bf16[:])
+        turn_m(1)
+        nc.vector.tensor_copy(out=vec_cols[:], in_=vec_ps[:, 0:12])
+        quantize_m(0)
+        quantize_x(0)
+        nc.vector.tensor_tensor(out=gain_coef[:, 0:4], in0=vec_cols[:, 0:4], in1=vec_cols[:, 8:12], op=MULT)
+        nc.vector.tensor_tensor(out=gain_coef[:, 4:8], in0=vec_cols[:, 4:8], in1=vec_cols[:, 8:12], op=MULT)
+        turn_m(2)
+        quantize_m(1)
+        widen("vector", 1, 0)
+        widen("vector", 1, 1)
+        quantize_m(2)
+        widen("vector", 1, 2)
+        widen("vector", 1, 3)
+
+        wo_words = const.tile([P, E, 4], BF16, name="wo_words", align_bytes=64)
+        wo_codes = const.tile([P, E], U32, name="wo_q", align_bytes=64)
+        wo_scales = const.tile([P, E], U8, name="wo_qs", align_bytes=64)
+
+        products(0)
+        third_order(0)
+        for t in (0, 1, 2):
+            widen("scalar", 2, t)
+        interleave_x(1)
+        products(1)
+        third_order(1)
+        widen("scalar", 2, 3)
+        for t in range(4):
+            widen("scalar", 3, t)
+        times_q(0)
+        quantize_x(1)
+        interleave_x(2)
+
+        for n in range(STEPS):
+            even = n % 2 == 0
+            if n + 1 < STEPS:
+                times_q(n + 1)
+            times_p(n)
+
+            if n == 0:
+                nc.vector.tensor_copy(out=wo_words[:], in_=wo_rows[:].rearrange("p j e -> p e j"))
+            if n == 2:
+                nc.vector.quantize_mx(
+                    out=wo_codes[:].bitcast(X4), scales=wo_scales[:], in_=wo_words[:].rearrange("p e j -> p (e j)")
+                )
+            if not even and (n + 3) // 2 < NB:
+                quantize_x((n + 3) // 2)
+            if not even and (n + 5) // 2 < NB:
+                interleave_x((n + 5) // 2)
+            if even and n >= 4:
+                quantize_z((n - 4) // 2)
+
+            if n + 2 < STEPS:
+                products(n + 2)
+                third_order(n + 2)
+
+            if even and n >= 2:
+                fetch_z((n - 2) // 2)
+            if not even and n >= 5:
+                store((n - 5) // 2)
+            if n == 0:
+                widen("scalar", SINGLE, 0)
+            t = (n + 1) % 4
+            pair = (n + 9 - t) // 2
+            if pair < NB:
+                widen("scalar", pair, t)
+
+            if not even and n // 2 not in (DIRECT, LAST):
+                turn_z(n // 2)
+            if even and n >= 4:
+                project((n - 4) // 2)
+
+        quantize_z(LAST - 1)
+        project(LAST - 1)
+        store(LAST - 1)
+        half_words = []
+        for c in range(2):
+            words = zq_pool.tile([P, P, 4], BF16, name="half_words%d" % c, align_bytes=64)
+            nc.vector.tensor_copy(
+                out=words[:], in_=z_tile[LAST][:, :, c * P : (c + 1) * P].rearrange("p j t -> p t j")
+            )
+            half_words.append(words)
+        for c in range(2):
+            codes = zq_pool.tile([P, P], U32, name="half_q%d" % c, align_bytes=64)
+            scales = zq_pool.tile([P, P], U8, name="half_qs%d" % c, align_bytes=64)
+            nc.vector.quantize_mx(
+                out=codes[:].bitcast(X4), scales=scales[:], in_=half_words[c][:].rearrange("p t j -> p (t j)")
+            )
+            half_ps = psum.tile([P, E], F32, name="half_ps", tag="O")
+            nc.tensor.matmul_mx(
+                out=half_ps[:],
+                lhsT=codes[:].bitcast(X4),
+                lhsT_scale=scales[:],
+                rhs=wo_codes[:].bitcast(X4),
+                rhs_scale=wo_scales[:],
+                start=True,
+                stop=True,
+            )
+            half_sb = out_pool.tile([P, E], F32, name="half_sb%d" % c, align_bytes=64)
+            if c == 0:
+                nc.scalar.copy(out=half_sb[:], in_=half_ps[:])
+            else:
+                nc.vector.tensor_copy(out=half_sb[:], in_=half_ps[:])
+            nc.sync.dma_start(out=out[LAST].rearrange("(p c) e -> p c e", c=2)[:, c, :], in_=half_sb[:])

@@ -20,8 +20,9 @@ MULT = mybir.AluOpType.mult
 
 STEPS = 2 * NB
 SINGLE = 4
+HEAD = 2
 LAST = NB - 1
-DIRECT = NB - 3
+TURNED = NB - 3
 
 
 def tile_volterrathirdordermixer_t_kernel(tc, x_bytes, x_scale, mp, mq, mr, coef, gain, wo, out):
@@ -29,8 +30,8 @@ def tile_volterrathirdordermixer_t_kernel(tc, x_bytes, x_scale, mp, mq, mr, coef
     with ExitStack() as ctx:
         const = ctx.enter_context(tc.tile_pool(name="const", bufs=1))
         bytes_pool = ctx.enter_context(tc.tile_pool(name="bytes_pool", bufs=8))
-        wide_pool = ctx.enter_context(tc.tile_pool(name="wide_pool", bufs=3))
-        x_pool = ctx.enter_context(tc.tile_pool(name="x_pool", bufs=3))
+        wide_pool = ctx.enter_context(tc.tile_pool(name="wide_pool", bufs=4))
+        x_pool = ctx.enter_context(tc.tile_pool(name="x_pool", bufs=1))
         xq_pool = ctx.enter_context(tc.tile_pool(name="xq_pool", bufs=5))
         poly = ctx.enter_context(tc.tile_pool(name="poly", bufs=3))
         z_pool = ctx.enter_context(tc.tile_pool(name="z_pool", bufs=3))
@@ -42,75 +43,90 @@ def tile_volterrathirdordermixer_t_kernel(tc, x_bytes, x_scale, mp, mq, mr, coef
         x_raw = {}
 
         def load_x(b, width):
-            codes = bytes_pool.tile([P, 4, width, D], U8, name="codes%d" % width, align_bytes=64)
+            codes = bytes_pool.tile([P, width, 4 * D], U8, name="codes%d" % width, align_bytes=64)
+            nc.sync.dma_start(out=codes[:], in_=x_bytes[b : b + width].rearrange("k (p t) d -> p k (t d)", t=4))
             for k in range(width):
-                nc.sync.dma_start(out=codes[:, :, k, :], in_=x_bytes[b + k].rearrange("(p t) d -> p t d", t=4))
-            x_raw[b] = codes
+                x_raw[b + k] = codes[:, k, :]
 
         load_x(0, 1)
         scale = const.tile([P, 4], F32, name="scale", align_bytes=64)
         nc.sync.dma_start(out=scale[:], in_=x_scale.rearrange("o (p t) z -> p (o t z)", t=4))
 
+        m_raw = []
+
+        def load_m(m):
+            m_rows = const.tile([P, 2, S], BF16, name="m_rows%d" % len(m_raw), align_bytes=64)
+            nc.sync.dma_start(out=m_rows[:], in_=m.rearrange("(p c) k -> p c k", c=2))
+            m_raw.append(m_rows)
+
+        load_m(mr)
+        load_m(mq)
         vec_rows = const.tile([P, P], BF16, name="vec_rows", align_bytes=64)
-        first_act = const.tile([P, 1], F32, name="first_act")
         nc.vector.memset(vec_rows[:], 0.0)
-        nc.vector.memset(first_act[:], 0.0)
         for v, vec in enumerate((coef[0], coef[1], gain)):
             nc.sync.dma_start(
                 out=vec_rows[4 * v : 4 * v + 4, :].rearrange("p (g i) -> p g i", i=8),
                 in_=vec.rearrange("(g j i) -> j g i", j=4, i=8),
             )
-        m_raw = []
-        for i, m in enumerate((mr, mq, mp)):
-            m_rows = const.tile([P, 2, S], BF16, name="m_rows%d" % i, align_bytes=64)
-            nc.sync.dma_start(out=m_rows[:], in_=m.rearrange("(p c) k -> p c k", c=2))
-            m_raw.append(m_rows)
-        for b in range(1, SINGLE):
+        load_x(1, 1)
+        load_m(mp)
+        for b in range(2, SINGLE):
             load_x(b, 1)
 
-        nc.scalar.activation(out=first_act[:], in_=first_act[:], func=IDENTITY)
         ident_f32 = const.tile([P, P], F32, name="ident_f32", align_bytes=64)
         make_identity(nc, ident_f32[:])
         ident_bf16 = const.tile([P, P], BF16, name="ident_bf16", align_bytes=64)
+        nc.scalar.activation(out=ident_bf16[:], in_=ident_f32[:], func=COPY)
 
         wo_rows = const.tile([P, 4, E], BF16, name="wo_rows", align_bytes=64)
-        for g in range(16):
-            nc.sync.dma_start(
-                out=wo_rows[8 * g : 8 * g + 8, :, :],
-                in_=wo[32 * g : 32 * g + 32, :].rearrange("(j i) e -> i j e", i=8),
-            )
-        for b in range(SINGLE, NB, 2):
+        load_x(SINGLE, 2)
+        for i in range(8):
+            nc.sync.dma_start(out=wo_rows[i:P:8, :, :], in_=wo.rearrange("(g j i) e -> i g j e", j=4, i=8)[i])
+        for b in range(SINGLE + 2, NB, 2):
             load_x(b, 2)
 
-        x_wide, x_rows, x_words, x_codes, x_scales = {}, {}, {}, {}, {}
+        x_wide, x_words, x_codes, x_scales = {}, {}, {}, {}
 
         def widen(engine, b, t):
-            width = 1 if b < SINGLE else 2
             if b not in x_wide:
-                wide = wide_pool.tile([P, 4, width, D], BF16, name="wide%d" % width, align_bytes=64)
+                wide = wide_pool.tile([P, 4, D], BF16, name="wide", align_bytes=64)
                 x_wide[b] = wide
-                for k in range(width):
-                    x_rows[b + k] = wide[:, :, k, :]
-            dst = x_wide[b][:, t, :, :].rearrange("p b d -> p (b d)")
-            src = x_raw[b][:, t, :, :].rearrange("p b d -> p (b d)").bitcast(FP8)
+            dst = x_wide[b][:, t, :]
+            src = x_raw[b][:, t * D : (t + 1) * D].bitcast(FP8)
             if engine == "scalar":
                 nc.scalar.activation(out=dst, in_=src, func=COPY, scale=scale[:, t : t + 1])
             else:
                 nc.vector.tensor_scalar(out=dst, in0=src, scalar1=scale[:, t : t + 1], scalar2=None, op0=MULT)
 
-        def interleave_x(b):
-            words = x_pool.tile([P, 4 * D], BF16, name="words", align_bytes=64)
-            nc.vector.tensor_copy(
-                out=words[:].rearrange("p (j g i t) -> p g j t i", j=4, g=16, i=8, t=4),
-                in_=x_rows[b].rearrange("p t (g j i) -> p g j t i", g=16, j=4, i=8),
-            )
-            x_words[b] = words
-
-        def quantize_x(b):
+        def new_x_words(b):
+            words = x_pool.tile([P, 4 * D], BF16, name="words%d" % min(b, 1), align_bytes=64)
             codes = xq_pool.tile([P, D], U32, name="x_q", align_bytes=64)
             scales = xq_pool.tile([P, D], U8, name="x_qs", align_bytes=64)
-            nc.vector.quantize_mx(out=codes[:].bitcast(X4), scales=scales[:], in_=x_words[b][:])
-            x_codes[b], x_scales[b] = codes, scales
+            x_words[b], x_codes[b], x_scales[b] = words, codes, scales
+
+        def interleave_x_vector(b, j0, j1):
+            nc.vector.tensor_copy(
+                out=x_words[b][:].rearrange("p (j g i t) -> p g j t i", j=4, g=16, i=8, t=4)[:, :, j0:j1],
+                in_=x_wide[b][:].rearrange("p t (g j i) -> p g j t i", g=16, j=4, i=8)[:, :, j0:j1],
+            )
+
+        def interleave_x_gpsimd(b):
+            nc.gpsimd.tensor_scalar(
+                out=x_words[b][:].rearrange("p (j g i t) -> p g j i t", j=4, g=16, i=8, t=4),
+                in0=x_wide[b][:].rearrange("p t (g j i) -> p g j i t", g=16, j=4, i=8),
+                scalar1=1.0,
+                scalar2=0.0,
+                op0=MULT,
+                op1=ADD,
+            )
+
+        def quantize_x(b, j0, j1):
+            cols = slice(j0 * P, j1 * P)
+            nc.vector.quantize_mx(
+                out=x_codes[b][:, cols].bitcast(X4),
+                scales=x_scales[b][:, cols],
+                in_=x_words[b][:, 4 * j0 * P : 4 * j1 * P],
+            )
 
         m_words, m_codes, m_scales = [], [], []
 
@@ -136,14 +152,13 @@ def tile_volterrathirdordermixer_t_kernel(tc, x_bytes, x_scale, mp, mq, mr, coef
             m_codes.append(codes)
             m_scales.append(scales)
 
-        r_sum, q_sum, p_sum, h_val, u_val, z_tile = {}, {}, {}, {}, {}, {}
+        sums, h_val, u_val, z_tile = {}, {}, {}, {}
 
-        def products(n):
+        def products(n, names):
             b, j0 = n // 2, 2 * (n % 2)
-            r_ps = psum.tile([P, 2, T], F32, name="r_ps", tag="R")
-            q_ps = psum.tile([P, 2, T], F32, name="q_ps", tag="Q")
-            p_ps = psum.tile([P, 2, T], F32, name="p_ps", tag="P")
-            for i, ps in enumerate((r_ps, q_ps, p_ps)):
+            for name in names:
+                i = "RQP".index(name)
+                ps = psum.tile([P, 2, T], F32, name="sum_ps", tag=name)
                 for k in range(2):
                     cols = slice((j0 + k) * P, (j0 + k + 1) * P)
                     nc.tensor.matmul_mx(
@@ -155,7 +170,7 @@ def tile_volterrathirdordermixer_t_kernel(tc, x_bytes, x_scale, mp, mq, mr, coef
                         start=True,
                         stop=True,
                     )
-            r_sum[n], q_sum[n], p_sum[n] = r_ps, q_ps, p_ps
+                sums[name, n] = ps
 
         def third_order(n):
             h = poly.tile([P, 2, T], F32, name="h", align_bytes=64)
@@ -163,7 +178,7 @@ def tile_volterrathirdordermixer_t_kernel(tc, x_bytes, x_scale, mp, mq, mr, coef
                 j = 2 * (n % 2) + k
                 nc.scalar.activation(
                     out=h[:, k, :],
-                    in_=r_sum[n][:, k, :],
+                    in_=sums["R", n][:, k, :],
                     func=IDENTITY,
                     bias=gain_coef[:, j : j + 1],
                     scale=gain_coef[:, 4 + j : 5 + j],
@@ -172,7 +187,7 @@ def tile_volterrathirdordermixer_t_kernel(tc, x_bytes, x_scale, mp, mq, mr, coef
 
         def times_q(n):
             u = poly.tile([P, 2, T], F32, name="u", align_bytes=64)
-            nc.vector.tensor_tensor(out=u[:], in0=h_val[n][:], in1=q_sum[n][:], op=MULT)
+            nc.vector.tensor_tensor(out=u[:], in0=h_val[n][:], in1=sums["Q", n][:], op=MULT)
             u_val[n] = u
 
         def times_p(n):
@@ -186,7 +201,7 @@ def tile_volterrathirdordermixer_t_kernel(tc, x_bytes, x_scale, mp, mq, mr, coef
                     out=z_tile[b][:, j, :],
                     in0=u_val[n][:, k, :],
                     scalar=vec_cols[:, 8 + j : 9 + j],
-                    in1=p_sum[n][:, k, :],
+                    in1=sums["P", n][:, k, :],
                     op0=ADD,
                     op1=MULT,
                 )
@@ -206,14 +221,22 @@ def tile_volterrathirdordermixer_t_kernel(tc, x_bytes, x_scale, mp, mq, mr, coef
                 )
             z_turned[b] = turned
 
-        def fetch_z(b):
+        def fetch_z(b, engine):
             words = zq_pool.tile([P, T, 4], BF16, name="z_words", align_bytes=64)
-            if b == DIRECT:
-                nc.scalar.copy(out=words[:], in_=z_tile[b][:].rearrange("p j t -> p t j"))
-            else:
-                nc.scalar.copy(
-                    out=words[:].rearrange("p t j -> p (t j)"), in_=z_turned[b][:].rearrange("p t j -> p (t j)")
+            dst = words[:].rearrange("p t j -> p (t j)")
+            if engine == "gpsimd":
+                nc.gpsimd.tensor_scalar(
+                    out=words[:],
+                    in0=z_tile[b][:].rearrange("p j t -> p t j"),
+                    scalar1=1.0,
+                    scalar2=0.0,
+                    op0=MULT,
+                    op1=ADD,
                 )
+            elif engine == "scalar":
+                nc.scalar.copy(out=dst, in_=z_turned[b][:].rearrange("p t j -> p (t j)"))
+            else:
+                nc.vector.tensor_copy(out=dst, in_=z_turned[b][:].rearrange("p t j -> p (t j)"))
             z_words[b] = words
 
         def quantize_z(b):
@@ -247,84 +270,97 @@ def tile_volterrathirdordermixer_t_kernel(tc, x_bytes, x_scale, mp, mq, mr, coef
         vec_cols = const.tile([P, 12], F32, name="vec_cols", align_bytes=64)
         gain_coef = const.tile([P, 8], F32, name="gain_coef", align_bytes=64)
         vec_ps = psum.tile([P, P], BF16, name="vec_ps", tag="O")
-        nc.vector.tensor_copy(out=ident_bf16[:], in_=ident_f32[:])
+        wo_words = const.tile([P, E, 4], BF16, name="wo_words", align_bytes=64)
+        wo_codes = const.tile([P, E], U32, name="wo_q", align_bytes=64)
+        wo_scales = const.tile([P, E], U8, name="wo_qs", align_bytes=64)
         for t in (1, 2, 3):
             widen("vector", 0, t)
         widen("scalar", 0, 0)
         turn_m(0)
-        interleave_x(0)
-        nc.tensor.transpose(vec_ps[:], vec_rows[:], ident_bf16[:])
+        new_x_words(0)
+        interleave_x_vector(0, 0, 2)
         turn_m(1)
-        nc.vector.tensor_copy(out=vec_cols[:], in_=vec_ps[:, 0:12])
+        nc.tensor.transpose(vec_ps[:], vec_rows[:], ident_bf16[:])
         quantize_m(0)
-        quantize_x(0)
+        quantize_x(0, 0, 2)
+        nc.vector.tensor_copy(out=vec_cols[:], in_=vec_ps[:, 0:12])
+        interleave_x_vector(0, 2, 4)
         nc.vector.tensor_tensor(out=gain_coef[:, 0:4], in0=vec_cols[:, 0:4], in1=vec_cols[:, 8:12], op=MULT)
         nc.vector.tensor_tensor(out=gain_coef[:, 4:8], in0=vec_cols[:, 4:8], in1=vec_cols[:, 8:12], op=MULT)
-        turn_m(2)
         quantize_m(1)
-        widen("vector", 1, 0)
-        widen("vector", 1, 1)
-        quantize_m(2)
-        widen("vector", 1, 2)
-        widen("vector", 1, 3)
-
-        wo_words = const.tile([P, E, 4], BF16, name="wo_words", align_bytes=64)
-        wo_codes = const.tile([P, E], U32, name="wo_q", align_bytes=64)
-        wo_scales = const.tile([P, E], U8, name="wo_qs", align_bytes=64)
-
-        products(0)
+        quantize_x(0, 2, 4)
+        widen("scalar", 1, 0)
+        turn_m(2)
+        products(0, "RQ")
         third_order(0)
-        for t in (0, 1, 2):
-            widen("scalar", 2, t)
-        interleave_x(1)
-        products(1)
+        for t in (1, 2, 3):
+            widen("vector", 1, t)
+        quantize_m(2)
+        new_x_words(1)
+        interleave_x_vector(1, 0, 4)
+        products(1, "RQ")
+        products(0, "P")
+        widen("scalar", 2, 0)
         third_order(1)
-        widen("scalar", 2, 3)
-        for t in range(4):
-            widen("scalar", 3, t)
-        times_q(0)
-        quantize_x(1)
-        interleave_x(2)
+        for t in (1, 2):
+            widen("scalar", 2, t)
+        widen("scalar", 3, 0)
 
-        for n in range(STEPS):
-            even = n % 2 == 0
-            if n + 1 < STEPS:
-                times_q(n + 1)
-            times_p(n)
-
-            if n == 0:
+        for b in range(NB):
+            n = 2 * b
+            times_q(n)
+            if b == 1:
                 nc.vector.tensor_copy(out=wo_words[:], in_=wo_rows[:].rearrange("p j e -> p e j"))
-            if n == 2:
+            if b == 2:
                 nc.vector.quantize_mx(
                     out=wo_codes[:].bitcast(X4), scales=wo_scales[:], in_=wo_words[:].rearrange("p e j -> p (e j)")
                 )
-            if not even and (n + 3) // 2 < NB:
-                quantize_x((n + 3) // 2)
-            if not even and (n + 5) // 2 < NB:
-                interleave_x((n + 5) // 2)
-            if even and n >= 4:
-                quantize_z((n - 4) // 2)
-
+            if b >= 3:
+                quantize_z(b - 3)
+            if b == LAST:
+                quantize_z(b - 2)
+            if b + 2 < NB and b % 2 == 0:
+                widen("vector", b + 2, 3)
+            if b + 1 < NB:
+                quantize_x(b + 1, 0, 4)
+            if b + 2 < NB:
+                new_x_words(b + 2)
+                interleave_x_gpsimd(b + 2)
             if n + 2 < STEPS:
-                products(n + 2)
+                products(n + 2, "RQ")
                 third_order(n + 2)
+            if b >= 3:
+                project(b - 3)
+            if b >= 1:
+                times_p(n - 1)
+            products(n + 1, "P")
+            if b - 1 >= TURNED:
+                fetch_z(b - 1, "gpsimd")
+            if 0 <= b - 2 < TURNED:
+                fetch_z(b - 2, "vector" if b + 2 < NB else "scalar")
+            if 0 <= b - 1 < TURNED:
+                turn_z(b - 1)
+            if b + 3 < NB:
+                widen("scalar", b + 3, 1)
+                widen("scalar", b + 3, 2)
+            if b >= 3:
+                store(b - 3)
+            if b == LAST:
+                project(b - 2)
+                store(b - 2)
+            if b + 3 < NB and b % 2 == 0:
+                widen("scalar", b + 3, 3)
+            times_q(n + 1)
+            if n + 3 < STEPS:
+                products(n + 3, "RQ")
+                third_order(n + 3)
+            times_p(n)
+            if n + 2 < STEPS:
+                products(n + 2, "P")
+            if b + 4 < NB:
+                widen("scalar", b + 4, 0)
 
-            if even and n >= 2:
-                fetch_z((n - 2) // 2)
-            if not even and n >= 5:
-                store((n - 5) // 2)
-            if n == 0:
-                widen("scalar", SINGLE, 0)
-            t = (n + 1) % 4
-            pair = (n + 9 - t) // 2
-            if pair < NB:
-                widen("scalar", pair, t)
-
-            if not even and n // 2 not in (DIRECT, LAST):
-                turn_z(n // 2)
-            if even and n >= 4:
-                project((n - 4) // 2)
-
+        times_p(STEPS - 1)
         quantize_z(LAST - 1)
         project(LAST - 1)
         store(LAST - 1)

@@ -21,6 +21,7 @@ MULT = mybir.AluOpType.mult
 STEPS = 2 * NB
 SINGLE = 4
 HEAD = 2
+SPLIT = 256
 LAST = NB - 1
 TURNED = NB - 3
 
@@ -31,7 +32,7 @@ def tile_volterrathirdordermixer_t_kernel(tc, x_bytes, x_scale, mp, mq, mr, coef
         const = ctx.enter_context(tc.tile_pool(name="const", bufs=1))
         bytes_pool = ctx.enter_context(tc.tile_pool(name="bytes_pool", bufs=8))
         wide_pool = ctx.enter_context(tc.tile_pool(name="wide_pool", bufs=4))
-        x_pool = ctx.enter_context(tc.tile_pool(name="x_pool", bufs=1))
+        x_pool = ctx.enter_context(tc.tile_pool(name="x_pool", bufs=2))
         xq_pool = ctx.enter_context(tc.tile_pool(name="xq_pool", bufs=5))
         poly = ctx.enter_context(tc.tile_pool(name="poly", bufs=3))
         z_pool = ctx.enter_context(tc.tile_pool(name="z_pool", bufs=3))
@@ -87,19 +88,19 @@ def tile_volterrathirdordermixer_t_kernel(tc, x_bytes, x_scale, mp, mq, mr, coef
 
         x_wide, x_words, x_codes, x_scales = {}, {}, {}, {}
 
-        def widen(engine, b, t):
+        def widen(engine, b, t, c0=0, c1=D):
             if b not in x_wide:
                 wide = wide_pool.tile([P, 4, D], BF16, name="wide", align_bytes=64)
                 x_wide[b] = wide
-            dst = x_wide[b][:, t, :]
-            src = x_raw[b][:, t * D : (t + 1) * D].bitcast(FP8)
+            dst = x_wide[b][:, t, c0:c1]
+            src = x_raw[b][:, t * D + c0 : t * D + c1].bitcast(FP8)
             if engine == "scalar":
                 nc.scalar.activation(out=dst, in_=src, func=COPY, scale=scale[:, t : t + 1])
             else:
                 nc.vector.tensor_scalar(out=dst, in0=src, scalar1=scale[:, t : t + 1], scalar2=None, op0=MULT)
 
         def new_x_words(b):
-            words = x_pool.tile([P, 4 * D], BF16, name="words%d" % min(b, 1), align_bytes=64)
+            words = x_pool.tile([P, 4 * D], BF16, name="words", align_bytes=64)
             codes = xq_pool.tile([P, D], U32, name="x_q", align_bytes=64)
             scales = xq_pool.tile([P, D], U8, name="x_qs", align_bytes=64)
             x_words[b], x_codes[b], x_scales[b] = words, codes, scales
@@ -304,6 +305,7 @@ def tile_volterrathirdordermixer_t_kernel(tc, x_bytes, x_scale, mp, mq, mr, coef
         third_order(1)
         for t in (1, 2):
             widen("scalar", 2, t)
+        widen("scalar", 2, 3, 0, SPLIT)
         widen("scalar", 3, 0)
 
         for b in range(NB):
@@ -319,8 +321,8 @@ def tile_volterrathirdordermixer_t_kernel(tc, x_bytes, x_scale, mp, mq, mr, coef
                 quantize_z(b - 3)
             if b == LAST:
                 quantize_z(b - 2)
-            if b + 2 < NB and b % 2 == 0:
-                widen("vector", b + 2, 3)
+            if b + 2 < NB:
+                widen("vector", b + 2, 3, SPLIT, D)
             if b + 1 < NB:
                 quantize_x(b + 1, 0, 4)
             if b + 2 < NB:
@@ -348,8 +350,8 @@ def tile_volterrathirdordermixer_t_kernel(tc, x_bytes, x_scale, mp, mq, mr, coef
             if b == LAST:
                 project(b - 2)
                 store(b - 2)
-            if b + 3 < NB and b % 2 == 0:
-                widen("scalar", b + 3, 3)
+            if b + 3 < NB:
+                widen("scalar", b + 3, 3, 0, SPLIT)
             times_q(n + 1)
             if n + 3 < STEPS:
                 products(n + 3, "RQ")

@@ -21,9 +21,17 @@ MULT = mybir.AluOpType.mult
 STEPS = 2 * NB
 SINGLE = 4
 HEAD = 2
-SPLIT = 256
+SPLIT = 384
 LAST = NB - 1
 TURNED = NB - 3
+
+
+def gpsimd_blocks(b):
+    return {1: 10}.get(b, 16)
+
+
+def stores_in(b):
+    return 2 if b >= NB - 2 else (0 if b % 4 == 0 else 1)
 
 
 def tile_volterrathirdordermixer_t_kernel(tc, x_bytes, x_scale, mp, mq, mr, coef, gain, wo, out):
@@ -36,8 +44,8 @@ def tile_volterrathirdordermixer_t_kernel(tc, x_bytes, x_scale, mp, mq, mr, coef
         xq_pool = ctx.enter_context(tc.tile_pool(name="xq_pool", bufs=5))
         poly = ctx.enter_context(tc.tile_pool(name="poly", bufs=3))
         z_pool = ctx.enter_context(tc.tile_pool(name="z_pool", bufs=3))
-        zq_pool = ctx.enter_context(tc.tile_pool(name="zq_pool", bufs=4))
-        out_pool = ctx.enter_context(tc.tile_pool(name="out_pool", bufs=4))
+        zq_pool = ctx.enter_context(tc.tile_pool(name="zq_pool", bufs=8))
+        out_pool = ctx.enter_context(tc.tile_pool(name="out_pool", bufs=8))
         psum = ctx.enter_context(tc.psum_pool(name="psum", bufs=2))
         ctx.enter_context(tc.manual_schedule())
 
@@ -60,8 +68,6 @@ def tile_volterrathirdordermixer_t_kernel(tc, x_bytes, x_scale, mp, mq, mr, coef
             nc.sync.dma_start(out=m_rows[:], in_=m.rearrange("(p c) k -> p c k", c=2))
             m_raw.append(m_rows)
 
-        load_m(mr)
-        load_m(mq)
         vec_rows = const.tile([P, P], BF16, name="vec_rows", align_bytes=64)
         nc.vector.memset(vec_rows[:], 0.0)
         for v, vec in enumerate((coef[0], coef[1], gain)):
@@ -69,10 +75,11 @@ def tile_volterrathirdordermixer_t_kernel(tc, x_bytes, x_scale, mp, mq, mr, coef
                 out=vec_rows[4 * v : 4 * v + 4, :].rearrange("p (g i) -> p g i", i=8),
                 in_=vec.rearrange("(g j i) -> j g i", j=4, i=8),
             )
+        load_m(mr)
         load_x(1, 1)
+        load_m(mq)
         load_m(mp)
-        for b in range(2, SINGLE):
-            load_x(b, 1)
+        load_x(2, 1)
 
         ident_f32 = const.tile([P, P], F32, name="ident_f32", align_bytes=64)
         make_identity(nc, ident_f32[:])
@@ -80,10 +87,10 @@ def tile_volterrathirdordermixer_t_kernel(tc, x_bytes, x_scale, mp, mq, mr, coef
         nc.scalar.activation(out=ident_bf16[:], in_=ident_f32[:], func=COPY)
 
         wo_rows = const.tile([P, 4, E], BF16, name="wo_rows", align_bytes=64)
-        load_x(SINGLE, 2)
         for i in range(8):
             nc.sync.dma_start(out=wo_rows[i:P:8, :, :], in_=wo.rearrange("(g j i) e -> i g j e", j=4, i=8)[i])
-        for b in range(SINGLE + 2, NB, 2):
+        load_x(3, 1)
+        for b in range(SINGLE, NB, 2):
             load_x(b, 2)
 
         x_wide, x_words, x_codes, x_scales = {}, {}, {}, {}
@@ -105,16 +112,16 @@ def tile_volterrathirdordermixer_t_kernel(tc, x_bytes, x_scale, mp, mq, mr, coef
             scales = xq_pool.tile([P, D], U8, name="x_qs", align_bytes=64)
             x_words[b], x_codes[b], x_scales[b] = words, codes, scales
 
-        def interleave_x_vector(b, j0, j1):
+        def interleave_x_vector(b, j0, j1, g0=0):
             nc.vector.tensor_copy(
-                out=x_words[b][:].rearrange("p (j g i t) -> p g j t i", j=4, g=16, i=8, t=4)[:, :, j0:j1],
-                in_=x_wide[b][:].rearrange("p t (g j i) -> p g j t i", g=16, j=4, i=8)[:, :, j0:j1],
+                out=x_words[b][:].rearrange("p (j g i t) -> p g j t i", j=4, g=16, i=8, t=4)[:, g0:, j0:j1],
+                in_=x_wide[b][:].rearrange("p t (g j i) -> p g j t i", g=16, j=4, i=8)[:, g0:, j0:j1],
             )
 
         def interleave_x_gpsimd(b):
             nc.gpsimd.tensor_scalar(
-                out=x_words[b][:].rearrange("p (j g i t) -> p g j i t", j=4, g=16, i=8, t=4),
-                in0=x_wide[b][:].rearrange("p t (g j i) -> p g j i t", g=16, j=4, i=8),
+                out=x_words[b][:].rearrange("p (j g i t) -> p g j i t", j=4, g=16, i=8, t=4)[:, : gpsimd_blocks(b)],
+                in0=x_wide[b][:].rearrange("p t (g j i) -> p g j i t", g=16, j=4, i=8)[:, : gpsimd_blocks(b)],
                 scalar1=1.0,
                 scalar2=0.0,
                 op0=MULT,
@@ -129,7 +136,7 @@ def tile_volterrathirdordermixer_t_kernel(tc, x_bytes, x_scale, mp, mq, mr, coef
                 in_=x_words[b][:, 4 * j0 * P : 4 * j1 * P],
             )
 
-        m_words, m_codes, m_scales = [], [], []
+        m_turned, m_words, m_codes, m_scales = [], [], [], []
 
         def turn_m(i):
             turned = psum.tile([P, 2, 2, P], F32, name="turned", tag="RQP"[i])
@@ -137,11 +144,14 @@ def tile_volterrathirdordermixer_t_kernel(tc, x_bytes, x_scale, mp, mq, mr, coef
                 words = m_raw[i][:, c, :].bitcast(F32)
                 for u in range(2):
                     nc.tensor.transpose(turned[:, c, u, :], words[:, u : S // 2 : 2], ident_f32[:])
+            m_turned.append(turned)
+
+        def fetch_m(i, engine):
+            turned = m_turned[i]
             grouped = const.tile([P, T, 4], BF16, name="m_words%d" % i, align_bytes=64)
             dst = grouped[:].rearrange("p n t -> p (n t)").bitcast(F32)
-            nc.scalar.copy(
-                out=dst.rearrange("p (c n u) -> p c n u", c=2, u=2), in_=turned[:].rearrange("p c u n -> p c n u")
-            )
+            copy = nc.scalar.copy if engine == "scalar" else nc.vector.tensor_copy
+            copy(out=dst.rearrange("p (c n u) -> p c n u", c=2, u=2), in_=turned[:].rearrange("p c u n -> p c n u"))
             m_words.append(grouped)
 
         def quantize_m(i):
@@ -271,101 +281,103 @@ def tile_volterrathirdordermixer_t_kernel(tc, x_bytes, x_scale, mp, mq, mr, coef
         vec_cols = const.tile([P, 12], F32, name="vec_cols", align_bytes=64)
         gain_coef = const.tile([P, 8], F32, name="gain_coef", align_bytes=64)
         vec_ps = psum.tile([P, P], BF16, name="vec_ps", tag="O")
-        wo_words = const.tile([P, E, 4], BF16, name="wo_words", align_bytes=64)
         wo_codes = const.tile([P, E], U32, name="wo_q", align_bytes=64)
         wo_scales = const.tile([P, E], U8, name="wo_qs", align_bytes=64)
+        nc.tensor.transpose(vec_ps[:], vec_rows[:], ident_bf16[:])
         for t in (1, 2, 3):
             widen("vector", 0, t)
         widen("scalar", 0, 0)
+        nc.vector.tensor_copy(out=vec_cols[:], in_=vec_ps[:, 0:12])
         turn_m(0)
+        widen("scalar", 1, 0)
+        fetch_m(0, "scalar")
         new_x_words(0)
         interleave_x_vector(0, 0, 2)
-        turn_m(1)
-        nc.tensor.transpose(vec_ps[:], vec_rows[:], ident_bf16[:])
-        quantize_m(0)
-        quantize_x(0, 0, 2)
-        nc.vector.tensor_copy(out=vec_cols[:], in_=vec_ps[:, 0:12])
-        interleave_x_vector(0, 2, 4)
         nc.vector.tensor_tensor(out=gain_coef[:, 0:4], in0=vec_cols[:, 0:4], in1=vec_cols[:, 8:12], op=MULT)
         nc.vector.tensor_tensor(out=gain_coef[:, 4:8], in0=vec_cols[:, 4:8], in1=vec_cols[:, 8:12], op=MULT)
-        quantize_m(1)
-        quantize_x(0, 2, 4)
-        widen("scalar", 1, 0)
-        turn_m(2)
-        products(0, "RQ")
+        turn_m(1)
+        widen("scalar", 1, 1)
+        fetch_m(1, "scalar")
+        quantize_x(0, 0, 2)
+        quantize_m(0)
+        products(0, "R")
         third_order(0)
-        for t in (1, 2, 3):
-            widen("vector", 1, t)
-        quantize_m(2)
-        new_x_words(1)
-        interleave_x_vector(1, 0, 4)
+        interleave_x_vector(0, 2, 4)
+        widen("vector", 1, 3)
+        quantize_m(1)
+        turn_m(2)
+        widen("vector", 1, 2)
+        quantize_x(0, 2, 4)
+        products(0, "Q")
         products(1, "RQ")
-        products(0, "P")
         widen("scalar", 2, 0)
         third_order(1)
+        new_x_words(1)
+        interleave_x_gpsimd(1)
         for t in (1, 2):
             widen("scalar", 2, t)
         widen("scalar", 2, 3, 0, SPLIT)
-        widen("scalar", 3, 0)
+        z_tile["wo"] = wo_rows
+        turn_z("wo")
+        times_q(0)
+        fetch_m(2, "vector")
+        times_q(1)
 
-        for b in range(NB):
+        stored = 0
+        for b in range(1, NB):
             n = 2 * b
-            times_q(n)
+            if gpsimd_blocks(b) < 16:
+                interleave_x_vector(b, 0, 4, gpsimd_blocks(b))
             if b == 1:
-                nc.vector.tensor_copy(out=wo_words[:], in_=wo_rows[:].rearrange("p j e -> p e j"))
+                quantize_m(2)
+                products(0, "P")
+                products(1, "P")
+            quantize_x(b, 0, 2)
+            products(n, "RQ")
+            third_order(n)
             if b == 2:
                 nc.vector.quantize_mx(
-                    out=wo_codes[:].bitcast(X4), scales=wo_scales[:], in_=wo_words[:].rearrange("p e j -> p (e j)")
+                    out=wo_codes[:].bitcast(X4), scales=wo_scales[:], in_=z_words["wo"][:].rearrange("p e j -> p (e j)")
                 )
             if b >= 3:
                 quantize_z(b - 3)
+            if b + 1 < NB:
+                widen("vector", b + 1, 3, SPLIT, D)
+            quantize_x(b, 2, 4)
+            if b + 1 < NB:
+                new_x_words(b + 1)
+                interleave_x_gpsimd(b + 1)
+            products(n + 1, "RQ")
+            third_order(n + 1)
+            if b == 1:
+                times_p(0)
+            products(n, "P")
+            times_p(n - 1)
+            products(n + 1, "P")
+            if b == LAST:
+                fetch_z(b - 1, "gpsimd")
+            fetch_z(b - 2 if b >= 2 else "wo", "vector")
+            if b < LAST:
+                turn_z(b - 1)
+            if b + 2 < NB:
+                for t in range(3):
+                    widen("scalar", b + 2, t)
+                widen("scalar", b + 2, 3, 0, SPLIT)
+            for k in range(min(stores_in(b), b - 2 - stored)):
+                project(stored)
+                store(stored)
+                stored += 1
+            times_q(n)
+            times_q(n + 1)
             if b == LAST:
                 quantize_z(b - 2)
-            if b + 2 < NB:
-                widen("vector", b + 2, 3, SPLIT, D)
-            if b + 1 < NB:
-                quantize_x(b + 1, 0, 4)
-            if b + 2 < NB:
-                new_x_words(b + 2)
-                interleave_x_gpsimd(b + 2)
-            if n + 2 < STEPS:
-                products(n + 2, "RQ")
-                third_order(n + 2)
-            if b >= 3:
-                project(b - 3)
-            if b >= 1:
-                times_p(n - 1)
-            products(n + 1, "P")
-            if b - 1 >= TURNED:
-                fetch_z(b - 1, "gpsimd")
-            if 0 <= b - 2 < TURNED:
-                fetch_z(b - 2, "vector" if b + 2 < NB else "scalar")
-            if 0 <= b - 1 < TURNED:
-                turn_z(b - 1)
-            if b + 3 < NB:
-                widen("scalar", b + 3, 1)
-                widen("scalar", b + 3, 2)
-            if b >= 3:
-                store(b - 3)
-            if b == LAST:
-                project(b - 2)
-                store(b - 2)
-            if b + 3 < NB:
-                widen("scalar", b + 3, 3, 0, SPLIT)
-            times_q(n + 1)
-            if n + 3 < STEPS:
-                products(n + 3, "RQ")
-                third_order(n + 3)
             times_p(n)
-            if n + 2 < STEPS:
-                products(n + 2, "P")
-            if b + 4 < NB:
-                widen("scalar", b + 4, 0)
 
-        times_p(STEPS - 1)
         quantize_z(LAST - 1)
-        project(LAST - 1)
-        store(LAST - 1)
+        times_p(STEPS - 1)
+        for b in range(stored, LAST):
+            project(b)
+            store(b)
         half_words = []
         for c in range(2):
             words = zq_pool.tile([P, P, 4], BF16, name="half_words%d" % c, align_bytes=64)

@@ -21,17 +21,12 @@ MULT = mybir.AluOpType.mult
 STEPS = 2 * NB
 SINGLE = 4
 HEAD = 2
-SPLIT = 384
+SPLIT = 288
 LAST = NB - 1
-TURNED = NB - 3
 
 
 def gpsimd_blocks(b):
-    return {1: 10}.get(b, 16)
-
-
-def stores_in(b):
-    return 2 if b >= NB - 2 else (0 if b % 4 == 0 else 1)
+    return {2: 13, 3: 13}.get(b, 16)
 
 
 def tile_volterrathirdordermixer_t_kernel(tc, x_bytes, x_scale, mp, mq, mr, coef, gain, wo, out):
@@ -44,7 +39,7 @@ def tile_volterrathirdordermixer_t_kernel(tc, x_bytes, x_scale, mp, mq, mr, coef
         xq_pool = ctx.enter_context(tc.tile_pool(name="xq_pool", bufs=5))
         poly = ctx.enter_context(tc.tile_pool(name="poly", bufs=3))
         z_pool = ctx.enter_context(tc.tile_pool(name="z_pool", bufs=3))
-        zq_pool = ctx.enter_context(tc.tile_pool(name="zq_pool", bufs=8))
+        zq_pool = ctx.enter_context(tc.tile_pool(name="zq_pool", bufs=3))
         out_pool = ctx.enter_context(tc.tile_pool(name="out_pool", bufs=8))
         psum = ctx.enter_context(tc.psum_pool(name="psum", bufs=2))
         ctx.enter_context(tc.manual_schedule())
@@ -165,31 +160,36 @@ def tile_volterrathirdordermixer_t_kernel(tc, x_bytes, x_scale, mp, mq, mr, coef
 
         sums, h_val, u_val, z_tile = {}, {}, {}, {}
 
+        def units(n):
+            if n // 2 == LAST:
+                c = n % 2
+                return [(j, slice(c * P, (c + 1) * P), slice(j * P, (j + 1) * P)) for j in range(4)]
+            return [(2 * (n % 2) + k, slice(0, T), slice(k * T, (k + 1) * T)) for k in range(2)]
+
         def products(n, names):
-            b, j0 = n // 2, 2 * (n % 2)
+            b = n // 2
             for name in names:
                 i = "RQP".index(name)
-                ps = psum.tile([P, 2, T], F32, name="sum_ps", tag=name)
-                for k in range(2):
-                    cols = slice((j0 + k) * P, (j0 + k + 1) * P)
+                ps = psum.tile([P, 2 * T], F32, name="sum_ps", tag=name)
+                for j, times, bank in units(n):
+                    cols = slice(j * P, (j + 1) * P)
                     nc.tensor.matmul_mx(
-                        out=ps[:, k, :],
+                        out=ps[:, bank],
                         lhsT=x_codes[b][:, cols].bitcast(X4),
                         lhsT_scale=x_scales[b][:, cols],
-                        rhs=m_codes[i][:].bitcast(X4),
-                        rhs_scale=m_scales[i][:],
+                        rhs=m_codes[i][:, times].bitcast(X4),
+                        rhs_scale=m_scales[i][:, times],
                         start=True,
                         stop=True,
                     )
                 sums[name, n] = ps
 
         def third_order(n):
-            h = poly.tile([P, 2, T], F32, name="h", align_bytes=64)
-            for k in range(2):
-                j = 2 * (n % 2) + k
+            h = poly.tile([P, 2 * T], F32, name="h", align_bytes=64)
+            for j, times, bank in units(n):
                 nc.scalar.activation(
-                    out=h[:, k, :],
-                    in_=sums["R", n][:, k, :],
+                    out=h[:, bank],
+                    in_=sums["R", n][:, bank],
                     func=IDENTITY,
                     bias=gain_coef[:, j : j + 1],
                     scale=gain_coef[:, 4 + j : 5 + j],
@@ -197,7 +197,7 @@ def tile_volterrathirdordermixer_t_kernel(tc, x_bytes, x_scale, mp, mq, mr, coef
             h_val[n] = h
 
         def times_q(n):
-            u = poly.tile([P, 2, T], F32, name="u", align_bytes=64)
+            u = poly.tile([P, 2 * T], F32, name="u", align_bytes=64)
             nc.vector.tensor_tensor(out=u[:], in0=h_val[n][:], in1=sums["Q", n][:], op=MULT)
             u_val[n] = u
 
@@ -206,18 +206,17 @@ def tile_volterrathirdordermixer_t_kernel(tc, x_bytes, x_scale, mp, mq, mr, coef
             if n % 2 == 0:
                 z_rows = z_pool.tile([P, 4, T], BF16, name="z_rows", align_bytes=64)
                 z_tile[b] = z_rows
-            for k in range(2):
-                j = 2 * (n % 2) + k
+            for j, times, bank in units(n):
                 nc.vector.scalar_tensor_tensor(
-                    out=z_tile[b][:, j, :],
-                    in0=u_val[n][:, k, :],
+                    out=z_tile[b][:, j, times],
+                    in0=u_val[n][:, bank],
                     scalar=vec_cols[:, 8 + j : 9 + j],
-                    in1=sums["P", n][:, k, :],
+                    in1=sums["P", n][:, bank],
                     op0=ADD,
                     op1=MULT,
                 )
 
-        z_turned, z_words, z_codes, z_scales, out_sum = {}, {}, {}, {}, {}
+        z_turned, z_group, z_words, z_codes, z_scales, out_sum = {}, {}, {}, {}, {}, {}
 
         def turn_z(b):
             turned = psum.tile([P, T, 4], BF16, name="z_turned", tag="O")
@@ -232,31 +231,31 @@ def tile_volterrathirdordermixer_t_kernel(tc, x_bytes, x_scale, mp, mq, mr, coef
                 )
             z_turned[b] = turned
 
-        def fetch_z(b, engine):
-            words = zq_pool.tile([P, T, 4], BF16, name="z_words", align_bytes=64)
-            dst = words[:].rearrange("p t j -> p (t j)")
-            if engine == "gpsimd":
-                nc.gpsimd.tensor_scalar(
-                    out=words[:],
-                    in0=z_tile[b][:].rearrange("p j t -> p t j"),
-                    scalar1=1.0,
-                    scalar2=0.0,
-                    op0=MULT,
-                    op1=ADD,
-                )
-            elif engine == "scalar":
-                nc.scalar.copy(out=dst, in_=z_turned[b][:].rearrange("p t j -> p (t j)"))
-            else:
-                nc.vector.tensor_copy(out=dst, in_=z_turned[b][:].rearrange("p t j -> p (t j)"))
-            z_words[b] = words
+        def new_z_words(first, count):
+            words = zq_pool.tile([P, count * T * 4], BF16, name="z_words%d" % count, align_bytes=64)
+            z_group[first] = words
+            for k in range(count):
+                z_words[first if count == 1 else first + k] = words[:, k * T * 4 : (k + 1) * T * 4]
 
-        def quantize_z(b):
-            codes = zq_pool.tile([P, T], U32, name="z_q", align_bytes=64)
-            scales = zq_pool.tile([P, T], U8, name="z_qs", align_bytes=64)
-            nc.vector.quantize_mx(
-                out=codes[:].bitcast(X4), scales=scales[:], in_=z_words[b][:].rearrange("p t j -> p (t j)")
+        def fetch_z(b, copy):
+            copy(out=z_words[b], in_=z_turned[b][:].rearrange("p t j -> p (t j)"))
+
+        def interleave_z_gpsimd(b):
+            nc.gpsimd.tensor_scalar(
+                out=z_words[b].rearrange("p (t j) -> p t j", j=4),
+                in0=z_tile[b][:].rearrange("p j t -> p t j"),
+                scalar1=1.0,
+                scalar2=0.0,
+                op0=MULT,
+                op1=ADD,
             )
-            z_codes[b], z_scales[b] = codes, scales
+
+        def quantize_z(first, count=1):
+            codes = zq_pool.tile([P, count * T], U32, name="z_q%d" % count, align_bytes=64)
+            scales = zq_pool.tile([P, count * T], U8, name="z_qs%d" % count, align_bytes=64)
+            nc.vector.quantize_mx(out=codes[:].bitcast(X4), scales=scales[:], in_=z_group[first][:])
+            for k in range(count):
+                z_codes[first + k], z_scales[first + k] = codes[:, k * T : (k + 1) * T], scales[:, k * T : (k + 1) * T]
 
         def project(b):
             o_ps = psum.tile([P, 2, E], F32, name="o_ps", tag="O")
@@ -287,8 +286,8 @@ def tile_volterrathirdordermixer_t_kernel(tc, x_bytes, x_scale, mp, mq, mr, coef
         for t in (1, 2, 3):
             widen("vector", 0, t)
         widen("scalar", 0, 0)
-        nc.vector.tensor_copy(out=vec_cols[:], in_=vec_ps[:, 0:12])
         turn_m(0)
+        nc.vector.tensor_copy(out=vec_cols[:], in_=vec_ps[:, 0:12])
         widen("scalar", 1, 0)
         fetch_m(0, "scalar")
         new_x_words(0)
@@ -299,99 +298,99 @@ def tile_volterrathirdordermixer_t_kernel(tc, x_bytes, x_scale, mp, mq, mr, coef
         widen("scalar", 1, 1)
         fetch_m(1, "scalar")
         quantize_x(0, 0, 2)
-        quantize_m(0)
-        products(0, "R")
-        third_order(0)
         interleave_x_vector(0, 2, 4)
-        widen("vector", 1, 3)
-        quantize_m(1)
+        quantize_m(0)
         turn_m(2)
+        products(0, "R")
         widen("vector", 1, 2)
+        widen("vector", 1, 3)
         quantize_x(0, 2, 4)
+        quantize_m(1)
+        fetch_m(2, "scalar")
+        third_order(0)
         products(0, "Q")
         products(1, "RQ")
-        widen("scalar", 2, 0)
-        third_order(1)
-        new_x_words(1)
-        interleave_x_gpsimd(1)
-        for t in (1, 2):
-            widen("scalar", 2, t)
-        widen("scalar", 2, 3, 0, SPLIT)
         z_tile["wo"] = wo_rows
         turn_z("wo")
-        times_q(0)
-        fetch_m(2, "vector")
-        times_q(1)
+        new_x_words(1)
+        interleave_x_vector(1, 0, 4)
+        widen("vector", 2, 2)
+        quantize_m(2)
+        products(0, "P")
+        widen("scalar", 2, 0)
+        widen("scalar", 2, 1)
+        third_order(1)
+        widen("scalar", 3, 0)
 
-        stored = 0
-        for b in range(1, NB):
+        for b in range(LAST):
             n = 2 * b
-            if gpsimd_blocks(b) < 16:
-                interleave_x_vector(b, 0, 4, gpsimd_blocks(b))
+            if b >= 1 and gpsimd_blocks(b + 1) < 16:
+                interleave_x_vector(b + 1, 0, 4, gpsimd_blocks(b + 1))
             if b == 1:
-                quantize_m(2)
-                products(0, "P")
-                products(1, "P")
-            quantize_x(b, 0, 2)
-            products(n, "RQ")
-            third_order(n)
-            if b == 2:
                 nc.vector.quantize_mx(
-                    out=wo_codes[:].bitcast(X4), scales=wo_scales[:], in_=z_words["wo"][:].rearrange("p e j -> p (e j)")
+                    out=wo_codes[:].bitcast(X4),
+                    scales=wo_scales[:],
+                    in_=z_words["wo"],
                 )
             if b >= 3:
                 quantize_z(b - 3)
-            if b + 1 < NB:
-                widen("vector", b + 1, 3, SPLIT, D)
-            quantize_x(b, 2, 4)
-            if b + 1 < NB:
-                new_x_words(b + 1)
-                interleave_x_gpsimd(b + 1)
-            products(n + 1, "RQ")
-            third_order(n + 1)
-            if b == 1:
-                times_p(0)
-            products(n, "P")
-            times_p(n - 1)
-            products(n + 1, "P")
-            if b == LAST:
-                fetch_z(b - 1, "gpsimd")
-            fetch_z(b - 2 if b >= 2 else "wo", "vector")
-            if b < LAST:
-                turn_z(b - 1)
             if b + 2 < NB:
-                for t in range(3):
-                    widen("scalar", b + 2, t)
-                widen("scalar", b + 2, 3, 0, SPLIT)
-            for k in range(min(stores_in(b), b - 2 - stored)):
-                project(stored)
-                store(stored)
-                stored += 1
+                widen("vector", b + 2, 3, SPLIT if b else 0, D)
+            quantize_x(b + 1, 0, 4)
+            if b + 2 < NB:
+                new_x_words(b + 2)
+                interleave_x_gpsimd(b + 2)
+            if b == LAST - 1:
+                new_z_words(b - 2, 2)
+                fetch_z(b - 2, nc.scalar.copy)
             times_q(n)
+            if b >= 3:
+                project(b - 3)
+            if b + 3 < NB:
+                widen("scalar", b + 3, 1)
+            if b >= 3:
+                store(b - 3)
+            products(n + 2, "RQ")
+            third_order(n + 2)
+            if b >= 1:
+                times_p(n - 1)
+            products(n + 1, "P")
+            if b == 0:
+                new_z_words("wo", 1)
+                fetch_z("wo", nc.vector.tensor_copy)
+            if 2 <= b < LAST - 1:
+                new_z_words(b - 2, 1)
+                fetch_z(b - 2, nc.vector.tensor_copy)
+            products(n + 3, "R")
+            if b == LAST - 1:
+                interleave_z_gpsimd(b - 1)
+            elif b >= 1:
+                turn_z(b - 1)
+            if b + 3 < NB:
+                widen("scalar", b + 3, 2)
+                widen("scalar", b + 3, 3, 0, SPLIT)
             times_q(n + 1)
-            if b == LAST:
-                quantize_z(b - 2)
+            products(n + 3, "Q")
+            third_order(n + 3)
+            if b + 4 < NB:
+                widen("scalar", b + 4, 0)
             times_p(n)
+            products(n + 2, "P")
 
-        quantize_z(LAST - 1)
-        times_p(STEPS - 1)
-        for b in range(stored, LAST):
-            project(b)
-            store(b)
-        half_words = []
-        for c in range(2):
+        half_words, half_sums = [], []
+
+        def interleave_half(c, copy):
             words = zq_pool.tile([P, P, 4], BF16, name="half_words%d" % c, align_bytes=64)
-            nc.vector.tensor_copy(
-                out=words[:], in_=z_tile[LAST][:, :, c * P : (c + 1) * P].rearrange("p j t -> p t j")
-            )
+            copy(out=words[:], in_=z_tile[LAST][:, :, c * P : (c + 1) * P].rearrange("p j t -> p t j"))
             half_words.append(words)
-        for c in range(2):
+
+        def project_half(c):
             codes = zq_pool.tile([P, P], U32, name="half_q%d" % c, align_bytes=64)
             scales = zq_pool.tile([P, P], U8, name="half_qs%d" % c, align_bytes=64)
             nc.vector.quantize_mx(
                 out=codes[:].bitcast(X4), scales=scales[:], in_=half_words[c][:].rearrange("p t j -> p (t j)")
             )
-            half_ps = psum.tile([P, E], F32, name="half_ps", tag="O")
+            half_ps = psum.tile([P, E], F32, name="half_ps", tag="RQ"[c])
             nc.tensor.matmul_mx(
                 out=half_ps[:],
                 lhsT=codes[:].bitcast(X4),
@@ -401,9 +400,33 @@ def tile_volterrathirdordermixer_t_kernel(tc, x_bytes, x_scale, mp, mq, mr, coef
                 start=True,
                 stop=True,
             )
+            half_sums.append(half_ps)
+
+        def store_half(c):
             half_sb = out_pool.tile([P, E], F32, name="half_sb%d" % c, align_bytes=64)
-            if c == 0:
-                nc.scalar.copy(out=half_sb[:], in_=half_ps[:])
-            else:
-                nc.vector.tensor_copy(out=half_sb[:], in_=half_ps[:])
+            nc.vector.tensor_copy(out=half_sb[:], in_=half_sums[c][:])
             nc.sync.dma_start(out=out[LAST].rearrange("(p c) e -> p c e", c=2)[:, c, :], in_=half_sb[:])
+
+        n = 2 * LAST
+        times_q(n)
+        times_p(n - 1)
+        products(n + 1, "P")
+        quantize_z(LAST - 3, 2)
+        new_z_words(LAST - 1, 1)
+        interleave_z_gpsimd(LAST - 1)
+        project(LAST - 3)
+        project(LAST - 2)
+        store(LAST - 3)
+        times_q(n + 1)
+        times_p(n)
+        interleave_half(0, nc.scalar.copy)
+        store(LAST - 2)
+        times_p(n + 1)
+        quantize_z(LAST - 1)
+        project(LAST - 1)
+        store(LAST - 1)
+        interleave_half(1, nc.vector.tensor_copy)
+        for c in range(2):
+            project_half(c)
+        for c in range(2):
+            store_half(c)

@@ -21,12 +21,12 @@ MULT = mybir.AluOpType.mult
 STEPS = 2 * NB
 SINGLE = 4
 HEAD = 2
-SPLIT = 288
+SKIP = 3
 LAST = NB - 1
 
 
 def gpsimd_blocks(b):
-    return {2: 13, 3: 13}.get(b, 16)
+    return {2: 10}.get(b, 16)
 
 
 def tile_volterrathirdordermixer_t_kernel(tc, x_bytes, x_scale, mp, mq, mr, coef, gain, wo, out):
@@ -35,11 +35,10 @@ def tile_volterrathirdordermixer_t_kernel(tc, x_bytes, x_scale, mp, mq, mr, coef
         const = ctx.enter_context(tc.tile_pool(name="const", bufs=1))
         bytes_pool = ctx.enter_context(tc.tile_pool(name="bytes_pool", bufs=8))
         wide_pool = ctx.enter_context(tc.tile_pool(name="wide_pool", bufs=4))
-        x_pool = ctx.enter_context(tc.tile_pool(name="x_pool", bufs=2))
         xq_pool = ctx.enter_context(tc.tile_pool(name="xq_pool", bufs=5))
         poly = ctx.enter_context(tc.tile_pool(name="poly", bufs=3))
         z_pool = ctx.enter_context(tc.tile_pool(name="z_pool", bufs=3))
-        zq_pool = ctx.enter_context(tc.tile_pool(name="zq_pool", bufs=3))
+        zq_pool = ctx.enter_context(tc.tile_pool(name="zq_pool", bufs=7))
         out_pool = ctx.enter_context(tc.tile_pool(name="out_pool", bufs=8))
         psum = ctx.enter_context(tc.psum_pool(name="psum", bufs=2))
         ctx.enter_context(tc.manual_schedule())
@@ -89,20 +88,24 @@ def tile_volterrathirdordermixer_t_kernel(tc, x_bytes, x_scale, mp, mq, mr, coef
             load_x(b, 2)
 
         x_wide, x_words, x_codes, x_scales = {}, {}, {}, {}
+        shared_words = []
+        for k in range(2):
+            shared = const.tile([P, 4 * D], BF16, name="shared_words%d" % k, align_bytes=64)
+            shared_words.append(shared)
 
-        def widen(engine, b, t, c0=0, c1=D):
+        def widen(engine, b, t):
             if b not in x_wide:
                 wide = wide_pool.tile([P, 4, D], BF16, name="wide", align_bytes=64)
                 x_wide[b] = wide
-            dst = x_wide[b][:, t, c0:c1]
-            src = x_raw[b][:, t * D + c0 : t * D + c1].bitcast(FP8)
+            dst = x_wide[b][:, t, :]
+            src = x_raw[b][:, t * D : (t + 1) * D].bitcast(FP8)
             if engine == "scalar":
                 nc.scalar.activation(out=dst, in_=src, func=COPY, scale=scale[:, t : t + 1])
             else:
                 nc.vector.tensor_scalar(out=dst, in0=src, scalar1=scale[:, t : t + 1], scalar2=None, op0=MULT)
 
         def new_x_words(b):
-            words = x_pool.tile([P, 4 * D], BF16, name="words", align_bytes=64)
+            words = shared_words[b % 2]
             codes = xq_pool.tile([P, D], U32, name="x_q", align_bytes=64)
             scales = xq_pool.tile([P, D], U8, name="x_qs", align_bytes=64)
             x_words[b], x_codes[b], x_scales[b] = words, codes, scales
@@ -216,7 +219,7 @@ def tile_volterrathirdordermixer_t_kernel(tc, x_bytes, x_scale, mp, mq, mr, coef
                     op1=MULT,
                 )
 
-        z_turned, z_group, z_words, z_codes, z_scales, out_sum = {}, {}, {}, {}, {}, {}
+        z_turned, z_words, z_codes, z_scales, out_sum = {}, {}, {}, {}, {}
 
         def turn_z(b):
             turned = psum.tile([P, T, 4], BF16, name="z_turned", tag="O")
@@ -231,12 +234,6 @@ def tile_volterrathirdordermixer_t_kernel(tc, x_bytes, x_scale, mp, mq, mr, coef
                 )
             z_turned[b] = turned
 
-        def new_z_words(first, count):
-            words = zq_pool.tile([P, count * T * 4], BF16, name="z_words%d" % count, align_bytes=64)
-            z_group[first] = words
-            for k in range(count):
-                z_words[first if count == 1 else first + k] = words[:, k * T * 4 : (k + 1) * T * 4]
-
         def fetch_z(b, copy):
             copy(out=z_words[b], in_=z_turned[b][:].rearrange("p t j -> p (t j)"))
 
@@ -250,10 +247,11 @@ def tile_volterrathirdordermixer_t_kernel(tc, x_bytes, x_scale, mp, mq, mr, coef
                 op1=ADD,
             )
 
-        def quantize_z(first, count=1):
+        def quantize_z(first, words):
+            count = words.shape[1] // (4 * T)
             codes = zq_pool.tile([P, count * T], U32, name="z_q%d" % count, align_bytes=64)
             scales = zq_pool.tile([P, count * T], U8, name="z_qs%d" % count, align_bytes=64)
-            nc.vector.quantize_mx(out=codes[:].bitcast(X4), scales=scales[:], in_=z_group[first][:])
+            nc.vector.quantize_mx(out=codes[:].bitcast(X4), scales=scales[:], in_=words)
             for k in range(count):
                 z_codes[first + k], z_scales[first + k] = codes[:, k * T : (k + 1) * T], scales[:, k * T : (k + 1) * T]
 
@@ -322,58 +320,69 @@ def tile_volterrathirdordermixer_t_kernel(tc, x_bytes, x_scale, mp, mq, mr, coef
         third_order(1)
         widen("scalar", 3, 0)
 
+        waiting = []
+
+        def emit(count):
+            for k in range(min(count, len(waiting))):
+                project(waiting[0])
+                store(waiting.pop(0))
+
         for b in range(LAST):
             n = 2 * b
             if b >= 1 and gpsimd_blocks(b + 1) < 16:
                 interleave_x_vector(b + 1, 0, 4, gpsimd_blocks(b + 1))
-            if b == 1:
+            if b == 2:
                 nc.vector.quantize_mx(
                     out=wo_codes[:].bitcast(X4),
                     scales=wo_scales[:],
                     in_=z_words["wo"],
                 )
             if b >= 3:
-                quantize_z(b - 3)
-            if b + 2 < NB:
-                widen("vector", b + 2, 3, SPLIT if b else 0, D)
+                quantize_z(b - 3, z_words[b - 3])
+                waiting.append(b - 3)
+            if b < 2:
+                widen("vector", b + 2, 3)
             quantize_x(b + 1, 0, 4)
             if b + 2 < NB:
                 new_x_words(b + 2)
                 interleave_x_gpsimd(b + 2)
             if b == LAST - 1:
-                new_z_words(b - 2, 2)
+                last_words = const.tile([P, 3, 4 * T], BF16, name="last_words", align_bytes=64)
+                for k in range(3):
+                    z_words[b - 2 + k] = last_words[:, k, :]
                 fetch_z(b - 2, nc.scalar.copy)
             times_q(n)
-            if b >= 3:
-                project(b - 3)
             if b + 3 < NB:
                 widen("scalar", b + 3, 1)
-            if b >= 3:
-                store(b - 3)
+            if b % SKIP and b < LAST - 1:
+                emit(1)
             products(n + 2, "RQ")
+            if b + 3 < NB:
+                widen("scalar", b + 3, 2)
+                if b > 0:
+                    widen("scalar", b + 3, 3)
             third_order(n + 2)
+            if b + 3 >= NB:
+                emit(b + 4 - NB)
             if b >= 1:
                 times_p(n - 1)
             products(n + 1, "P")
-            if b == 0:
-                new_z_words("wo", 1)
-                fetch_z("wo", nc.vector.tensor_copy)
-            if 2 <= b < LAST - 1:
-                new_z_words(b - 2, 1)
-                fetch_z(b - 2, nc.vector.tensor_copy)
+            if 1 <= b < LAST - 1:
+                turned = b - 2 if b >= 2 else "wo"
+                z_words[turned] = shared_words[(b + 1) % 2][:, : 4 * T]
+                fetch_z(turned, nc.vector.tensor_copy)
             products(n + 3, "R")
             if b == LAST - 1:
                 interleave_z_gpsimd(b - 1)
             elif b >= 1:
                 turn_z(b - 1)
-            if b + 3 < NB:
-                widen("scalar", b + 3, 2)
-                widen("scalar", b + 3, 3, 0, SPLIT)
             times_q(n + 1)
             products(n + 3, "Q")
             third_order(n + 3)
             if b + 4 < NB:
                 widen("scalar", b + 4, 0)
+            if b == LAST - 1:
+                emit(NB)
             times_p(n)
             products(n + 2, "P")
 
@@ -411,8 +420,7 @@ def tile_volterrathirdordermixer_t_kernel(tc, x_bytes, x_scale, mp, mq, mr, coef
         times_q(n)
         times_p(n - 1)
         products(n + 1, "P")
-        quantize_z(LAST - 3, 2)
-        new_z_words(LAST - 1, 1)
+        quantize_z(LAST - 3, last_words[:, 0:2, :].rearrange("p k w -> p (k w)"))
         interleave_z_gpsimd(LAST - 1)
         project(LAST - 3)
         project(LAST - 2)
@@ -422,7 +430,7 @@ def tile_volterrathirdordermixer_t_kernel(tc, x_bytes, x_scale, mp, mq, mr, coef
         interleave_half(0, nc.scalar.copy)
         store(LAST - 2)
         times_p(n + 1)
-        quantize_z(LAST - 1)
+        quantize_z(LAST - 1, z_words[LAST - 1])
         project(LAST - 1)
         store(LAST - 1)
         interleave_half(1, nc.vector.tensor_copy)

@@ -40,7 +40,7 @@ def tile_volterrathirdordermixer_t_kernel(tc, x_bytes, x_scale, mp, mq, mr, coef
         z_pool = ctx.enter_context(tc.tile_pool(name="z_pool", bufs=3))
         zq_pool = ctx.enter_context(tc.tile_pool(name="zq_pool", bufs=7))
         out_pool = ctx.enter_context(tc.tile_pool(name="out_pool", bufs=8))
-        psum = ctx.enter_context(tc.psum_pool(name="psum", bufs=2))
+        psum = ctx.enter_context(tc.psum_pool(name="psum", bufs=1))
         ctx.enter_context(tc.manual_schedule())
 
         x_raw = {}
@@ -51,41 +51,50 @@ def tile_volterrathirdordermixer_t_kernel(tc, x_bytes, x_scale, mp, mq, mr, coef
             for k in range(width):
                 x_raw[b + k] = codes[:, k, :]
 
-        load_x(0, 1)
         scale = const.tile([P, 4], F32, name="scale", align_bytes=64)
-        nc.sync.dma_start(out=scale[:], in_=x_scale.rearrange("o (p t) z -> p (o t z)", t=4))
+        m_raw = {}
 
-        m_raw = []
-
-        def load_m(m):
-            m_rows = const.tile([P, 2, S], BF16, name="m_rows%d" % len(m_raw), align_bytes=64)
-            nc.sync.dma_start(out=m_rows[:], in_=m.rearrange("(p c) k -> p c k", c=2))
-            m_raw.append(m_rows)
+        def load_m(i):
+            m_rows = const.tile([P, 2, S], BF16, name="m_rows%d" % i, align_bytes=64)
+            nc.sync.dma_start(out=m_rows[:], in_=(mr, mq, mp)[i].rearrange("(p c) k -> p c k", c=2))
+            m_raw[i] = m_rows
 
         vec_rows = const.tile([P, P], BF16, name="vec_rows", align_bytes=64)
         nc.vector.memset(vec_rows[:], 0.0)
-        for v, vec in enumerate((coef[0], coef[1], gain)):
-            nc.sync.dma_start(
-                out=vec_rows[4 * v : 4 * v + 4, :].rearrange("p (g i) -> p g i", i=8),
-                in_=vec.rearrange("(g j i) -> j g i", j=4, i=8),
-            )
-        load_m(mr)
+
+        def load_vectors():
+            for v, vec in enumerate((coef[0], coef[1], gain)):
+                nc.sync.dma_start(
+                    out=vec_rows[4 * v : 4 * v + 4, :].rearrange("p (g i) -> p g i", i=8),
+                    in_=vec.rearrange("(g j i) -> j g i", j=4, i=8),
+                )
+
+        wo_rows = const.tile([P, 4, E], BF16, name="wo_rows", align_bytes=64)
+
+        def load_wo():
+            for i in range(8):
+                nc.sync.dma_start(out=wo_rows[i:P:8, :, :], in_=wo.rearrange("(g j i) e -> i g j e", j=4, i=8)[i])
+
+        def load_scale():
+            nc.sync.dma_start(out=scale[:], in_=x_scale.rearrange("o (p t) z -> p (o t z)", t=4))
+
+        load_scale()
+        load_x(0, 1)
         load_x(1, 1)
-        load_m(mq)
-        load_m(mp)
+        load_m(0)
+        load_m(1)
+        load_m(2)
+        load_vectors()
         load_x(2, 1)
+        load_x(3, 1)
+        load_wo()
+        for b in range(SINGLE, NB, 2):
+            load_x(b, 2)
 
         ident_f32 = const.tile([P, P], F32, name="ident_f32", align_bytes=64)
         make_identity(nc, ident_f32[:])
         ident_bf16 = const.tile([P, P], BF16, name="ident_bf16", align_bytes=64)
         nc.scalar.activation(out=ident_bf16[:], in_=ident_f32[:], func=COPY)
-
-        wo_rows = const.tile([P, 4, E], BF16, name="wo_rows", align_bytes=64)
-        for i in range(8):
-            nc.sync.dma_start(out=wo_rows[i:P:8, :, :], in_=wo.rearrange("(g j i) e -> i g j e", j=4, i=8)[i])
-        load_x(3, 1)
-        for b in range(SINGLE, NB, 2):
-            load_x(b, 2)
 
         x_wide, x_words, x_codes, x_scales = {}, {}, {}, {}
         shared_words = []
@@ -116,10 +125,17 @@ def tile_volterrathirdordermixer_t_kernel(tc, x_bytes, x_scale, mp, mq, mr, coef
                 in_=x_wide[b][:].rearrange("p t (g j i) -> p g j t i", g=16, j=4, i=8)[:, g0:, j0:j1],
             )
 
-        def interleave_x_gpsimd(b):
+        def interleave_x_scalar(b, j):
+            nc.scalar.copy(
+                out=x_words[b][:].rearrange("p (j g i t) -> p g j i t", j=4, g=16, i=8, t=4)[:, :, j],
+                in_=x_wide[b][:].rearrange("p t (g j i) -> p g j i t", g=16, j=4, i=8)[:, :, j],
+            )
+
+        def interleave_x_gpsimd(b, tiles=4):
+            blocks = gpsimd_blocks(b)
             nc.gpsimd.tensor_scalar(
-                out=x_words[b][:].rearrange("p (j g i t) -> p g j i t", j=4, g=16, i=8, t=4)[:, : gpsimd_blocks(b)],
-                in0=x_wide[b][:].rearrange("p t (g j i) -> p g j i t", g=16, j=4, i=8)[:, : gpsimd_blocks(b)],
+                out=x_words[b][:].rearrange("p (j g i t) -> p g j i t", j=4, g=16, i=8, t=4)[:, :blocks, :tiles],
+                in0=x_wide[b][:].rearrange("p t (g j i) -> p g j i t", g=16, j=4, i=8)[:, :blocks, :tiles],
                 scalar1=1.0,
                 scalar2=0.0,
                 op0=MULT,
@@ -137,7 +153,7 @@ def tile_volterrathirdordermixer_t_kernel(tc, x_bytes, x_scale, mp, mq, mr, coef
         m_turned, m_words, m_codes, m_scales = [], [], [], []
 
         def turn_m(i):
-            turned = psum.tile([P, 2, 2, P], F32, name="turned", tag="RQP"[i])
+            turned = psum.tile([P, 2, 2, P], F32, name="turned", tag="RQP"[i] + "1")
             for c in range(2):
                 words = m_raw[i][:, c, :].bitcast(F32)
                 for u in range(2):
@@ -173,7 +189,7 @@ def tile_volterrathirdordermixer_t_kernel(tc, x_bytes, x_scale, mp, mq, mr, coef
             b = n // 2
             for name in names:
                 i = "RQP".index(name)
-                ps = psum.tile([P, 2 * T], F32, name="sum_ps", tag=name)
+                ps = psum.tile([P, 2 * T], F32, name="sum_ps", tag=name + "01"[n % 2])
                 for j, times, bank in units(n):
                     cols = slice(j * P, (j + 1) * P)
                     nc.tensor.matmul_mx(
@@ -222,7 +238,7 @@ def tile_volterrathirdordermixer_t_kernel(tc, x_bytes, x_scale, mp, mq, mr, coef
         z_turned, z_words, z_codes, z_scales, out_sum = {}, {}, {}, {}, {}
 
         def turn_z(b):
-            turned = psum.tile([P, T, 4], BF16, name="z_turned", tag="O")
+            turned = psum.tile([P, T, 4], BF16, name="z_turned", tag="Z")
             for c in range(2):
                 t = slice(c * P, (c + 1) * P)
                 nc.tensor.matmul(
@@ -255,8 +271,8 @@ def tile_volterrathirdordermixer_t_kernel(tc, x_bytes, x_scale, mp, mq, mr, coef
             for k in range(count):
                 z_codes[first + k], z_scales[first + k] = codes[:, k * T : (k + 1) * T], scales[:, k * T : (k + 1) * T]
 
-        def project(b):
-            o_ps = psum.tile([P, 2, E], F32, name="o_ps", tag="O")
+        def project(b, bank="O"):
+            o_ps = psum.tile([P, 2, E], F32, name="o_ps", tag=bank)
             for c in range(2):
                 cols = slice(c * P, (c + 1) * P)
                 nc.tensor.matmul_mx(
@@ -280,54 +296,54 @@ def tile_volterrathirdordermixer_t_kernel(tc, x_bytes, x_scale, mp, mq, mr, coef
         vec_ps = psum.tile([P, P], BF16, name="vec_ps", tag="O")
         wo_codes = const.tile([P, E], U32, name="wo_q", align_bytes=64)
         wo_scales = const.tile([P, E], U8, name="wo_qs", align_bytes=64)
-        nc.tensor.transpose(vec_ps[:], vec_rows[:], ident_bf16[:])
-        for t in (1, 2, 3):
-            widen("vector", 0, t)
-        widen("scalar", 0, 0)
+        widen("vector", 0, 0)
+        widen("vector", 0, 1)
+        widen("scalar", 0, 2)
+        widen("vector", 0, 3)
+        widen("vector", 1, 3)
         turn_m(0)
-        nc.vector.tensor_copy(out=vec_cols[:], in_=vec_ps[:, 0:12])
-        widen("scalar", 1, 0)
-        fetch_m(0, "scalar")
+        turn_m(1)
+        turn_m(2)
+        nc.tensor.transpose(vec_ps[:], vec_rows[:], ident_bf16[:])
+        for t in (0, 1, 2):
+            widen("scalar", 1, t)
+        for i in range(3):
+            fetch_m(i, "scalar")
         new_x_words(0)
         interleave_x_vector(0, 0, 2)
+        interleave_x_vector(0, 2, 4)
+        quantize_x(0, 0, 2)
+        quantize_x(0, 2, 4)
+        new_x_words(1)
+        interleave_x_vector(1, 0, 2)
+        quantize_m(0)
+        nc.vector.tensor_copy(out=vec_cols[:], in_=vec_ps[:, 0:12])
+        quantize_m(1)
         nc.vector.tensor_tensor(out=gain_coef[:, 0:4], in0=vec_cols[:, 0:4], in1=vec_cols[:, 8:12], op=MULT)
         nc.vector.tensor_tensor(out=gain_coef[:, 4:8], in0=vec_cols[:, 4:8], in1=vec_cols[:, 8:12], op=MULT)
-        turn_m(1)
-        widen("scalar", 1, 1)
-        fetch_m(1, "scalar")
-        quantize_x(0, 0, 2)
-        interleave_x_vector(0, 2, 4)
-        quantize_m(0)
-        turn_m(2)
         products(0, "R")
-        widen("vector", 1, 2)
-        widen("vector", 1, 3)
-        quantize_x(0, 2, 4)
-        quantize_m(1)
-        fetch_m(2, "scalar")
-        third_order(0)
+        products(1, "R")
         products(0, "Q")
-        products(1, "RQ")
-        z_tile["wo"] = wo_rows
-        turn_z("wo")
-        new_x_words(1)
-        interleave_x_vector(1, 0, 4)
-        widen("vector", 2, 2)
-        quantize_m(2)
-        products(0, "P")
+        products(1, "Q")
+        interleave_x_vector(1, 2, 4)
         widen("scalar", 2, 0)
         widen("scalar", 2, 1)
+        third_order(0)
         third_order(1)
+        quantize_m(2)
+        widen("vector", 2, 2)
+        products(0, "P")
+        z_tile["wo"] = wo_rows
+        turn_z("wo")
         widen("scalar", 3, 0)
 
         waiting = []
 
-        def emit(count):
-            for k in range(min(count, len(waiting))):
-                project(waiting[0])
-                store(waiting.pop(0))
+        def emit(bank="O"):
+            project(waiting[0], bank)
+            store(waiting.pop(0))
 
-        for b in range(LAST):
+        for b in range(LAST - 2):
             n = 2 * b
             if b >= 1 and gpsimd_blocks(b + 1) < 16:
                 interleave_x_vector(b + 1, 0, 4, gpsimd_blocks(b + 1))
@@ -343,46 +359,32 @@ def tile_volterrathirdordermixer_t_kernel(tc, x_bytes, x_scale, mp, mq, mr, coef
             if b < 2:
                 widen("vector", b + 2, 3)
             quantize_x(b + 1, 0, 4)
-            if b + 2 < NB:
-                new_x_words(b + 2)
-                interleave_x_gpsimd(b + 2)
-            if b == LAST - 1:
-                last_words = const.tile([P, 3, 4 * T], BF16, name="last_words", align_bytes=64)
-                for k in range(3):
-                    z_words[b - 2 + k] = last_words[:, k, :]
-                fetch_z(b - 2, nc.scalar.copy)
+            new_x_words(b + 2)
+            interleave_x_gpsimd(b + 2)
             times_q(n)
-            if b + 3 < NB:
-                widen("scalar", b + 3, 1)
-            if b % SKIP and b < LAST - 1:
-                emit(1)
+            widen("scalar", b + 3, 1)
+            if b % SKIP and b > 3:
+                emit()
             products(n + 2, "RQ")
-            if b + 3 < NB:
-                widen("scalar", b + 3, 2)
-                if b > 0:
-                    widen("scalar", b + 3, 3)
+            widen("scalar", b + 3, 2)
+            if b > 0:
+                widen("scalar", b + 3, 3)
             third_order(n + 2)
-            if b + 3 >= NB:
-                emit(b + 4 - NB)
             if b >= 1:
                 times_p(n - 1)
             products(n + 1, "P")
-            if 1 <= b < LAST - 1:
+            if b >= 1:
                 turned = b - 2 if b >= 2 else "wo"
                 z_words[turned] = shared_words[(b + 1) % 2][:, : 4 * T]
                 fetch_z(turned, nc.vector.tensor_copy)
             products(n + 3, "R")
-            if b == LAST - 1:
-                interleave_z_gpsimd(b - 1)
-            elif b >= 1:
+            if b >= 1:
                 turn_z(b - 1)
             times_q(n + 1)
             products(n + 3, "Q")
             third_order(n + 3)
             if b + 4 < NB:
                 widen("scalar", b + 4, 0)
-            if b == LAST - 1:
-                emit(NB)
             times_p(n)
             products(n + 2, "P")
 
@@ -399,7 +401,7 @@ def tile_volterrathirdordermixer_t_kernel(tc, x_bytes, x_scale, mp, mq, mr, coef
             nc.vector.quantize_mx(
                 out=codes[:].bitcast(X4), scales=scales[:], in_=half_words[c][:].rearrange("p t j -> p (t j)")
             )
-            half_ps = psum.tile([P, E], F32, name="half_ps", tag="RQ"[c])
+            half_ps = psum.tile([P, E], F32, name="half_ps", tag="RQ"[c] + "0")
             nc.tensor.matmul_mx(
                 out=half_ps[:],
                 lhsT=codes[:].bitcast(X4),
@@ -411,30 +413,79 @@ def tile_volterrathirdordermixer_t_kernel(tc, x_bytes, x_scale, mp, mq, mr, coef
             )
             half_sums.append(half_ps)
 
-        def store_half(c):
+        def store_half(c, copy):
             half_sb = out_pool.tile([P, E], F32, name="half_sb%d" % c, align_bytes=64)
-            nc.vector.tensor_copy(out=half_sb[:], in_=half_sums[c][:])
+            copy(out=half_sb[:], in_=half_sums[c][:])
             nc.sync.dma_start(out=out[LAST].rearrange("(p c) e -> p c e", c=2)[:, c, :], in_=half_sb[:])
 
-        n = 2 * LAST
+        last_words = const.tile([P, 4, 4 * T], BF16, name="last_words", align_bytes=64)
+        for k in range(4):
+            z_words[LAST - 4 + k] = last_words[:, k, :]
+
+        n = 2 * (LAST - 2)
+        quantize_z(LAST - 5, z_words[LAST - 5])
+        waiting.append(LAST - 5)
+        quantize_x(LAST - 1, 0, 4)
+        new_x_words(LAST)
+        interleave_x_gpsimd(LAST, 3)
+        interleave_x_scalar(LAST, 3)
+        fetch_z(LAST - 4, nc.scalar.copy)
         times_q(n)
+        products(n + 2, "RQ")
+        third_order(n + 2)
         times_p(n - 1)
         products(n + 1, "P")
-        quantize_z(LAST - 3, last_words[:, 0:2, :].rearrange("p k w -> p (k w)"))
+        products(n + 3, "R")
+        third_order(n + 3)
+        emit("O")
+        emit("Z")
+        times_q(n + 1)
+        products(n + 3, "Q")
+        times_p(n)
+        products(n + 2, "P")
+
+        n = 2 * (LAST - 1)
+        quantize_z(LAST - 4, z_words[LAST - 4])
+        quantize_x(LAST, 0, 4)
+        interleave_z_gpsimd(LAST - 3)
+        products(n + 2, "R")
+        third_order(n + 2)
+        products(n + 3, "R")
+        third_order(n + 3)
+        times_p(n - 1)
+        interleave_z_gpsimd(LAST - 2)
+        products(n + 1, "P")
+        emit("O")
+        times_q(n)
+        products(n + 2, "Q")
+        emit("Z")
+        times_q(n + 1)
+        products(n + 3, "Q")
+        emit("R0")
+        waiting.append(LAST - 4)
+        times_p(n)
+        products(n + 2, "P")
+        emit("R1")
+
+        n = 2 * LAST
+        times_p(n - 1)
+        products(n + 1, "P")
+        quantize_z(LAST - 3, last_words[:, 1:3, :].rearrange("p k w -> p (k w)"))
         interleave_z_gpsimd(LAST - 1)
-        project(LAST - 3)
-        project(LAST - 2)
+        project(LAST - 3, "O")
+        project(LAST - 2, "Z")
         store(LAST - 3)
+        store(LAST - 2)
+        times_q(n)
         times_q(n + 1)
         times_p(n)
-        interleave_half(0, nc.scalar.copy)
-        store(LAST - 2)
-        times_p(n + 1)
         quantize_z(LAST - 1, z_words[LAST - 1])
         project(LAST - 1)
         store(LAST - 1)
-        interleave_half(1, nc.vector.tensor_copy)
+        times_p(n + 1)
+        for c in range(2):
+            interleave_half(c, nc.vector.tensor_copy)
         for c in range(2):
             project_half(c)
-        for c in range(2):
-            store_half(c)
+        store_half(0, nc.scalar.copy)
+        store_half(1, nc.vector.tensor_copy)

@@ -21,7 +21,7 @@ MULT = mybir.AluOpType.mult
 STEPS = 2 * NB
 SINGLE = 4
 HEAD = 2
-SKIP = 3
+GATE = 32
 LAST = NB - 1
 
 
@@ -363,7 +363,7 @@ def tile_volterrathirdordermixer_t_kernel(tc, x_bytes, x_scale, mp, mq, mr, coef
             interleave_x_gpsimd(b + 2)
             times_q(n)
             widen("scalar", b + 3, 1)
-            if b % SKIP and b > 3:
+            if b >= 4 and b % 2 == 0:
                 emit()
             products(n + 2, "RQ")
             widen("scalar", b + 3, 2)
@@ -418,9 +418,10 @@ def tile_volterrathirdordermixer_t_kernel(tc, x_bytes, x_scale, mp, mq, mr, coef
             copy(out=half_sb[:], in_=half_sums[c][:])
             nc.sync.dma_start(out=out[LAST].rearrange("(p c) e -> p c e", c=2)[:, c, :], in_=half_sb[:])
 
-        last_words = const.tile([P, 4, 4 * T], BF16, name="last_words", align_bytes=64)
-        for k in range(4):
-            z_words[LAST - 4 + k] = last_words[:, k, :]
+        for k in range(2):
+            chained = const.tile([P, 8 * T - GATE], BF16, name="chained_words%d" % k, align_bytes=64)
+            z_words[LAST - 4 + 2 * k] = chained[:, : 4 * T]
+            z_words[LAST - 3 + 2 * k] = chained[:, 4 * T - GATE :]
 
         n = 2 * (LAST - 2)
         quantize_z(LAST - 5, z_words[LAST - 5])
@@ -433,12 +434,13 @@ def tile_volterrathirdordermixer_t_kernel(tc, x_bytes, x_scale, mp, mq, mr, coef
         times_q(n)
         products(n + 2, "RQ")
         third_order(n + 2)
+        emit("O")
         times_p(n - 1)
         products(n + 1, "P")
         products(n + 3, "R")
         third_order(n + 3)
-        emit("O")
         emit("Z")
+        emit("O")
         times_q(n + 1)
         products(n + 3, "Q")
         times_p(n)
@@ -470,12 +472,13 @@ def tile_volterrathirdordermixer_t_kernel(tc, x_bytes, x_scale, mp, mq, mr, coef
         n = 2 * LAST
         times_p(n - 1)
         products(n + 1, "P")
-        quantize_z(LAST - 3, last_words[:, 1:3, :].rearrange("p k w -> p (k w)"))
+        quantize_z(LAST - 2, z_words[LAST - 2])
+        quantize_z(LAST - 3, z_words[LAST - 3])
         interleave_z_gpsimd(LAST - 1)
-        project(LAST - 3, "O")
-        project(LAST - 2, "Z")
-        store(LAST - 3)
+        project(LAST - 2, "O")
+        project(LAST - 3, "Z")
         store(LAST - 2)
+        store(LAST - 3)
         times_q(n)
         times_q(n + 1)
         times_p(n)

@@ -21,12 +21,14 @@ MULT = mybir.AluOpType.mult
 STEPS = 2 * NB
 SINGLE = 4
 HEAD = 2
+SPLIT = 128
+PIECE = 384
 GATE = 32
 LAST = NB - 1
 
 
 def gpsimd_blocks(b):
-    return {2: 10}.get(b, 16)
+    return {2: 8}.get(b, 16)
 
 
 def tile_volterrathirdordermixer_t_kernel(tc, x_bytes, x_scale, mp, mq, mr, coef, gain, wo, out):
@@ -102,12 +104,12 @@ def tile_volterrathirdordermixer_t_kernel(tc, x_bytes, x_scale, mp, mq, mr, coef
             shared = const.tile([P, 4 * D], BF16, name="shared_words%d" % k, align_bytes=64)
             shared_words.append(shared)
 
-        def widen(engine, b, t):
+        def widen(engine, b, t, first=0, last=D):
             if b not in x_wide:
                 wide = wide_pool.tile([P, 4, D], BF16, name="wide", align_bytes=64)
                 x_wide[b] = wide
-            dst = x_wide[b][:, t, :]
-            src = x_raw[b][:, t * D : (t + 1) * D].bitcast(FP8)
+            dst = x_wide[b][:, t, first:last]
+            src = x_raw[b][:, t * D + first : t * D + last].bitcast(FP8)
             if engine == "scalar":
                 nc.scalar.activation(out=dst, in_=src, func=COPY, scale=scale[:, t : t + 1])
             else:
@@ -253,23 +255,23 @@ def tile_volterrathirdordermixer_t_kernel(tc, x_bytes, x_scale, mp, mq, mr, coef
         def fetch_z(b, copy):
             copy(out=z_words[b], in_=z_turned[b][:].rearrange("p t j -> p (t j)"))
 
-        def interleave_z_gpsimd(b):
+        def interleave_z_gpsimd(b, times=T):
             nc.gpsimd.tensor_scalar(
-                out=z_words[b].rearrange("p (t j) -> p t j", j=4),
-                in0=z_tile[b][:].rearrange("p j t -> p t j"),
+                out=z_words[b].rearrange("p (t j) -> p t j", j=4)[:, :times],
+                in0=z_tile[b][:].rearrange("p j t -> p t j")[:, :times],
                 scalar1=1.0,
                 scalar2=0.0,
                 op0=MULT,
                 op1=ADD,
             )
 
-        def quantize_z(first, words):
+        def quantize_z(first, words, step=1):
             count = words.shape[1] // (4 * T)
             codes = zq_pool.tile([P, count * T], U32, name="z_q%d" % count, align_bytes=64)
             scales = zq_pool.tile([P, count * T], U8, name="z_qs%d" % count, align_bytes=64)
             nc.vector.quantize_mx(out=codes[:].bitcast(X4), scales=scales[:], in_=words)
             for k in range(count):
-                z_codes[first + k], z_scales[first + k] = codes[:, k * T : (k + 1) * T], scales[:, k * T : (k + 1) * T]
+                z_codes[first + step * k], z_scales[first + step * k] = codes[:, k * T : (k + 1) * T], scales[:, k * T : (k + 1) * T]
 
         def project(b, bank="O"):
             o_ps = psum.tile([P, 2, E], F32, name="o_ps", tag=bank)
@@ -330,8 +332,9 @@ def tile_volterrathirdordermixer_t_kernel(tc, x_bytes, x_scale, mp, mq, mr, coef
         widen("scalar", 2, 1)
         third_order(0)
         third_order(1)
-        quantize_m(2)
         widen("vector", 2, 2)
+        widen("vector", 2, 3, D - PIECE)
+        quantize_m(2)
         products(0, "P")
         z_tile["wo"] = wo_rows
         turn_z("wo")
@@ -345,8 +348,6 @@ def tile_volterrathirdordermixer_t_kernel(tc, x_bytes, x_scale, mp, mq, mr, coef
 
         for b in range(LAST - 2):
             n = 2 * b
-            if b >= 1 and gpsimd_blocks(b + 1) < 16:
-                interleave_x_vector(b + 1, 0, 4, gpsimd_blocks(b + 1))
             if b == 2:
                 nc.vector.quantize_mx(
                     out=wo_codes[:].bitcast(X4),
@@ -356,10 +357,13 @@ def tile_volterrathirdordermixer_t_kernel(tc, x_bytes, x_scale, mp, mq, mr, coef
             if b >= 3:
                 quantize_z(b - 3, z_words[b - 3])
                 waiting.append(b - 3)
-            if b < 2:
-                widen("vector", b + 2, 3)
-            quantize_x(b + 1, 0, 4)
             new_x_words(b + 2)
+            if b == 0:
+                interleave_x_vector(2, 0, 4, gpsimd_blocks(2))
+                widen("vector", 2, 3, 0, D - PIECE)
+            if b == 1:
+                widen("vector", 3, 3, PIECE)
+            quantize_x(b + 1, 0, 4)
             interleave_x_gpsimd(b + 2)
             times_q(n)
             widen("scalar", b + 3, 1)
@@ -367,8 +371,7 @@ def tile_volterrathirdordermixer_t_kernel(tc, x_bytes, x_scale, mp, mq, mr, coef
                 emit()
             products(n + 2, "RQ")
             widen("scalar", b + 3, 2)
-            if b > 0:
-                widen("scalar", b + 3, 3)
+            widen("scalar", b + 3, 3, 0, D if b else PIECE)
             third_order(n + 2)
             if b >= 1:
                 times_p(n - 1)
@@ -418,72 +421,77 @@ def tile_volterrathirdordermixer_t_kernel(tc, x_bytes, x_scale, mp, mq, mr, coef
             copy(out=half_sb[:], in_=half_sums[c][:])
             nc.sync.dma_start(out=out[LAST].rearrange("(p c) e -> p c e", c=2)[:, c, :], in_=half_sb[:])
 
-        for k in range(2):
-            chained = const.tile([P, 8 * T - GATE], BF16, name="chained_words%d" % k, align_bytes=64)
-            z_words[LAST - 4 + 2 * k] = chained[:, : 4 * T]
-            z_words[LAST - 3 + 2 * k] = chained[:, 4 * T - GATE :]
+        last_words = const.tile([P, 12 * T - GATE], BF16, name="last_words", align_bytes=64)
+        z_words[LAST - 4] = last_words[:, : 4 * T]
+        z_words[LAST - 2] = last_words[:, 4 * T - GATE : 8 * T - GATE]
+        z_words[LAST - 3] = last_words[:, 8 * T - GATE :]
+        words_14 = const.tile([P, 4 * T], BF16, name="words_14", align_bytes=64)
+        z_words[LAST - 1] = words_14[:]
 
         n = 2 * (LAST - 2)
         quantize_z(LAST - 5, z_words[LAST - 5])
         waiting.append(LAST - 5)
         quantize_x(LAST - 1, 0, 4)
         new_x_words(LAST)
-        interleave_x_gpsimd(LAST, 3)
-        interleave_x_scalar(LAST, 3)
+        interleave_x_gpsimd(LAST)
         fetch_z(LAST - 4, nc.scalar.copy)
+        emit("O")
         times_q(n)
         products(n + 2, "RQ")
         third_order(n + 2)
+        products(n + 3, "R")
+        third_order(n + 3)
         emit("O")
         times_p(n - 1)
         products(n + 1, "P")
-        products(n + 3, "R")
-        third_order(n + 3)
-        emit("Z")
-        emit("O")
+        emit("R0")
+        turn_z(LAST - 3)
+        fetch_z(LAST - 3, nc.scalar.copy)
         times_q(n + 1)
         products(n + 3, "Q")
+        emit("O")
         times_p(n)
         products(n + 2, "P")
+        times_p(n + 1)
+        products(n + 3, "P")
+        emit("Z")
 
         n = 2 * (LAST - 1)
         quantize_z(LAST - 4, z_words[LAST - 4])
         quantize_x(LAST, 0, 4)
-        interleave_z_gpsimd(LAST - 3)
+        interleave_z_gpsimd(LAST - 2)
         products(n + 2, "R")
         third_order(n + 2)
         products(n + 3, "R")
         third_order(n + 3)
-        times_p(n - 1)
-        interleave_z_gpsimd(LAST - 2)
-        products(n + 1, "P")
+        waiting.append(LAST - 4)
         emit("O")
         times_q(n)
         products(n + 2, "Q")
-        emit("Z")
         times_q(n + 1)
         products(n + 3, "Q")
-        emit("R0")
-        waiting.append(LAST - 4)
         times_p(n)
         products(n + 2, "P")
+        project(waiting[0], "Z")
+        quantize_z(LAST - 2, last_words[:, 4 * T - GATE :], -1)
+        times_p(n + 1)
+        products(n + 3, "P")
+        interleave_z_gpsimd(LAST - 1, SPLIT)
+        waiting.extend([LAST - 3, LAST - 2])
+        nc.scalar.copy(
+            out=z_words[LAST - 1].rearrange("p (t j) -> p t j", j=4)[:, SPLIT:],
+            in_=z_tile[LAST - 1][:].rearrange("p j t -> p t j")[:, SPLIT:],
+        )
+        store(waiting.pop(0))
+        emit("R0")
         emit("R1")
 
         n = 2 * LAST
-        times_p(n - 1)
-        products(n + 1, "P")
-        quantize_z(LAST - 2, z_words[LAST - 2])
-        quantize_z(LAST - 3, z_words[LAST - 3])
-        interleave_z_gpsimd(LAST - 1)
-        project(LAST - 2, "O")
-        project(LAST - 3, "Z")
-        store(LAST - 2)
-        store(LAST - 3)
         times_q(n)
         times_q(n + 1)
         times_p(n)
         quantize_z(LAST - 1, z_words[LAST - 1])
-        project(LAST - 1)
+        project(LAST - 1, "O")
         store(LAST - 1)
         times_p(n + 1)
         for c in range(2):

@@ -38,7 +38,7 @@ def tile_volterrathirdordermixer_t_kernel(tc, x_bytes, x_scale, mp, mq, mr, coef
         bytes_pool = ctx.enter_context(tc.tile_pool(name="bytes_pool", bufs=8))
         wide_pool = ctx.enter_context(tc.tile_pool(name="wide_pool", bufs=4))
         xq_pool = ctx.enter_context(tc.tile_pool(name="xq_pool", bufs=5))
-        poly = ctx.enter_context(tc.tile_pool(name="poly", bufs=3))
+        poly = ctx.enter_context(tc.tile_pool(name="poly", bufs=4))
         z_pool = ctx.enter_context(tc.tile_pool(name="z_pool", bufs=3))
         zq_pool = ctx.enter_context(tc.tile_pool(name="zq_pool", bufs=7))
         out_pool = ctx.enter_context(tc.tile_pool(name="out_pool", bufs=8))
@@ -265,6 +265,12 @@ def tile_volterrathirdordermixer_t_kernel(tc, x_bytes, x_scale, mp, mq, mr, coef
                 op1=ADD,
             )
 
+        def interleave_z_scalar(b, first=0):
+            nc.scalar.copy(
+                out=z_words[b].rearrange("p (t j) -> p t j", j=4)[:, first:],
+                in_=z_tile[b][:].rearrange("p j t -> p t j")[:, first:],
+            )
+
         def quantize_z(first, words, step=1):
             count = words.shape[1] // (4 * T)
             codes = zq_pool.tile([P, count * T], U32, name="z_q%d" % count, align_bytes=64)
@@ -337,7 +343,6 @@ def tile_volterrathirdordermixer_t_kernel(tc, x_bytes, x_scale, mp, mq, mr, coef
         quantize_m(2)
         products(0, "P")
         z_tile["wo"] = wo_rows
-        turn_z("wo")
         widen("scalar", 3, 0)
 
         waiting = []
@@ -367,9 +372,11 @@ def tile_volterrathirdordermixer_t_kernel(tc, x_bytes, x_scale, mp, mq, mr, coef
             interleave_x_gpsimd(b + 2)
             times_q(n)
             widen("scalar", b + 3, 1)
-            if b >= 4 and b % 2 == 0:
+            if b >= 3 and (b % 2 or b + 4 == NB):
                 emit()
-            products(n + 2, "RQ")
+            products(n + 2, "R")
+            products(n + 3, "R")
+            products(n + 2, "Q")
             widen("scalar", b + 3, 2)
             widen("scalar", b + 3, 3, 0, D if b else PIECE)
             third_order(n + 2)
@@ -380,9 +387,7 @@ def tile_volterrathirdordermixer_t_kernel(tc, x_bytes, x_scale, mp, mq, mr, coef
                 turned = b - 2 if b >= 2 else "wo"
                 z_words[turned] = shared_words[(b + 1) % 2][:, : 4 * T]
                 fetch_z(turned, nc.vector.tensor_copy)
-            products(n + 3, "R")
-            if b >= 1:
-                turn_z(b - 1)
+            turn_z(b - 1 if b else "wo")
             times_q(n + 1)
             products(n + 3, "Q")
             third_order(n + 3)
@@ -435,53 +440,51 @@ def tile_volterrathirdordermixer_t_kernel(tc, x_bytes, x_scale, mp, mq, mr, coef
         new_x_words(LAST)
         interleave_x_gpsimd(LAST)
         fetch_z(LAST - 4, nc.scalar.copy)
-        emit("O")
-        times_q(n)
-        products(n + 2, "RQ")
-        third_order(n + 2)
+        products(n + 2, "R")
         products(n + 3, "R")
-        third_order(n + 3)
+        third_order(n + 2)
         emit("O")
+        third_order(n + 3)
+        times_q(n)
+        products(n + 2, "Q")
         times_p(n - 1)
         products(n + 1, "P")
-        emit("R0")
-        turn_z(LAST - 3)
-        fetch_z(LAST - 3, nc.scalar.copy)
+        interleave_z_scalar(LAST - 3)
+        project(waiting[0], "O")
+        project(waiting[1], "Z")
         times_q(n + 1)
         products(n + 3, "Q")
-        emit("O")
         times_p(n)
         products(n + 2, "P")
+        store(waiting.pop(0))
+        store(waiting.pop(0))
         times_p(n + 1)
-        products(n + 3, "P")
-        emit("Z")
 
         n = 2 * (LAST - 1)
         quantize_z(LAST - 4, z_words[LAST - 4])
         quantize_x(LAST, 0, 4)
         interleave_z_gpsimd(LAST - 2)
+        products(n + 1, "P")
         products(n + 2, "R")
-        third_order(n + 2)
         products(n + 3, "R")
+        third_order(n + 2)
+        emit("O")
         third_order(n + 3)
         waiting.append(LAST - 4)
-        emit("O")
         times_q(n)
         products(n + 2, "Q")
+        emit("Z")
         times_q(n + 1)
         products(n + 3, "Q")
         times_p(n)
         products(n + 2, "P")
-        project(waiting[0], "Z")
+        project(waiting[0], "O")
         quantize_z(LAST - 2, last_words[:, 4 * T - GATE :], -1)
         times_p(n + 1)
         products(n + 3, "P")
         interleave_z_gpsimd(LAST - 1, SPLIT)
         waiting.extend([LAST - 3, LAST - 2])
-        nc.scalar.copy(
-            out=z_words[LAST - 1].rearrange("p (t j) -> p t j", j=4)[:, SPLIT:],
-            in_=z_tile[LAST - 1][:].rearrange("p j t -> p t j")[:, SPLIT:],
-        )
+        interleave_z_scalar(LAST - 1, SPLIT)
         store(waiting.pop(0))
         emit("R0")
         emit("R1")
@@ -491,7 +494,7 @@ def tile_volterrathirdordermixer_t_kernel(tc, x_bytes, x_scale, mp, mq, mr, coef
         times_q(n + 1)
         times_p(n)
         quantize_z(LAST - 1, z_words[LAST - 1])
-        project(LAST - 1, "O")
+        project(LAST - 1, "Z")
         store(LAST - 1)
         times_p(n + 1)
         for c in range(2):

@@ -23,6 +23,7 @@ SINGLE = 4
 HEAD = 2
 SPLIT = 128
 PIECE = 384
+RUN = 4
 GATE = 32
 LAST = NB - 1
 
@@ -267,8 +268,8 @@ def tile_volterrathirdordermixer_t_kernel(tc, x_bytes, x_scale, mp, mq, mr, coef
 
         def interleave_z_scalar(b, first=0):
             nc.scalar.copy(
-                out=z_words[b].rearrange("p (t j) -> p t j", j=4)[:, first:],
-                in_=z_tile[b][:].rearrange("p j t -> p t j")[:, first:],
+                out=z_words[b].rearrange("p (c i j) -> p c j i", i=RUN, j=4)[:, first // RUN :],
+                in_=z_tile[b][:].rearrange("p j (c i) -> p c j i", i=RUN)[:, first // RUN :],
             )
 
         def quantize_z(first, words, step=1):
@@ -400,7 +401,10 @@ def tile_volterrathirdordermixer_t_kernel(tc, x_bytes, x_scale, mp, mq, mr, coef
 
         def interleave_half(c, copy):
             words = zq_pool.tile([P, P, 4], BF16, name="half_words%d" % c, align_bytes=64)
-            copy(out=words[:], in_=z_tile[LAST][:, :, c * P : (c + 1) * P].rearrange("p j t -> p t j"))
+            copy(
+                out=words[:].rearrange("p (c i) j -> p c j i", i=RUN),
+                in_=z_tile[LAST][:, :, c * P : (c + 1) * P].rearrange("p j (c i) -> p c j i", i=RUN),
+            )
             half_words.append(words)
 
         def project_half(c):

@@ -21,7 +21,6 @@ MULT = mybir.AluOpType.mult
 STEPS = 2 * NB
 SINGLE = 4
 HEAD = 2
-SPLIT = 128
 PIECE = 384
 RUN = 4
 GATE = 32
@@ -102,7 +101,7 @@ def tile_volterrathirdordermixer_t_kernel(tc, x_bytes, x_scale, mp, mq, mr, coef
         x_wide, x_words, x_codes, x_scales = {}, {}, {}, {}
         shared_words = []
         for k in range(2):
-            shared = const.tile([P, 4 * D], BF16, name="shared_words%d" % k, align_bytes=64)
+            shared = const.tile([P, 4 * T - GATE + 4 * D], BF16, name="shared_words%d" % k, align_bytes=64)
             shared_words.append(shared)
 
         def widen(engine, b, t, first=0, last=D):
@@ -117,27 +116,27 @@ def tile_volterrathirdordermixer_t_kernel(tc, x_bytes, x_scale, mp, mq, mr, coef
                 nc.vector.tensor_scalar(out=dst, in0=src, scalar1=scale[:, t : t + 1], scalar2=None, op0=MULT)
 
         def new_x_words(b):
-            words = shared_words[b % 2]
+            words = shared_words[b % 2][:, 4 * T - GATE :]
             codes = xq_pool.tile([P, D], U32, name="x_q", align_bytes=64)
             scales = xq_pool.tile([P, D], U8, name="x_qs", align_bytes=64)
             x_words[b], x_codes[b], x_scales[b] = words, codes, scales
 
         def interleave_x_vector(b, j0, j1, g0=0):
             nc.vector.tensor_copy(
-                out=x_words[b][:].rearrange("p (j g i t) -> p g j t i", j=4, g=16, i=8, t=4)[:, g0:, j0:j1],
+                out=x_words[b].rearrange("p (j g i t) -> p g j t i", j=4, g=16, i=8, t=4)[:, g0:, j0:j1],
                 in_=x_wide[b][:].rearrange("p t (g j i) -> p g j t i", g=16, j=4, i=8)[:, g0:, j0:j1],
             )
 
         def interleave_x_scalar(b, j):
             nc.scalar.copy(
-                out=x_words[b][:].rearrange("p (j g i t) -> p g j i t", j=4, g=16, i=8, t=4)[:, :, j],
+                out=x_words[b].rearrange("p (j g i t) -> p g j i t", j=4, g=16, i=8, t=4)[:, :, j],
                 in_=x_wide[b][:].rearrange("p t (g j i) -> p g j i t", g=16, j=4, i=8)[:, :, j],
             )
 
         def interleave_x_gpsimd(b, tiles=4):
             blocks = gpsimd_blocks(b)
             nc.gpsimd.tensor_scalar(
-                out=x_words[b][:].rearrange("p (j g i t) -> p g j i t", j=4, g=16, i=8, t=4)[:, :blocks, :tiles],
+                out=x_words[b].rearrange("p (j g i t) -> p g j i t", j=4, g=16, i=8, t=4)[:, :blocks, :tiles],
                 in0=x_wide[b][:].rearrange("p t (g j i) -> p g j i t", g=16, j=4, i=8)[:, :blocks, :tiles],
                 scalar1=1.0,
                 scalar2=0.0,
@@ -188,11 +187,11 @@ def tile_volterrathirdordermixer_t_kernel(tc, x_bytes, x_scale, mp, mq, mr, coef
                 return [(j, slice(c * P, (c + 1) * P), slice(j * P, (j + 1) * P)) for j in range(4)]
             return [(2 * (n % 2) + k, slice(0, T), slice(k * T, (k + 1) * T)) for k in range(2)]
 
-        def products(n, names):
+        def products(n, names, side=None):
             b = n // 2
             for name in names:
                 i = "RQP".index(name)
-                ps = psum.tile([P, 2 * T], F32, name="sum_ps", tag=name + "01"[n % 2])
+                ps = psum.tile([P, 2 * T], F32, name="sum_ps", tag=name + "01"[n % 2 if side is None else side])
                 for j, times, bank in units(n):
                     cols = slice(j * P, (j + 1) * P)
                     nc.tensor.matmul_mx(
@@ -240,9 +239,9 @@ def tile_volterrathirdordermixer_t_kernel(tc, x_bytes, x_scale, mp, mq, mr, coef
 
         z_turned, z_words, z_codes, z_scales, out_sum = {}, {}, {}, {}, {}
 
-        def turn_z(b):
-            turned = psum.tile([P, T, 4], BF16, name="z_turned", tag="Z")
-            for c in range(2):
+        def turn_z(b, first=0, bank="Z"):
+            turned = psum.tile([P, T, 4], BF16, name="z_turned", tag=bank)
+            for c in range(first, 2):
                 t = slice(c * P, (c + 1) * P)
                 nc.tensor.matmul(
                     turned[:, t, :].rearrange("p t j -> p j t"),
@@ -253,8 +252,8 @@ def tile_volterrathirdordermixer_t_kernel(tc, x_bytes, x_scale, mp, mq, mr, coef
                 )
             z_turned[b] = turned
 
-        def fetch_z(b, copy):
-            copy(out=z_words[b], in_=z_turned[b][:].rearrange("p t j -> p (t j)"))
+        def fetch_z(b, copy, first=0):
+            copy(out=z_words[b][:, 4 * first * P :], in_=z_turned[b][:, first * P :, :].rearrange("p t j -> p (t j)"))
 
         def interleave_z_gpsimd(b, times=T):
             nc.gpsimd.tensor_scalar(
@@ -266,10 +265,10 @@ def tile_volterrathirdordermixer_t_kernel(tc, x_bytes, x_scale, mp, mq, mr, coef
                 op1=ADD,
             )
 
-        def interleave_z_scalar(b, first=0):
+        def interleave_z_scalar(b):
             nc.scalar.copy(
-                out=z_words[b].rearrange("p (c i j) -> p c j i", i=RUN, j=4)[:, first // RUN :],
-                in_=z_tile[b][:].rearrange("p j (c i) -> p c j i", i=RUN)[:, first // RUN :],
+                out=z_words[b].rearrange("p (c i j) -> p c j i", i=RUN, j=4)[:, : P // RUN],
+                in_=z_tile[b][:].rearrange("p j (c i) -> p c j i", i=RUN)[:, : P // RUN],
             )
 
         def quantize_z(first, words, step=1):
@@ -279,6 +278,18 @@ def tile_volterrathirdordermixer_t_kernel(tc, x_bytes, x_scale, mp, mq, mr, coef
             nc.vector.quantize_mx(out=codes[:].bitcast(X4), scales=scales[:], in_=words)
             for k in range(count):
                 z_codes[first + step * k], z_scales[first + step * k] = codes[:, k * T : (k + 1) * T], scales[:, k * T : (k + 1) * T]
+
+        def quantize_z_halves(b):
+            codes = zq_pool.tile([P, T], U32, name="z_q1", align_bytes=64)
+            scales = zq_pool.tile([P, T], U8, name="z_qs1", align_bytes=64)
+            for c in (1, 0):
+                cols = slice(c * P, (c + 1) * P)
+                nc.vector.quantize_mx(
+                    out=codes[:, cols].bitcast(X4),
+                    scales=scales[:, cols],
+                    in_=z_words[b][:, 4 * c * P : 4 * (c + 1) * P],
+                )
+            z_codes[b], z_scales[b] = codes[:], scales[:]
 
         def project(b, bank="O"):
             o_ps = psum.tile([P, 2, E], F32, name="o_ps", tag=bank)
@@ -361,7 +372,7 @@ def tile_volterrathirdordermixer_t_kernel(tc, x_bytes, x_scale, mp, mq, mr, coef
                     in_=z_words["wo"],
                 )
             if b >= 3:
-                quantize_z(b - 3, z_words[b - 3])
+                quantize_z_halves(b - 3)
                 waiting.append(b - 3)
             new_x_words(b + 2)
             if b == 0:
@@ -373,8 +384,10 @@ def tile_volterrathirdordermixer_t_kernel(tc, x_bytes, x_scale, mp, mq, mr, coef
             interleave_x_gpsimd(b + 2)
             times_q(n)
             widen("scalar", b + 3, 1)
-            if b >= 3 and (b % 2 or b + 4 == NB):
+            if b >= 3 and b % 2:
                 emit()
+            if b + 4 == NB:
+                project(waiting[0])
             products(n + 2, "R")
             products(n + 3, "R")
             products(n + 2, "Q")
@@ -394,6 +407,8 @@ def tile_volterrathirdordermixer_t_kernel(tc, x_bytes, x_scale, mp, mq, mr, coef
             third_order(n + 3)
             if b + 4 < NB:
                 widen("scalar", b + 4, 0)
+            else:
+                store(waiting.pop(0))
             times_p(n)
             products(n + 2, "P")
 
@@ -438,8 +453,7 @@ def tile_volterrathirdordermixer_t_kernel(tc, x_bytes, x_scale, mp, mq, mr, coef
         z_words[LAST - 1] = words_14[:]
 
         n = 2 * (LAST - 2)
-        quantize_z(LAST - 5, z_words[LAST - 5])
-        waiting.append(LAST - 5)
+        quantize_z_halves(LAST - 5)
         quantize_x(LAST - 1, 0, 4)
         new_x_words(LAST)
         interleave_x_gpsimd(LAST)
@@ -447,58 +461,59 @@ def tile_volterrathirdordermixer_t_kernel(tc, x_bytes, x_scale, mp, mq, mr, coef
         products(n + 2, "R")
         products(n + 3, "R")
         third_order(n + 2)
-        emit("O")
-        third_order(n + 3)
         times_q(n)
         products(n + 2, "Q")
+        emit("O")
+        third_order(n + 3)
         times_p(n - 1)
         products(n + 1, "P")
+        turn_z(LAST - 3, 1)
         interleave_z_scalar(LAST - 3)
-        project(waiting[0], "O")
-        project(waiting[1], "Z")
+        fetch_z(LAST - 3, nc.scalar.copy, 1)
+        emit("R0")
+        emit("O")
         times_q(n + 1)
         products(n + 3, "Q")
         times_p(n)
         products(n + 2, "P")
-        store(waiting.pop(0))
-        store(waiting.pop(0))
         times_p(n + 1)
 
         n = 2 * (LAST - 1)
-        quantize_z(LAST - 4, z_words[LAST - 4])
+        quantize_z_halves(LAST - 4)
         quantize_x(LAST, 0, 4)
         interleave_z_gpsimd(LAST - 2)
         products(n + 1, "P")
-        products(n + 2, "R")
-        products(n + 3, "R")
+        products(n + 2, "R", 1)
+        products(n + 3, "R", 0)
         third_order(n + 2)
-        emit("O")
         third_order(n + 3)
-        waiting.append(LAST - 4)
+        waiting.extend([LAST - 5, LAST - 4])
         times_q(n)
         products(n + 2, "Q")
         emit("Z")
         times_q(n + 1)
         products(n + 3, "Q")
+        emit("O")
         times_p(n)
         products(n + 2, "P")
-        project(waiting[0], "O")
+        emit("R1")
         quantize_z(LAST - 2, last_words[:, 4 * T - GATE :], -1)
         times_p(n + 1)
+        turn_z(LAST - 1, 1, "R0")
         products(n + 3, "P")
-        interleave_z_gpsimd(LAST - 1, SPLIT)
-        waiting.extend([LAST - 3, LAST - 2])
-        interleave_z_scalar(LAST - 1, SPLIT)
-        store(waiting.pop(0))
-        emit("R0")
-        emit("R1")
+        project(LAST - 3, "Z")
+        interleave_z_gpsimd(LAST - 1, P)
+        fetch_z(LAST - 1, nc.scalar.copy, 1)
+        store(LAST - 3)
+        project(LAST - 2, "O")
+        store(LAST - 2)
 
         n = 2 * LAST
         times_q(n)
         times_q(n + 1)
         times_p(n)
         quantize_z(LAST - 1, z_words[LAST - 1])
-        project(LAST - 1, "Z")
+        project(LAST - 1, "R1")
         store(LAST - 1)
         times_p(n + 1)
         for c in range(2):

@@ -23,6 +23,7 @@ SINGLE = 4
 HEAD = 2
 PIECE = 384
 RUN = 4
+PAD = 24
 GATE = 32
 LAST = NB - 1
 
@@ -106,8 +107,8 @@ def tile_volterrathirdordermixer_t_kernel(tc, x_bytes, x_scale, mp, mq, mr, coef
 
         def widen(engine, b, t, first=0, last=D):
             if b not in x_wide:
-                wide = wide_pool.tile([P, 4, D], BF16, name="wide", align_bytes=64)
-                x_wide[b] = wide
+                wide = wide_pool.tile([P, 4, D + PAD], BF16, name="wide", align_bytes=64)
+                x_wide[b] = wide[:, :, :D]
             dst = x_wide[b][:, t, first:last]
             src = x_raw[b][:, t * D + first : t * D + last].bitcast(FP8)
             if engine == "scalar":
@@ -124,20 +125,20 @@ def tile_volterrathirdordermixer_t_kernel(tc, x_bytes, x_scale, mp, mq, mr, coef
         def interleave_x_vector(b, j0, j1, g0=0):
             nc.vector.tensor_copy(
                 out=x_words[b].rearrange("p (j g i t) -> p g j t i", j=4, g=16, i=8, t=4)[:, g0:, j0:j1],
-                in_=x_wide[b][:].rearrange("p t (g j i) -> p g j t i", g=16, j=4, i=8)[:, g0:, j0:j1],
+                in_=x_wide[b].rearrange("p t (g j i) -> p g j t i", g=16, j=4, i=8)[:, g0:, j0:j1],
             )
 
         def interleave_x_scalar(b, j):
             nc.scalar.copy(
                 out=x_words[b].rearrange("p (j g i t) -> p g j i t", j=4, g=16, i=8, t=4)[:, :, j],
-                in_=x_wide[b][:].rearrange("p t (g j i) -> p g j i t", g=16, j=4, i=8)[:, :, j],
+                in_=x_wide[b].rearrange("p t (g j i) -> p g j i t", g=16, j=4, i=8)[:, :, j],
             )
 
         def interleave_x_gpsimd(b, tiles=4):
             blocks = gpsimd_blocks(b)
             nc.gpsimd.tensor_scalar(
                 out=x_words[b].rearrange("p (j g i t) -> p g j i t", j=4, g=16, i=8, t=4)[:, :blocks, :tiles],
-                in0=x_wide[b][:].rearrange("p t (g j i) -> p g j i t", g=16, j=4, i=8)[:, :blocks, :tiles],
+                in0=x_wide[b].rearrange("p t (g j i) -> p g j i t", g=16, j=4, i=8)[:, :blocks, :tiles],
                 scalar1=1.0,
                 scalar2=0.0,
                 op0=MULT,
@@ -279,18 +280,6 @@ def tile_volterrathirdordermixer_t_kernel(tc, x_bytes, x_scale, mp, mq, mr, coef
             for k in range(count):
                 z_codes[first + step * k], z_scales[first + step * k] = codes[:, k * T : (k + 1) * T], scales[:, k * T : (k + 1) * T]
 
-        def quantize_z_halves(b):
-            codes = zq_pool.tile([P, T], U32, name="z_q1", align_bytes=64)
-            scales = zq_pool.tile([P, T], U8, name="z_qs1", align_bytes=64)
-            for c in (1, 0):
-                cols = slice(c * P, (c + 1) * P)
-                nc.vector.quantize_mx(
-                    out=codes[:, cols].bitcast(X4),
-                    scales=scales[:, cols],
-                    in_=z_words[b][:, 4 * c * P : 4 * (c + 1) * P],
-                )
-            z_codes[b], z_scales[b] = codes[:], scales[:]
-
         def project(b, bank="O"):
             o_ps = psum.tile([P, 2, E], F32, name="o_ps", tag=bank)
             for c in range(2):
@@ -339,8 +328,12 @@ def tile_volterrathirdordermixer_t_kernel(tc, x_bytes, x_scale, mp, mq, mr, coef
         quantize_m(0)
         nc.vector.tensor_copy(out=vec_cols[:], in_=vec_ps[:, 0:12])
         quantize_m(1)
-        nc.vector.tensor_tensor(out=gain_coef[:, 0:4], in0=vec_cols[:, 0:4], in1=vec_cols[:, 8:12], op=MULT)
-        nc.vector.tensor_tensor(out=gain_coef[:, 4:8], in0=vec_cols[:, 4:8], in1=vec_cols[:, 8:12], op=MULT)
+        nc.vector.tensor_tensor(
+            out=gain_coef[:].rearrange("p (v j) -> p v j", v=2),
+            in0=vec_cols[:, 0:8].rearrange("p (v j) -> p v j", v=2),
+            in1=vec_cols[:, 8:12].unsqueeze(1).to_broadcast([P, 2, 4]),
+            op=MULT,
+        )
         products(0, "R")
         products(1, "R")
         products(0, "Q")
@@ -372,7 +365,7 @@ def tile_volterrathirdordermixer_t_kernel(tc, x_bytes, x_scale, mp, mq, mr, coef
                     in_=z_words["wo"],
                 )
             if b >= 3:
-                quantize_z_halves(b - 3)
+                quantize_z(b - 3, z_words[b - 3])
                 waiting.append(b - 3)
             new_x_words(b + 2)
             if b == 0:
@@ -453,7 +446,7 @@ def tile_volterrathirdordermixer_t_kernel(tc, x_bytes, x_scale, mp, mq, mr, coef
         z_words[LAST - 1] = words_14[:]
 
         n = 2 * (LAST - 2)
-        quantize_z_halves(LAST - 5)
+        quantize_z(LAST - 5, z_words[LAST - 5])
         quantize_x(LAST - 1, 0, 4)
         new_x_words(LAST)
         interleave_x_gpsimd(LAST)
@@ -479,7 +472,7 @@ def tile_volterrathirdordermixer_t_kernel(tc, x_bytes, x_scale, mp, mq, mr, coef
         times_p(n + 1)
 
         n = 2 * (LAST - 1)
-        quantize_z_halves(LAST - 4)
+        quantize_z(LAST - 4, z_words[LAST - 4])
         quantize_x(LAST, 0, 4)
         interleave_z_gpsimd(LAST - 2)
         products(n + 1, "P")

@@ -24,6 +24,7 @@ HEAD = 2
 PIECE = 384
 RUN = 4
 PAD = 24
+CUT = 192
 GATE = 32
 LAST = NB - 1
 
@@ -102,7 +103,7 @@ def tile_volterrathirdordermixer_t_kernel(tc, x_bytes, x_scale, mp, mq, mr, coef
         x_wide, x_words, x_codes, x_scales = {}, {}, {}, {}
         shared_words = []
         for k in range(2):
-            shared = const.tile([P, 4 * T - GATE + 4 * D], BF16, name="shared_words%d" % k, align_bytes=64)
+            shared = const.tile([P, 4 * D], BF16, name="shared_words%d" % k, align_bytes=64)
             shared_words.append(shared)
 
         def widen(engine, b, t, first=0, last=D):
@@ -117,7 +118,7 @@ def tile_volterrathirdordermixer_t_kernel(tc, x_bytes, x_scale, mp, mq, mr, coef
                 nc.vector.tensor_scalar(out=dst, in0=src, scalar1=scale[:, t : t + 1], scalar2=None, op0=MULT)
 
         def new_x_words(b):
-            words = shared_words[b % 2][:, 4 * T - GATE :]
+            words = shared_words[b % 2][:]
             codes = xq_pool.tile([P, D], U32, name="x_q", align_bytes=64)
             scales = xq_pool.tile([P, D], U8, name="x_qs", align_bytes=64)
             x_words[b], x_codes[b], x_scales[b] = words, codes, scales
@@ -356,6 +357,17 @@ def tile_volterrathirdordermixer_t_kernel(tc, x_bytes, x_scale, mp, mq, mr, coef
             project(waiting[0], bank)
             store(waiting.pop(0))
 
+        def turn_x(b):
+            turned = psum.tile([P, P, 4], BF16, name="x_turned", tag="O")
+            nc.tensor.matmul(
+                turned[:].rearrange("p (g i) t -> p t g i", i=8),
+                lhsT=ident_bf16[:],
+                rhs=x_wide[b].rearrange("p t (g j i) -> p j t g i", j=4, i=8)[:, 3],
+                start=True,
+                stop=True,
+            )
+            nc.scalar.copy(out=x_words[b][:, 3 * D :], in_=turned[:].rearrange("p n t -> p (n t)"))
+
         for b in range(LAST - 2):
             n = 2 * b
             if b == 2:
@@ -371,37 +383,35 @@ def tile_volterrathirdordermixer_t_kernel(tc, x_bytes, x_scale, mp, mq, mr, coef
             if b == 0:
                 interleave_x_vector(2, 0, 4, gpsimd_blocks(2))
                 widen("vector", 2, 3, 0, D - PIECE)
-            if b == 1:
-                widen("vector", 3, 3, PIECE)
+            else:
+                widen("vector", b + 2, 2, CUT)
+                widen("vector", b + 2, 3)
             quantize_x(b + 1, 0, 4)
-            interleave_x_gpsimd(b + 2)
+            interleave_x_gpsimd(b + 2, 3 if b else 4)
             times_q(n)
             widen("scalar", b + 3, 1)
-            if b >= 3 and b % 2:
-                emit()
-            if b + 4 == NB:
-                project(waiting[0])
+            if b >= 1:
+                turned = b - 2 if b >= 2 else "wo"
+                words = z_pool.tile([P, 4 * T], BF16, name="z_words", align_bytes=64)
+                z_words[turned] = words[:]
+                fetch_z(turned, nc.scalar.copy)
+                turn_x(b + 2)
+            widen("scalar", b + 3, 2, 0, CUT)
             products(n + 2, "R")
             products(n + 3, "R")
             products(n + 2, "Q")
-            widen("scalar", b + 3, 2)
-            widen("scalar", b + 3, 3, 0, D if b else PIECE)
             third_order(n + 2)
+            third_order(n + 3)
             if b >= 1:
                 times_p(n - 1)
             products(n + 1, "P")
-            if b >= 1:
-                turned = b - 2 if b >= 2 else "wo"
-                z_words[turned] = shared_words[(b + 1) % 2][:, : 4 * T]
-                fetch_z(turned, nc.vector.tensor_copy)
+            if b >= 3 and b % 3 != 2:
+                emit()
             turn_z(b - 1 if b else "wo")
             times_q(n + 1)
             products(n + 3, "Q")
-            third_order(n + 3)
             if b + 4 < NB:
                 widen("scalar", b + 4, 0)
-            else:
-                store(waiting.pop(0))
             times_p(n)
             products(n + 2, "P")
 
@@ -447,6 +457,8 @@ def tile_volterrathirdordermixer_t_kernel(tc, x_bytes, x_scale, mp, mq, mr, coef
 
         n = 2 * (LAST - 2)
         quantize_z(LAST - 5, z_words[LAST - 5])
+        widen("vector", LAST, 2, CUT)
+        widen("vector", LAST, 3)
         quantize_x(LAST - 1, 0, 4)
         new_x_words(LAST)
         interleave_x_gpsimd(LAST)
@@ -455,11 +467,10 @@ def tile_volterrathirdordermixer_t_kernel(tc, x_bytes, x_scale, mp, mq, mr, coef
         products(n + 3, "R")
         third_order(n + 2)
         times_q(n)
-        products(n + 2, "Q")
-        emit("O")
-        third_order(n + 3)
         times_p(n - 1)
         products(n + 1, "P")
+        third_order(n + 3)
+        products(n + 2, "Q")
         turn_z(LAST - 3, 1)
         interleave_z_scalar(LAST - 3)
         fetch_z(LAST - 3, nc.scalar.copy, 1)

@@ -25,12 +25,15 @@ PIECE = 384
 RUN = 4
 PAD = 24
 CUT = 192
+CUTS = {2: 0, 3: 64, NB - 1: 256}
+VHEAD = False
+STRIDED = 1
 GATE = 32
 LAST = NB - 1
 
 
-def gpsimd_blocks(b):
-    return {2: 8}.get(b, 16)
+def cut(b):
+    return CUTS.get(b, CUT)
 
 
 def tile_volterrathirdordermixer_t_kernel(tc, x_bytes, x_scale, mp, mq, mr, coef, gain, wo, out):
@@ -41,7 +44,7 @@ def tile_volterrathirdordermixer_t_kernel(tc, x_bytes, x_scale, mp, mq, mr, coef
         wide_pool = ctx.enter_context(tc.tile_pool(name="wide_pool", bufs=4))
         xq_pool = ctx.enter_context(tc.tile_pool(name="xq_pool", bufs=5))
         poly = ctx.enter_context(tc.tile_pool(name="poly", bufs=4))
-        z_pool = ctx.enter_context(tc.tile_pool(name="z_pool", bufs=3))
+        z_pool = ctx.enter_context(tc.tile_pool(name="z_pool", bufs=4))
         zq_pool = ctx.enter_context(tc.tile_pool(name="zq_pool", bufs=7))
         out_pool = ctx.enter_context(tc.tile_pool(name="out_pool", bufs=8))
         psum = ctx.enter_context(tc.psum_pool(name="psum", bufs=1))
@@ -136,10 +139,9 @@ def tile_volterrathirdordermixer_t_kernel(tc, x_bytes, x_scale, mp, mq, mr, coef
             )
 
         def interleave_x_gpsimd(b, tiles=4):
-            blocks = gpsimd_blocks(b)
             nc.gpsimd.tensor_scalar(
-                out=x_words[b].rearrange("p (j g i t) -> p g j i t", j=4, g=16, i=8, t=4)[:, :blocks, :tiles],
-                in0=x_wide[b].rearrange("p t (g j i) -> p g j i t", g=16, j=4, i=8)[:, :blocks, :tiles],
+                out=x_words[b].rearrange("p (j g i t) -> p g j i t", j=4, g=16, i=8, t=4)[:, :, :tiles],
+                in0=x_wide[b].rearrange("p t (g j i) -> p g j i t", g=16, j=4, i=8)[:, :, :tiles],
                 scalar1=1.0,
                 scalar2=0.0,
                 op0=MULT,
@@ -325,8 +327,9 @@ def tile_volterrathirdordermixer_t_kernel(tc, x_bytes, x_scale, mp, mq, mr, coef
         quantize_x(0, 0, 2)
         quantize_x(0, 2, 4)
         new_x_words(1)
-        interleave_x_vector(1, 0, 2)
+        interleave_x_vector(1, 0, 1)
         quantize_m(0)
+        interleave_x_vector(1, 1, 2)
         nc.vector.tensor_copy(out=vec_cols[:], in_=vec_ps[:, 0:12])
         quantize_m(1)
         nc.vector.tensor_tensor(
@@ -344,18 +347,23 @@ def tile_volterrathirdordermixer_t_kernel(tc, x_bytes, x_scale, mp, mq, mr, coef
         widen("scalar", 2, 1)
         third_order(0)
         third_order(1)
-        widen("vector", 2, 2)
-        widen("vector", 2, 3, D - PIECE)
         quantize_m(2)
         products(0, "P")
+        products(1, "P")
         z_tile["wo"] = wo_rows
         widen("scalar", 3, 0)
+        widen("scalar", 3, 2, 0, cut(3))
 
         waiting = []
 
         def emit(bank="O"):
             project(waiting[0], bank)
             store(waiting.pop(0))
+
+        def widen_rest(b):
+            if cut(b) < D:
+                widen("vector", b, 2, cut(b))
+            widen("vector", b, 3, max(0, cut(b) - D))
 
         def turn_x(b):
             turned = psum.tile([P, P, 4], BF16, name="x_turned", tag="O")
@@ -368,7 +376,8 @@ def tile_volterrathirdordermixer_t_kernel(tc, x_bytes, x_scale, mp, mq, mr, coef
             )
             nc.scalar.copy(out=x_words[b][:, 3 * D :], in_=turned[:].rearrange("p n t -> p (n t)"))
 
-        for b in range(LAST - 2):
+        chained = const.tile([P, 8 * T - GATE], BF16, name="chained", align_bytes=64)
+        for b in range(LAST - 1):
             n = 2 * b
             if b == 2:
                 nc.vector.quantize_mx(
@@ -380,40 +389,51 @@ def tile_volterrathirdordermixer_t_kernel(tc, x_bytes, x_scale, mp, mq, mr, coef
                 quantize_z(b - 3, z_words[b - 3])
                 waiting.append(b - 3)
             new_x_words(b + 2)
-            if b == 0:
-                interleave_x_vector(2, 0, 4, gpsimd_blocks(2))
-                widen("vector", 2, 3, 0, D - PIECE)
-            else:
-                widen("vector", b + 2, 2, CUT)
-                widen("vector", b + 2, 3)
+            if b == 0 and VHEAD:
+                widen("vector", 2, 2)
+                widen("vector", 2, 3, 0, D - 128)
+                quantize_m(2)
+                products(0, "P")
+                products(1, "P")
+                interleave_x_vector(2, 3, 4)
+            widen_rest(b + 2)
             quantize_x(b + 1, 0, 4)
-            interleave_x_gpsimd(b + 2, 3 if b else 4)
-            times_q(n)
-            widen("scalar", b + 3, 1)
-            if b >= 1:
-                turned = b - 2 if b >= 2 else "wo"
+            interleave_x_gpsimd(b + 2, 3)
+            if b + 3 < NB:
+                widen("scalar", b + 3, 1)
+            if b + 2 > LAST - STRIDED:
+                interleave_x_scalar(b + 2, 3)
+            turned = b - 1 if b else "wo"
+            if turned == LAST - 4:
+                z_words[turned] = chained[:, : 4 * T]
+            else:
                 words = z_pool.tile([P, 4 * T], BF16, name="z_words", align_bytes=64)
                 z_words[turned] = words[:]
+            if b:
+                turn_z(turned)
                 fetch_z(turned, nc.scalar.copy)
+            if b + 2 <= LAST - STRIDED and (b or not VHEAD):
                 turn_x(b + 2)
-            widen("scalar", b + 3, 2, 0, CUT)
             products(n + 2, "R")
             products(n + 3, "R")
-            products(n + 2, "Q")
             third_order(n + 2)
             third_order(n + 3)
-            if b >= 1:
-                times_p(n - 1)
-            products(n + 1, "P")
-            if b >= 3 and b % 3 != 2:
-                emit()
-            turn_z(b - 1 if b else "wo")
+            if b == 0:
+                turn_z(turned)
+                fetch_z(turned, nc.scalar.copy)
+            times_q(n)
+            products(n + 2, "Q")
             times_q(n + 1)
             products(n + 3, "Q")
+            if b >= 3 and (b % 2 or b == 12):
+                emit()
             if b + 4 < NB:
                 widen("scalar", b + 4, 0)
+                widen("scalar", b + 4, 2, 0, cut(b + 4))
             times_p(n)
             products(n + 2, "P")
+            times_p(n + 1)
+            products(n + 3, "P")
 
         half_words, half_sums = [], []
 
@@ -431,7 +451,7 @@ def tile_volterrathirdordermixer_t_kernel(tc, x_bytes, x_scale, mp, mq, mr, coef
             nc.vector.quantize_mx(
                 out=codes[:].bitcast(X4), scales=scales[:], in_=half_words[c][:].rearrange("p t j -> p (t j)")
             )
-            half_ps = psum.tile([P, E], F32, name="half_ps", tag="RQ"[c] + "0")
+            half_ps = psum.tile([P, E], F32, name="half_ps", tag="Q" + "01"[c])
             nc.tensor.matmul_mx(
                 out=half_ps[:],
                 lhsT=codes[:].bitcast(X4),
@@ -448,76 +468,46 @@ def tile_volterrathirdordermixer_t_kernel(tc, x_bytes, x_scale, mp, mq, mr, coef
             copy(out=half_sb[:], in_=half_sums[c][:])
             nc.sync.dma_start(out=out[LAST].rearrange("(p c) e -> p c e", c=2)[:, c, :], in_=half_sb[:])
 
-        last_words = const.tile([P, 12 * T - GATE], BF16, name="last_words", align_bytes=64)
-        z_words[LAST - 4] = last_words[:, : 4 * T]
-        z_words[LAST - 2] = last_words[:, 4 * T - GATE : 8 * T - GATE]
-        z_words[LAST - 3] = last_words[:, 8 * T - GATE :]
-        words_14 = const.tile([P, 4 * T], BF16, name="words_14", align_bytes=64)
-        z_words[LAST - 1] = words_14[:]
-
-        n = 2 * (LAST - 2)
-        quantize_z(LAST - 5, z_words[LAST - 5])
-        widen("vector", LAST, 2, CUT)
-        widen("vector", LAST, 3)
-        quantize_x(LAST - 1, 0, 4)
-        new_x_words(LAST)
-        interleave_x_gpsimd(LAST)
-        fetch_z(LAST - 4, nc.scalar.copy)
-        products(n + 2, "R")
-        products(n + 3, "R")
-        third_order(n + 2)
-        times_q(n)
-        times_p(n - 1)
-        products(n + 1, "P")
-        third_order(n + 3)
-        products(n + 2, "Q")
-        turn_z(LAST - 3, 1)
-        interleave_z_scalar(LAST - 3)
-        fetch_z(LAST - 3, nc.scalar.copy, 1)
-        emit("R0")
-        emit("O")
-        times_q(n + 1)
-        products(n + 3, "Q")
-        times_p(n)
-        products(n + 2, "P")
-        times_p(n + 1)
-
         n = 2 * (LAST - 1)
         quantize_z(LAST - 4, z_words[LAST - 4])
         quantize_x(LAST, 0, 4)
+        z_words[LAST - 2] = chained[:, 4 * T - GATE :]
+        words_14 = const.tile([P, 4 * T], BF16, name="words_14", align_bytes=64)
+        z_words[LAST - 1] = words_14[:]
         interleave_z_gpsimd(LAST - 2)
-        products(n + 1, "P")
-        products(n + 2, "R", 1)
-        products(n + 3, "R", 0)
+        waiting.append(LAST - 4)
+        emit("Z")
+        products(n + 2, "R")
         third_order(n + 2)
+        products(n + 3, "R")
         third_order(n + 3)
-        waiting.extend([LAST - 5, LAST - 4])
         times_q(n)
         products(n + 2, "Q")
-        emit("Z")
+        emit("O")
         times_q(n + 1)
         products(n + 3, "Q")
-        emit("O")
+        emit("Z")
+        emit("R0")
         times_p(n)
         products(n + 2, "P")
-        emit("R1")
-        quantize_z(LAST - 2, last_words[:, 4 * T - GATE :], -1)
+        quantize_z(LAST - 3, z_words[LAST - 3])
+        quantize_z(LAST - 2, z_words[LAST - 2])
+        waiting.extend([LAST - 3, LAST - 2])
         times_p(n + 1)
-        turn_z(LAST - 1, 1, "R0")
+        turn_z(LAST - 1, 1, "R1")
         products(n + 3, "P")
-        project(LAST - 3, "Z")
         interleave_z_gpsimd(LAST - 1, P)
         fetch_z(LAST - 1, nc.scalar.copy, 1)
-        store(LAST - 3)
-        project(LAST - 2, "O")
-        store(LAST - 2)
+        emit("O")
+        emit("Z")
+        emit("R0")
 
         n = 2 * LAST
         times_q(n)
         times_q(n + 1)
         times_p(n)
         quantize_z(LAST - 1, z_words[LAST - 1])
-        project(LAST - 1, "R1")
+        project(LAST - 1, "P0")
         store(LAST - 1)
         times_p(n + 1)
         for c in range(2):

@@ -18,22 +18,15 @@ IDENTITY = mybir.ActivationFunctionType.Identity
 ADD = mybir.AluOpType.add
 MULT = mybir.AluOpType.mult
 
-STEPS = 2 * NB
 SINGLE = 4
-HEAD = 2
-PIECE = 384
-RUN = 4
-PAD = 24
-CUT = 192
-CUTS = {2: 0, 3: 64, NB - 1: 256}
-VHEAD = False
-STRIDED = 1
-GATE = 32
 LAST = NB - 1
+PITCH = D + 24
+RUN = 4
+GATE = 32
 
 
-def cut(b):
-    return CUTS.get(b, CUT)
+def scalar_share(b):
+    return {2: 0, 3: 512, 4: 512}.get(b, 208)
 
 
 def tile_volterrathirdordermixer_t_kernel(tc, x_bytes, x_scale, mp, mq, mr, coef, gain, wo, out):
@@ -104,14 +97,14 @@ def tile_volterrathirdordermixer_t_kernel(tc, x_bytes, x_scale, mp, mq, mr, coef
         nc.scalar.activation(out=ident_bf16[:], in_=ident_f32[:], func=COPY)
 
         x_wide, x_words, x_codes, x_scales = {}, {}, {}, {}
-        shared_words = []
+        word_buffers = []
         for k in range(2):
-            shared = const.tile([P, 4 * D], BF16, name="shared_words%d" % k, align_bytes=64)
-            shared_words.append(shared)
+            buffer = const.tile([P, 4 * D], BF16, name="x_words%d" % k, align_bytes=64)
+            word_buffers.append(buffer)
 
         def widen(engine, b, t, first=0, last=D):
             if b not in x_wide:
-                wide = wide_pool.tile([P, 4, D + PAD], BF16, name="wide", align_bytes=64)
+                wide = wide_pool.tile([P, 4, PITCH], BF16, name="wide", align_bytes=64)
                 x_wide[b] = wide[:, :, :D]
             dst = x_wide[b][:, t, first:last]
             src = x_raw[b][:, t * D + first : t * D + last].bitcast(FP8)
@@ -120,35 +113,51 @@ def tile_volterrathirdordermixer_t_kernel(tc, x_bytes, x_scale, mp, mq, mr, coef
             else:
                 nc.vector.tensor_scalar(out=dst, in0=src, scalar1=scale[:, t : t + 1], scalar2=None, op0=MULT)
 
+        def widen_rest(b):
+            if scalar_share(b) < D:
+                widen("vector", b, 2, scalar_share(b))
+            widen("vector", b, 3, max(0, scalar_share(b) - D))
+
         def new_x_words(b):
-            words = shared_words[b % 2][:]
+            words = word_buffers[b % 2][:]
             codes = xq_pool.tile([P, D], U32, name="x_q", align_bytes=64)
             scales = xq_pool.tile([P, D], U8, name="x_qs", align_bytes=64)
             x_words[b], x_codes[b], x_scales[b] = words, codes, scales
 
-        def interleave_x_vector(b, j0, j1, g0=0):
+        def interleave_x_vector(b, j0, j1):
             nc.vector.tensor_copy(
-                out=x_words[b].rearrange("p (j g i t) -> p g j t i", j=4, g=16, i=8, t=4)[:, g0:, j0:j1],
-                in_=x_wide[b].rearrange("p t (g j i) -> p g j t i", g=16, j=4, i=8)[:, g0:, j0:j1],
+                out=x_words[b].rearrange("p (j g i t) -> p g j t i", j=4, g=16, i=8, t=4)[:, :, j0:j1],
+                in_=x_wide[b].rearrange("p t (g j i) -> p g j t i", g=16, j=4, i=8)[:, :, j0:j1],
             )
 
-        def interleave_x_scalar(b, j):
+        def interleave_x_scalar(b):
             nc.scalar.copy(
-                out=x_words[b].rearrange("p (j g i t) -> p g j i t", j=4, g=16, i=8, t=4)[:, :, j],
-                in_=x_wide[b].rearrange("p t (g j i) -> p g j i t", g=16, j=4, i=8)[:, :, j],
+                out=x_words[b].rearrange("p (j g i t) -> p g j i t", j=4, g=16, i=8, t=4)[:, :, 3],
+                in_=x_wide[b].rearrange("p t (g j i) -> p g j i t", g=16, j=4, i=8)[:, :, 3],
             )
 
-        def interleave_x_gpsimd(b, tiles=4):
+        def interleave_x_gpsimd(b):
             nc.gpsimd.tensor_scalar(
-                out=x_words[b].rearrange("p (j g i t) -> p g j i t", j=4, g=16, i=8, t=4)[:, :, :tiles],
-                in0=x_wide[b].rearrange("p t (g j i) -> p g j i t", g=16, j=4, i=8)[:, :, :tiles],
+                out=x_words[b].rearrange("p (j g i t) -> p g j i t", j=4, g=16, i=8, t=4)[:, :, :3],
+                in0=x_wide[b].rearrange("p t (g j i) -> p g j i t", g=16, j=4, i=8)[:, :, :3],
                 scalar1=1.0,
                 scalar2=0.0,
                 op0=MULT,
                 op1=ADD,
             )
 
-        def quantize_x(b, j0, j1):
+        def turn_x(b):
+            turned = psum.tile([P, P, 4], BF16, name="x_turned", tag="O")
+            nc.tensor.matmul(
+                turned[:].rearrange("p (g i) t -> p t g i", i=8),
+                lhsT=ident_bf16[:],
+                rhs=x_wide[b].rearrange("p t (g j i) -> p j t g i", j=4, i=8)[:, 3],
+                start=True,
+                stop=True,
+            )
+            nc.scalar.copy(out=x_words[b][:, 3 * D :], in_=turned[:].rearrange("p n t -> p (n t)"))
+
+        def quantize_x(b, j0=0, j1=4):
             cols = slice(j0 * P, j1 * P)
             nc.vector.quantize_mx(
                 out=x_codes[b][:, cols].bitcast(X4),
@@ -166,12 +175,13 @@ def tile_volterrathirdordermixer_t_kernel(tc, x_bytes, x_scale, mp, mq, mr, coef
                     nc.tensor.transpose(turned[:, c, u, :], words[:, u : S // 2 : 2], ident_f32[:])
             m_turned.append(turned)
 
-        def fetch_m(i, engine):
+        def fetch_m(i):
             turned = m_turned[i]
             grouped = const.tile([P, T, 4], BF16, name="m_words%d" % i, align_bytes=64)
             dst = grouped[:].rearrange("p n t -> p (n t)").bitcast(F32)
-            copy = nc.scalar.copy if engine == "scalar" else nc.vector.tensor_copy
-            copy(out=dst.rearrange("p (c n u) -> p c n u", c=2, u=2), in_=turned[:].rearrange("p c u n -> p c n u"))
+            nc.scalar.copy(
+                out=dst.rearrange("p (c n u) -> p c n u", c=2, u=2), in_=turned[:].rearrange("p c u n -> p c n u")
+            )
             m_words.append(grouped)
 
         def quantize_m(i):
@@ -191,23 +201,22 @@ def tile_volterrathirdordermixer_t_kernel(tc, x_bytes, x_scale, mp, mq, mr, coef
                 return [(j, slice(c * P, (c + 1) * P), slice(j * P, (j + 1) * P)) for j in range(4)]
             return [(2 * (n % 2) + k, slice(0, T), slice(k * T, (k + 1) * T)) for k in range(2)]
 
-        def products(n, names, side=None):
+        def products(n, name):
             b = n // 2
-            for name in names:
-                i = "RQP".index(name)
-                ps = psum.tile([P, 2 * T], F32, name="sum_ps", tag=name + "01"[n % 2 if side is None else side])
-                for j, times, bank in units(n):
-                    cols = slice(j * P, (j + 1) * P)
-                    nc.tensor.matmul_mx(
-                        out=ps[:, bank],
-                        lhsT=x_codes[b][:, cols].bitcast(X4),
-                        lhsT_scale=x_scales[b][:, cols],
-                        rhs=m_codes[i][:, times].bitcast(X4),
-                        rhs_scale=m_scales[i][:, times],
-                        start=True,
-                        stop=True,
-                    )
-                sums[name, n] = ps
+            i = "RQP".index(name)
+            ps = psum.tile([P, 2 * T], F32, name="sum_ps", tag=name + "01"[n % 2])
+            for j, times, bank in units(n):
+                cols = slice(j * P, (j + 1) * P)
+                nc.tensor.matmul_mx(
+                    out=ps[:, bank],
+                    lhsT=x_codes[b][:, cols].bitcast(X4),
+                    lhsT_scale=x_scales[b][:, cols],
+                    rhs=m_codes[i][:, times].bitcast(X4),
+                    rhs_scale=m_scales[i][:, times],
+                    start=True,
+                    stop=True,
+                )
+            sums[name, n] = ps
 
         def third_order(n):
             h = poly.tile([P, 2 * T], F32, name="h", align_bytes=64)
@@ -256,8 +265,10 @@ def tile_volterrathirdordermixer_t_kernel(tc, x_bytes, x_scale, mp, mq, mr, coef
                 )
             z_turned[b] = turned
 
-        def fetch_z(b, copy, first=0):
-            copy(out=z_words[b][:, 4 * first * P :], in_=z_turned[b][:, first * P :, :].rearrange("p t j -> p (t j)"))
+        def fetch_z(b, first=0):
+            nc.scalar.copy(
+                out=z_words[b][:, 4 * first * P :], in_=z_turned[b][:, first * P :, :].rearrange("p t j -> p (t j)")
+            )
 
         def interleave_z_gpsimd(b, times=T):
             nc.gpsimd.tensor_scalar(
@@ -269,19 +280,11 @@ def tile_volterrathirdordermixer_t_kernel(tc, x_bytes, x_scale, mp, mq, mr, coef
                 op1=ADD,
             )
 
-        def interleave_z_scalar(b):
-            nc.scalar.copy(
-                out=z_words[b].rearrange("p (c i j) -> p c j i", i=RUN, j=4)[:, : P // RUN],
-                in_=z_tile[b][:].rearrange("p j (c i) -> p c j i", i=RUN)[:, : P // RUN],
-            )
-
-        def quantize_z(first, words, step=1):
-            count = words.shape[1] // (4 * T)
-            codes = zq_pool.tile([P, count * T], U32, name="z_q%d" % count, align_bytes=64)
-            scales = zq_pool.tile([P, count * T], U8, name="z_qs%d" % count, align_bytes=64)
-            nc.vector.quantize_mx(out=codes[:].bitcast(X4), scales=scales[:], in_=words)
-            for k in range(count):
-                z_codes[first + step * k], z_scales[first + step * k] = codes[:, k * T : (k + 1) * T], scales[:, k * T : (k + 1) * T]
+        def quantize_z(b):
+            codes = zq_pool.tile([P, T], U32, name="z_q", align_bytes=64)
+            scales = zq_pool.tile([P, T], U8, name="z_qs", align_bytes=64)
+            nc.vector.quantize_mx(out=codes[:].bitcast(X4), scales=scales[:], in_=z_words[b])
+            z_codes[b], z_scales[b] = codes, scales
 
         def project(b, bank="O"):
             o_ps = psum.tile([P, 2, E], F32, name="o_ps", tag=bank)
@@ -320,7 +323,7 @@ def tile_volterrathirdordermixer_t_kernel(tc, x_bytes, x_scale, mp, mq, mr, coef
         for t in (0, 1, 2):
             widen("scalar", 1, t)
         for i in range(3):
-            fetch_m(i, "scalar")
+            fetch_m(i)
         new_x_words(0)
         interleave_x_vector(0, 0, 2)
         interleave_x_vector(0, 2, 4)
@@ -350,9 +353,8 @@ def tile_volterrathirdordermixer_t_kernel(tc, x_bytes, x_scale, mp, mq, mr, coef
         quantize_m(2)
         products(0, "P")
         products(1, "P")
-        z_tile["wo"] = wo_rows
         widen("scalar", 3, 0)
-        widen("scalar", 3, 2, 0, cut(3))
+        widen("scalar", 3, 2, 0, scalar_share(3))
 
         waiting = []
 
@@ -360,86 +362,61 @@ def tile_volterrathirdordermixer_t_kernel(tc, x_bytes, x_scale, mp, mq, mr, coef
             project(waiting[0], bank)
             store(waiting.pop(0))
 
-        def widen_rest(b):
-            if cut(b) < D:
-                widen("vector", b, 2, cut(b))
-            widen("vector", b, 3, max(0, cut(b) - D))
-
-        def turn_x(b):
-            turned = psum.tile([P, P, 4], BF16, name="x_turned", tag="O")
-            nc.tensor.matmul(
-                turned[:].rearrange("p (g i) t -> p t g i", i=8),
-                lhsT=ident_bf16[:],
-                rhs=x_wide[b].rearrange("p t (g j i) -> p j t g i", j=4, i=8)[:, 3],
-                start=True,
-                stop=True,
-            )
-            nc.scalar.copy(out=x_words[b][:, 3 * D :], in_=turned[:].rearrange("p n t -> p (n t)"))
-
         chained = const.tile([P, 8 * T - GATE], BF16, name="chained", align_bytes=64)
+        wo_words = const.tile([P, E, 4], BF16, name="wo_words", align_bytes=64)
         for b in range(LAST - 1):
             n = 2 * b
+            if b == 1:
+                nc.vector.tensor_copy(
+                    out=wo_words[:].rearrange("p (c i) j -> p c j i", i=RUN),
+                    in_=wo_rows[:].rearrange("p j (c i) -> p c j i", i=RUN),
+                )
             if b == 2:
                 nc.vector.quantize_mx(
-                    out=wo_codes[:].bitcast(X4),
-                    scales=wo_scales[:],
-                    in_=z_words["wo"],
+                    out=wo_codes[:].bitcast(X4), scales=wo_scales[:], in_=wo_words[:].rearrange("p e j -> p (e j)")
                 )
             if b >= 3:
-                quantize_z(b - 3, z_words[b - 3])
+                quantize_z(b - 3)
                 waiting.append(b - 3)
             new_x_words(b + 2)
-            if b == 0 and VHEAD:
-                widen("vector", 2, 2)
-                widen("vector", 2, 3, 0, D - 128)
-                quantize_m(2)
-                products(0, "P")
-                products(1, "P")
-                interleave_x_vector(2, 3, 4)
             widen_rest(b + 2)
-            quantize_x(b + 1, 0, 4)
-            interleave_x_gpsimd(b + 2, 3)
-            if b + 3 < NB:
+            quantize_x(b + 1)
+            interleave_x_gpsimd(b + 2)
+            if b + 2 < LAST:
                 widen("scalar", b + 3, 1)
-            if b + 2 > LAST - STRIDED:
-                interleave_x_scalar(b + 2, 3)
-            turned = b - 1 if b else "wo"
-            if turned == LAST - 4:
-                z_words[turned] = chained[:, : 4 * T]
             else:
-                words = z_pool.tile([P, 4 * T], BF16, name="z_words", align_bytes=64)
-                z_words[turned] = words[:]
-            if b:
-                turn_z(turned)
-                fetch_z(turned, nc.scalar.copy)
-            if b + 2 <= LAST - STRIDED and (b or not VHEAD):
+                interleave_x_scalar(LAST)
+            if b >= 1:
+                if b - 1 == LAST - 4:
+                    z_words[b - 1] = chained[:, : 4 * T]
+                else:
+                    words = z_pool.tile([P, 4 * T], BF16, name="z_words", align_bytes=64)
+                    z_words[b - 1] = words[:]
+                turn_z(b - 1)
+                fetch_z(b - 1)
+            if b + 2 < LAST:
                 turn_x(b + 2)
-            products(n + 2, "R")
-            products(n + 3, "R")
-            third_order(n + 2)
-            third_order(n + 3)
-            if b == 0:
-                turn_z(turned)
-                fetch_z(turned, nc.scalar.copy)
-            times_q(n)
-            products(n + 2, "Q")
-            times_q(n + 1)
-            products(n + 3, "Q")
-            if b >= 3 and (b % 2 or b == 12):
+            for k in (n + 2, n + 3):
+                products(k, "R")
+            for k in (n + 2, n + 3):
+                third_order(k)
+            for k in (n, n + 1):
+                times_q(k)
+                products(k + 2, "Q")
+            if b >= 3 and (b % 2 or b + 4 >= NB):
                 emit()
             if b + 4 < NB:
                 widen("scalar", b + 4, 0)
-                widen("scalar", b + 4, 2, 0, cut(b + 4))
-            times_p(n)
-            products(n + 2, "P")
-            times_p(n + 1)
-            products(n + 3, "P")
+                widen("scalar", b + 4, 2, 0, scalar_share(b + 4))
+            for k in (n, n + 1):
+                times_p(k)
+                products(k + 2, "P")
 
         half_words, half_sums = [], []
 
-        def interleave_half(c, copy):
+        def interleave_half(c):
             words = zq_pool.tile([P, P, 4], BF16, name="half_words%d" % c, align_bytes=64)
-            copy(
+            nc.vector.tensor_copy(
                 out=words[:].rearrange("p (c i) j -> p c j i", i=RUN),
                 in_=z_tile[LAST][:, :, c * P : (c + 1) * P].rearrange("p j (c i) -> p c j i", i=RUN),
             )
@@ -469,36 +446,37 @@ def tile_volterrathirdordermixer_t_kernel(tc, x_bytes, x_scale, mp, mq, mr, coef
             nc.sync.dma_start(out=out[LAST].rearrange("(p c) e -> p c e", c=2)[:, c, :], in_=half_sb[:])
 
         n = 2 * (LAST - 1)
-        quantize_z(LAST - 4, z_words[LAST - 4])
-        quantize_x(LAST, 0, 4)
+        quantize_z(LAST - 4)
+        quantize_x(LAST)
         z_words[LAST - 2] = chained[:, 4 * T - GATE :]
-        words_14 = const.tile([P, 4 * T], BF16, name="words_14", align_bytes=64)
-        z_words[LAST - 1] = words_14[:]
+        late_words = const.tile([P, 4 * T], BF16, name="late_words", align_bytes=64)
+        z_words[LAST - 1] = late_words[:]
         interleave_z_gpsimd(LAST - 2)
         waiting.append(LAST - 4)
         emit("Z")
         products(n + 2, "R")
         third_order(n + 2)
         products(n + 3, "R")
+        emit("O")
         third_order(n + 3)
         times_q(n)
         products(n + 2, "Q")
-        emit("O")
         times_q(n + 1)
         products(n + 3, "Q")
         emit("Z")
         emit("R0")
         times_p(n)
         products(n + 2, "P")
-        quantize_z(LAST - 3, z_words[LAST - 3])
-        quantize_z(LAST - 2, z_words[LAST - 2])
+        quantize_z(LAST - 3)
+        quantize_z(LAST - 2)
         waiting.extend([LAST - 3, LAST - 2])
+        project(waiting[0], "O")
         times_p(n + 1)
         turn_z(LAST - 1, 1, "R1")
         products(n + 3, "P")
         interleave_z_gpsimd(LAST - 1, P)
-        fetch_z(LAST - 1, nc.scalar.copy, 1)
-        emit("O")
+        fetch_z(LAST - 1, 1)
+        store(waiting.pop(0))
         emit("Z")
         emit("R0")
 
@@ -506,12 +484,12 @@ def tile_volterrathirdordermixer_t_kernel(tc, x_bytes, x_scale, mp, mq, mr, coef
         times_q(n)
         times_q(n + 1)
         times_p(n)
-        quantize_z(LAST - 1, z_words[LAST - 1])
+        quantize_z(LAST - 1)
         project(LAST - 1, "P0")
         store(LAST - 1)
         times_p(n + 1)
         for c in range(2):
-            interleave_half(c, nc.vector.tensor_copy)
+            interleave_half(c)
         for c in range(2):
             project_half(c)
         store_half(0, nc.scalar.copy)

@@ -26,7 +26,7 @@ GATE = 32
 
 
 def scalar_share(b):
-    return {2: 0, 3: 512, 4: 512}.get(b, 208)
+    return {2: 0, 3: 256, 4: 256}.get(b, 208)
 
 
 def tile_volterrathirdordermixer_t_kernel(tc, x_bytes, x_scale, mp, mq, mr, coef, gain, wo, out):
@@ -148,13 +148,14 @@ def tile_volterrathirdordermixer_t_kernel(tc, x_bytes, x_scale, mp, mq, mr, coef
 
         def turn_x(b):
             turned = psum.tile([P, P, 4], BF16, name="x_turned", tag="O")
-            nc.tensor.matmul(
-                turned[:].rearrange("p (g i) t -> p t g i", i=8),
-                lhsT=ident_bf16[:],
-                rhs=x_wide[b].rearrange("p t (g j i) -> p j t g i", j=4, i=8)[:, 3],
-                start=True,
-                stop=True,
-            )
+            for u in range(2):
+                nc.tensor.matmul(
+                    turned[:, :, 2 * u : 2 * u + 2].rearrange("p (g i) t -> p g i t", i=8),
+                    lhsT=ident_bf16[:],
+                    rhs=x_wide[b][:, 2 * u : 2 * u + 2, :].rearrange("p t (g j i) -> p j g i t", j=4, i=8)[:, 3],
+                    start=True,
+                    stop=True,
+                )
             nc.scalar.copy(out=x_words[b][:, 3 * D :], in_=turned[:].rearrange("p n t -> p (n t)"))
 
         def quantize_x(b, j0=0, j1=4):
@@ -254,12 +255,11 @@ def tile_volterrathirdordermixer_t_kernel(tc, x_bytes, x_scale, mp, mq, mr, coef
 
         def turn_z(b, first=0, bank="Z"):
             turned = psum.tile([P, T, 4], BF16, name="z_turned", tag=bank)
-            for c in range(first, 2):
-                t = slice(c * P, (c + 1) * P)
+            for u in range(2):
                 nc.tensor.matmul(
-                    turned[:, t, :].rearrange("p t j -> p j t"),
+                    turned[:, first * P :, 2 * u : 2 * u + 2],
                     lhsT=ident_bf16[:],
-                    rhs=z_tile[b][:, :, t],
+                    rhs=z_tile[b][:, 2 * u : 2 * u + 2, first * P :].rearrange("p j t -> p t j"),
                     start=True,
                     stop=True,
                 )
@@ -366,11 +366,6 @@ def tile_volterrathirdordermixer_t_kernel(tc, x_bytes, x_scale, mp, mq, mr, coef
         wo_words = const.tile([P, E, 4], BF16, name="wo_words", align_bytes=64)
         for b in range(LAST - 1):
             n = 2 * b
-            if b == 1:
-                nc.vector.tensor_copy(
-                    out=wo_words[:].rearrange("p (c i) j -> p c j i", i=RUN),
-                    in_=wo_rows[:].rearrange("p j (c i) -> p c j i", i=RUN),
-                )
             if b == 2:
                 nc.vector.quantize_mx(
                     out=wo_codes[:].bitcast(X4), scales=wo_scales[:], in_=wo_words[:].rearrange("p e j -> p (e j)")
@@ -400,6 +395,10 @@ def tile_volterrathirdordermixer_t_kernel(tc, x_bytes, x_scale, mp, mq, mr, coef
                 products(k, "R")
             for k in (n + 2, n + 3):
                 third_order(k)
+            if b == 0:
+                z_tile["wo"], z_words["wo"] = wo_rows, wo_words[:].rearrange("p e j -> p (e j)")
+                turn_z("wo")
+                fetch_z("wo")
             for k in (n, n + 1):
                 times_q(k)
                 products(k + 2, "Q")

@@ -21,6 +21,7 @@ MULT = mybir.AluOpType.mult
 SINGLE = 4
 LAST = NB - 1
 PITCH = D + 24
+BLOCKS = 13
 RUN = 4
 GATE = 32
 
@@ -96,7 +97,7 @@ def tile_volterrathirdordermixer_t_kernel(tc, x_bytes, x_scale, mp, mq, mr, coef
         ident_bf16 = const.tile([P, P], BF16, name="ident_bf16", align_bytes=64)
         nc.scalar.activation(out=ident_bf16[:], in_=ident_f32[:], func=COPY)
 
-        x_wide, x_words, x_codes, x_scales = {}, {}, {}, {}
+        x_wide, x_words, x_codes, x_scales, x_turned = {}, {}, {}, {}, {}
         word_buffers = []
         for k in range(2):
             buffer = const.tile([P, 4 * D], BF16, name="x_words%d" % k, align_bytes=64)
@@ -130,16 +131,10 @@ def tile_volterrathirdordermixer_t_kernel(tc, x_bytes, x_scale, mp, mq, mr, coef
                 in_=x_wide[b].rearrange("p t (g j i) -> p g j t i", g=16, j=4, i=8)[:, :, j0:j1],
             )
 
-        def interleave_x_scalar(b):
-            nc.scalar.copy(
-                out=x_words[b].rearrange("p (j g i t) -> p g j i t", j=4, g=16, i=8, t=4)[:, :, 3],
-                in_=x_wide[b].rearrange("p t (g j i) -> p g j i t", g=16, j=4, i=8)[:, :, 3],
-            )
-
         def interleave_x_gpsimd(b):
             nc.gpsimd.tensor_scalar(
-                out=x_words[b].rearrange("p (j g i t) -> p g j i t", j=4, g=16, i=8, t=4)[:, :, :3],
-                in0=x_wide[b].rearrange("p t (g j i) -> p g j i t", g=16, j=4, i=8)[:, :, :3],
+                out=x_words[b].rearrange("p (j g i t) -> p g j i t", j=4, g=16, i=8, t=4)[:, : BLOCKS],
+                in0=x_wide[b].rearrange("p t (g j i) -> p g j i t", g=16, j=4, i=8)[:, : BLOCKS],
                 scalar1=1.0,
                 scalar2=0.0,
                 op0=MULT,
@@ -147,16 +142,23 @@ def tile_volterrathirdordermixer_t_kernel(tc, x_bytes, x_scale, mp, mq, mr, coef
             )
 
         def turn_x(b):
-            turned = psum.tile([P, P, 4], BF16, name="x_turned", tag="O")
+            first = 32 * BLOCKS
+            turned = psum.tile([P, D - first, 4], BF16, name="x_turned", tag="O")
             for u in range(2):
                 nc.tensor.matmul(
-                    turned[:, :, 2 * u : 2 * u + 2].rearrange("p (g i) t -> p g i t", i=8),
+                    turned[:, :, 2 * u : 2 * u + 2],
                     lhsT=ident_bf16[:],
-                    rhs=x_wide[b][:, 2 * u : 2 * u + 2, :].rearrange("p t (g j i) -> p j g i t", j=4, i=8)[:, 3],
+                    rhs=x_wide[b][:, 2 * u : 2 * u + 2, first:].rearrange("p t d -> p d t"),
                     start=True,
                     stop=True,
                 )
-            nc.scalar.copy(out=x_words[b][:, 3 * D :], in_=turned[:].rearrange("p n t -> p (n t)"))
+            x_turned[b] = turned
+
+        def fetch_x(b):
+            nc.scalar.copy(
+                out=x_words[b].rearrange("p (j g w) -> p g j w", j=4, g=16)[:, BLOCKS :],
+                in_=x_turned[b][:].rearrange("p (g j i) t -> p g j (i t)", j=4, i=8),
+            )
 
         def quantize_x(b, j0=0, j1=4):
             cols = slice(j0 * P, j1 * P)
@@ -379,8 +381,6 @@ def tile_volterrathirdordermixer_t_kernel(tc, x_bytes, x_scale, mp, mq, mr, coef
             interleave_x_gpsimd(b + 2)
             if b + 2 < LAST:
                 widen("scalar", b + 3, 1)
-            else:
-                interleave_x_scalar(LAST)
             if b >= 1:
                 if b - 1 == LAST - 4:
                     z_words[b - 1] = chained[:, : 4 * T]
@@ -389,8 +389,8 @@ def tile_volterrathirdordermixer_t_kernel(tc, x_bytes, x_scale, mp, mq, mr, coef
                     z_words[b - 1] = words[:]
                 turn_z(b - 1)
                 fetch_z(b - 1)
-            if b + 2 < LAST:
-                turn_x(b + 2)
+            turn_x(b + 2)
+            fetch_x(b + 2)
             for k in (n + 2, n + 3):
                 products(k, "R")
             for k in (n + 2, n + 3):

@@ -23,11 +23,10 @@ LAST = NB - 1
 PITCH = D + 24
 BLOCKS = 13
 RUN = 4
-GATE = 32
 
 
 def scalar_share(b):
-    return {2: 0, 3: 256, 4: 256}.get(b, 208)
+    return {2: D, 3: 320, 4: 320}.get(b, 272)
 
 
 def tile_volterrathirdordermixer_t_kernel(tc, x_bytes, x_scale, mp, mq, mr, coef, gain, wo, out):
@@ -39,7 +38,7 @@ def tile_volterrathirdordermixer_t_kernel(tc, x_bytes, x_scale, mp, mq, mr, coef
         xq_pool = ctx.enter_context(tc.tile_pool(name="xq_pool", bufs=5))
         poly = ctx.enter_context(tc.tile_pool(name="poly", bufs=4))
         z_pool = ctx.enter_context(tc.tile_pool(name="z_pool", bufs=4))
-        zq_pool = ctx.enter_context(tc.tile_pool(name="zq_pool", bufs=7))
+        zq_pool = ctx.enter_context(tc.tile_pool(name="zq_pool", bufs=1))
         out_pool = ctx.enter_context(tc.tile_pool(name="out_pool", bufs=8))
         psum = ctx.enter_context(tc.psum_pool(name="psum", bufs=1))
         ctx.enter_context(tc.manual_schedule())
@@ -197,6 +196,7 @@ def tile_volterrathirdordermixer_t_kernel(tc, x_bytes, x_scale, mp, mq, mr, coef
             m_scales.append(scales)
 
         sums, h_val, u_val, z_tile = {}, {}, {}, {}
+        pair_rows = const.tile([P, 2, 4, T], BF16, name="pair_rows", align_bytes=64)
 
         def units(n):
             if n // 2 == LAST:
@@ -240,7 +240,9 @@ def tile_volterrathirdordermixer_t_kernel(tc, x_bytes, x_scale, mp, mq, mr, coef
 
         def times_p(n):
             b = n // 2
-            if n % 2 == 0:
+            if b in (LAST - 3, LAST - 2):
+                z_tile[b] = pair_rows[:, b - (LAST - 3)]
+            elif n % 2 == 0:
                 z_rows = z_pool.tile([P, 4, T], BF16, name="z_rows", align_bytes=64)
                 z_tile[b] = z_rows
             for j, times, bank in units(n):
@@ -282,11 +284,16 @@ def tile_volterrathirdordermixer_t_kernel(tc, x_bytes, x_scale, mp, mq, mr, coef
                 op1=ADD,
             )
 
-        def quantize_z(b):
-            codes = zq_pool.tile([P, T], U32, name="z_q", align_bytes=64)
-            scales = zq_pool.tile([P, T], U8, name="z_qs", align_bytes=64)
-            nc.vector.quantize_mx(out=codes[:].bitcast(X4), scales=scales[:], in_=z_words[b])
-            z_codes[b], z_scales[b] = codes, scales
+        def quantize_z(b, count=1):
+            codes = zq_pool.tile([P, count, T], U32, name="z_q%d" % b, align_bytes=64)
+            scales = zq_pool.tile([P, count, T], U8, name="z_qs%d" % b, align_bytes=64)
+            nc.vector.quantize_mx(
+                out=codes[:].rearrange("p k t -> p (k t)").bitcast(X4),
+                scales=scales[:].rearrange("p k t -> p (k t)"),
+                in_=z_words[b],
+            )
+            for k in range(count):
+                z_codes[b + k], z_scales[b + k] = codes[:, k, :], scales[:, k, :]
 
         def project(b, bank="O"):
             o_ps = psum.tile([P, 2, E], F32, name="o_ps", tag=bank)
@@ -334,21 +341,21 @@ def tile_volterrathirdordermixer_t_kernel(tc, x_bytes, x_scale, mp, mq, mr, coef
         new_x_words(1)
         interleave_x_vector(1, 0, 1)
         quantize_m(0)
-        interleave_x_vector(1, 1, 2)
-        nc.vector.tensor_copy(out=vec_cols[:], in_=vec_ps[:, 0:12])
+        interleave_x_vector(1, 1, 4)
         quantize_m(1)
+        nc.vector.tensor_copy(out=vec_cols[:], in_=vec_ps[:, 0:12])
+        products(0, "R")
+        products(1, "R")
+        products(0, "Q")
+        products(1, "Q")
+        widen("vector", 2, 2)
         nc.vector.tensor_tensor(
             out=gain_coef[:].rearrange("p (v j) -> p v j", v=2),
             in0=vec_cols[:, 0:8].rearrange("p (v j) -> p v j", v=2),
             in1=vec_cols[:, 8:12].unsqueeze(1).to_broadcast([P, 2, 4]),
             op=MULT,
         )
-        products(0, "R")
-        products(1, "R")
-        products(0, "Q")
-        products(1, "Q")
-        interleave_x_vector(1, 2, 4)
-        widen("scalar", 2, 0)
+        widen("vector", 2, 0)
         widen("scalar", 2, 1)
         third_order(0)
         third_order(1)
@@ -364,7 +371,7 @@ def tile_volterrathirdordermixer_t_kernel(tc, x_bytes, x_scale, mp, mq, mr, coef
             project(waiting[0], bank)
             store(waiting.pop(0))
 
-        chained = const.tile([P, 8 * T - GATE], BF16, name="chained", align_bytes=64)
+        pair_words = const.tile([P, 2, 4 * T], BF16, name="pair_words", align_bytes=64)
         wo_words = const.tile([P, E, 4], BF16, name="wo_words", align_bytes=64)
         for b in range(LAST - 1):
             n = 2 * b
@@ -381,9 +388,11 @@ def tile_volterrathirdordermixer_t_kernel(tc, x_bytes, x_scale, mp, mq, mr, coef
             interleave_x_gpsimd(b + 2)
             if b + 2 < LAST:
                 widen("scalar", b + 3, 1)
-            if b >= 1:
+            if b == LAST - 2:
+                emit("Z")
+            elif b >= 1:
                 if b - 1 == LAST - 4:
-                    z_words[b - 1] = chained[:, : 4 * T]
+                    z_words[b - 1] = pair_words[:, 0, :]
                 else:
                     words = z_pool.tile([P, 4 * T], BF16, name="z_words", align_bytes=64)
                     z_words[b - 1] = words[:]
@@ -402,7 +411,7 @@ def tile_volterrathirdordermixer_t_kernel(tc, x_bytes, x_scale, mp, mq, mr, coef
             for k in (n, n + 1):
                 times_q(k)
                 products(k + 2, "Q")
-            if b >= 3 and (b % 2 or b + 4 >= NB):
+            if b in (5, 8, 11) or b + 4 >= NB:
                 emit()
             if b + 4 < NB:
                 widen("scalar", b + 4, 0)
@@ -445,38 +454,50 @@ def tile_volterrathirdordermixer_t_kernel(tc, x_bytes, x_scale, mp, mq, mr, coef
             nc.sync.dma_start(out=out[LAST].rearrange("(p c) e -> p c e", c=2)[:, c, :], in_=half_sb[:])
 
         n = 2 * (LAST - 1)
+        emit("Z")
         quantize_z(LAST - 4)
         quantize_x(LAST)
-        z_words[LAST - 2] = chained[:, 4 * T - GATE :]
-        late_words = const.tile([P, 4 * T], BF16, name="late_words", align_bytes=64)
-        z_words[LAST - 1] = late_words[:]
-        interleave_z_gpsimd(LAST - 2)
         waiting.append(LAST - 4)
-        emit("Z")
+        split = T * BLOCKS // 16
+        rows = pair_rows[:].rearrange("p b j t -> p b t j")
+        words = pair_words[:].rearrange("p b (t j) -> p b t j", j=4)
+        nc.gpsimd.tensor_scalar(
+            out=words[:, :, :split], in0=rows[:, :, :split], scalar1=1.0, scalar2=0.0, op0=MULT, op1=ADD
+        )
         products(n + 2, "R")
         third_order(n + 2)
+        pair_turned = psum.tile([P, 2, T - split, 4], BF16, name="pair_turned", tag="O")
+        for u in range(2):
+            nc.tensor.matmul(
+                pair_turned[:, :, :, 2 * u : 2 * u + 2],
+                lhsT=ident_bf16[:],
+                rhs=rows[:, :, split:, 2 * u : 2 * u + 2],
+                start=True,
+                stop=True,
+            )
         products(n + 3, "R")
-        emit("O")
+        nc.scalar.copy(out=words[:, :, split:], in_=pair_turned[:])
         third_order(n + 3)
         times_q(n)
         products(n + 2, "Q")
+        emit("Z")
         times_q(n + 1)
         products(n + 3, "Q")
-        emit("Z")
+        emit("O")
         emit("R0")
         times_p(n)
         products(n + 2, "P")
-        quantize_z(LAST - 3)
-        quantize_z(LAST - 2)
-        waiting.extend([LAST - 3, LAST - 2])
-        project(waiting[0], "O")
-        times_p(n + 1)
-        turn_z(LAST - 1, 1, "R1")
-        products(n + 3, "P")
-        interleave_z_gpsimd(LAST - 1, P)
-        fetch_z(LAST - 1, 1)
-        store(waiting.pop(0))
         emit("Z")
+        times_p(n + 1)
+        z_words[LAST - 3] = pair_words[:].rearrange("p b w -> p (b w)")
+        quantize_z(LAST - 3, 2)
+        waiting.extend([LAST - 3, LAST - 2])
+        late_words = const.tile([P, 4 * T], BF16, name="late_words", align_bytes=64)
+        z_words[LAST - 1] = late_words[:]
+        products(n + 3, "P")
+        interleave_z_gpsimd(LAST - 1)
+        emit("R1")
+        emit("O")
         emit("R0")
 
         n = 2 * LAST

@@ -388,9 +388,7 @@ def tile_volterrathirdordermixer_t_kernel(tc, x_bytes, x_scale, mp, mq, mr, coef
             interleave_x_gpsimd(b + 2)
             if b + 2 < LAST:
                 widen("scalar", b + 3, 1)
-            if b == LAST - 2:
-                emit("Z")
-            elif b >= 1:
+            if 1 <= b < LAST - 2:
                 if b - 1 == LAST - 4:
                     z_words[b - 1] = pair_words[:, 0, :]
                 else:
@@ -408,17 +406,25 @@ def tile_volterrathirdordermixer_t_kernel(tc, x_bytes, x_scale, mp, mq, mr, coef
                 z_tile["wo"], z_words["wo"] = wo_rows, wo_words[:].rearrange("p e j -> p (e j)")
                 turn_z("wo")
                 fetch_z("wo")
+            if b == LAST - 2:
+                emit("Z")
             for k in (n, n + 1):
                 times_q(k)
                 products(k + 2, "Q")
-            if b in (5, 8, 11) or b + 4 >= NB:
+            if b in (5, 8, 11):
                 emit()
+            elif b == LAST - 3:
+                emit("Z")
+            elif b == LAST - 2:
+                emit("O")
             if b + 4 < NB:
                 widen("scalar", b + 4, 0)
                 widen("scalar", b + 4, 2, 0, scalar_share(b + 4))
             for k in (n, n + 1):
                 times_p(k)
                 products(k + 2, "P")
+                if b == LAST - 2 and k == n:
+                    emit("R0")
 
         half_words, half_sums = [], []
 
@@ -454,7 +460,7 @@ def tile_volterrathirdordermixer_t_kernel(tc, x_bytes, x_scale, mp, mq, mr, coef
             nc.sync.dma_start(out=out[LAST].rearrange("(p c) e -> p c e", c=2)[:, c, :], in_=half_sb[:])
 
         n = 2 * (LAST - 1)
-        emit("Z")
+        emit("R1")
         quantize_z(LAST - 4)
         quantize_x(LAST)
         waiting.append(LAST - 4)
@@ -464,9 +470,7 @@ def tile_volterrathirdordermixer_t_kernel(tc, x_bytes, x_scale, mp, mq, mr, coef
         nc.gpsimd.tensor_scalar(
             out=words[:, :, :split], in0=rows[:, :, :split], scalar1=1.0, scalar2=0.0, op0=MULT, op1=ADD
         )
-        products(n + 2, "R")
-        third_order(n + 2)
-        pair_turned = psum.tile([P, 2, T - split, 4], BF16, name="pair_turned", tag="O")
+        pair_turned = psum.tile([P, 2, T - split, 4], BF16, name="pair_turned", tag="Z")
         for u in range(2):
             nc.tensor.matmul(
                 pair_turned[:, :, :, 2 * u : 2 * u + 2],
@@ -475,19 +479,21 @@ def tile_volterrathirdordermixer_t_kernel(tc, x_bytes, x_scale, mp, mq, mr, coef
                 start=True,
                 stop=True,
             )
-        products(n + 3, "R")
         nc.scalar.copy(out=words[:, :, split:], in_=pair_turned[:])
+        emit("O")
+        products(n + 2, "R")
+        products(n + 3, "R")
+        third_order(n + 2)
         third_order(n + 3)
         times_q(n)
         products(n + 2, "Q")
-        emit("Z")
         times_q(n + 1)
         products(n + 3, "Q")
+        emit("Z")
         emit("O")
-        emit("R0")
         times_p(n)
         products(n + 2, "P")
-        emit("Z")
+        emit("R0")
         times_p(n + 1)
         z_words[LAST - 3] = pair_words[:].rearrange("p b w -> p (b w)")
         quantize_z(LAST - 3, 2)
@@ -497,8 +503,7 @@ def tile_volterrathirdordermixer_t_kernel(tc, x_bytes, x_scale, mp, mq, mr, coef
         products(n + 3, "P")
         interleave_z_gpsimd(LAST - 1)
         emit("R1")
-        emit("O")
-        emit("R0")
+        emit("Z")
 
         n = 2 * LAST
         times_q(n)

@@ -26,7 +26,7 @@ RUN = 4
 
 
 def scalar_share(b):
-    return {2: D, 3: 320, 4: 320}.get(b, 272)
+    return {2: D, 3: 272}.get(b, 272)
 
 
 def tile_volterrathirdordermixer_t_kernel(tc, x_bytes, x_scale, mp, mq, mr, coef, gain, wo, out):
@@ -59,15 +59,12 @@ def tile_volterrathirdordermixer_t_kernel(tc, x_bytes, x_scale, mp, mq, mr, coef
             nc.sync.dma_start(out=m_rows[:], in_=(mr, mq, mp)[i].rearrange("(p c) k -> p c k", c=2))
             m_raw[i] = m_rows
 
-        vec_rows = const.tile([P, P], BF16, name="vec_rows", align_bytes=64)
+        vec_rows = const.tile([P, 3, 32], BF16, name="vec_rows", align_bytes=64)
         nc.vector.memset(vec_rows[:], 0.0)
 
         def load_vectors():
-            for v, vec in enumerate((coef[0], coef[1], gain)):
-                nc.sync.dma_start(
-                    out=vec_rows[4 * v : 4 * v + 4, :].rearrange("p (g i) -> p g i", i=8),
-                    in_=vec.rearrange("(g j i) -> j g i", j=4, i=8),
-                )
+            nc.sync.dma_start(out=vec_rows[0:16, 0:2, :], in_=coef.rearrange("v (g c) -> g v c", c=32))
+            nc.sync.dma_start(out=vec_rows[0:16, 2, :], in_=gain.rearrange("(g c) -> g c", c=32))
 
         wo_rows = const.tile([P, 4, E], BF16, name="wo_rows", align_bytes=64)
 
@@ -81,20 +78,27 @@ def tile_volterrathirdordermixer_t_kernel(tc, x_bytes, x_scale, mp, mq, mr, coef
         load_scale()
         load_x(0, 1)
         load_x(1, 1)
+        load_vectors()
         load_m(0)
         load_m(1)
         load_m(2)
-        load_vectors()
         load_x(2, 1)
         load_x(3, 1)
+        load_x(SINGLE, 2)
         load_wo()
-        for b in range(SINGLE, NB, 2):
+        for b in range(SINGLE + 2, NB, 2):
             load_x(b, 2)
 
         ident_f32 = const.tile([P, P], F32, name="ident_f32", align_bytes=64)
         make_identity(nc, ident_f32[:])
         ident_bf16 = const.tile([P, P], BF16, name="ident_bf16", align_bytes=64)
         nc.scalar.activation(out=ident_bf16[:], in_=ident_f32[:], func=COPY)
+        spread = const.tile([P, 16, 8], BF16, name="spread", align_bytes=64)
+        nc.vector.tensor_copy(out=spread[:], in_=ident_f32[:, 0:16].unsqueeze(2).to_broadcast([P, 16, 8]))
+        pick = const.tile([P, 8], F32, name="pick", align_bytes=64)
+        nc.vector.tensor_reduce(
+            out=pick[:], in_=ident_f32[:].rearrange("p (g i) -> p i g", i=8), axis=mybir.AxisListType.X, op=ADD
+        )
 
         x_wide, x_words, x_codes, x_scales, x_turned = {}, {}, {}, {}, {}
         word_buffers = []
@@ -317,7 +321,8 @@ def tile_volterrathirdordermixer_t_kernel(tc, x_bytes, x_scale, mp, mq, mr, coef
 
         vec_cols = const.tile([P, 12], F32, name="vec_cols", align_bytes=64)
         gain_coef = const.tile([P, 8], F32, name="gain_coef", align_bytes=64)
-        vec_ps = psum.tile([P, P], BF16, name="vec_ps", tag="O")
+        vec_ps = psum.tile([P, 12, 8], F32, name="vec_ps", tag="O")
+        vec_picked = const.tile([P, 12, 8], F32, name="vec_picked", align_bytes=64)
         wo_codes = const.tile([P, E], U32, name="wo_q", align_bytes=64)
         wo_scales = const.tile([P, E], U8, name="wo_qs", align_bytes=64)
         widen("vector", 0, 0)
@@ -325,10 +330,16 @@ def tile_volterrathirdordermixer_t_kernel(tc, x_bytes, x_scale, mp, mq, mr, coef
         widen("scalar", 0, 2)
         widen("vector", 0, 3)
         widen("vector", 1, 3)
+        nc.tensor.matmul(
+            vec_ps[:].rearrange("p w i -> p (w i)"),
+            lhsT=spread[:].rearrange("p g i -> p (g i)"),
+            rhs=vec_rows[:].rearrange("p v c -> p (v c)"),
+            start=True,
+            stop=True,
+        )
         turn_m(0)
         turn_m(1)
         turn_m(2)
-        nc.tensor.transpose(vec_ps[:], vec_rows[:], ident_bf16[:])
         for t in (0, 1, 2):
             widen("scalar", 1, t)
         for i in range(3):
@@ -342,8 +353,11 @@ def tile_volterrathirdordermixer_t_kernel(tc, x_bytes, x_scale, mp, mq, mr, coef
         interleave_x_vector(1, 0, 1)
         quantize_m(0)
         interleave_x_vector(1, 1, 4)
+        nc.vector.tensor_tensor(
+            out=vec_picked[:], in0=vec_ps[:], in1=pick[:].unsqueeze(1).to_broadcast([P, 12, 8]), op=MULT
+        )
         quantize_m(1)
-        nc.vector.tensor_copy(out=vec_cols[:], in_=vec_ps[:, 0:12])
+        nc.vector.tensor_reduce(out=vec_cols[:], in_=vec_picked[:], axis=mybir.AxisListType.X, op=ADD)
         products(0, "R")
         products(1, "R")
         products(0, "Q")
@@ -375,7 +389,7 @@ def tile_volterrathirdordermixer_t_kernel(tc, x_bytes, x_scale, mp, mq, mr, coef
         wo_words = const.tile([P, E, 4], BF16, name="wo_words", align_bytes=64)
         for b in range(LAST - 1):
             n = 2 * b
-            if b == 2:
+            if b == 5:
                 nc.vector.quantize_mx(
                     out=wo_codes[:].bitcast(X4), scales=wo_scales[:], in_=wo_words[:].rearrange("p e j -> p (e j)")
                 )
@@ -402,16 +416,16 @@ def tile_volterrathirdordermixer_t_kernel(tc, x_bytes, x_scale, mp, mq, mr, coef
                 products(k, "R")
             for k in (n + 2, n + 3):
                 third_order(k)
-            if b == 0:
-                z_tile["wo"], z_words["wo"] = wo_rows, wo_words[:].rearrange("p e j -> p (e j)")
-                turn_z("wo")
-                fetch_z("wo")
             if b == LAST - 2:
                 emit("Z")
             for k in (n, n + 1):
                 times_q(k)
                 products(k + 2, "Q")
-            if b in (5, 8, 11):
+            if b == 3:
+                z_tile["wo"], z_words["wo"] = wo_rows, wo_words[:].rearrange("p e j -> p (e j)")
+                turn_z("wo", bank="O")
+                fetch_z("wo")
+            elif b in (6, 9, 11):
                 emit()
             elif b == LAST - 3:
                 emit("Z")

@@ -21,7 +21,7 @@ MULT = mybir.AluOpType.mult
 SINGLE = 4
 LAST = NB - 1
 PITCH = D + 24
-BLOCKS = 13
+BLOCKS = 15
 RUN = 4
 
 
@@ -135,13 +135,9 @@ def tile_volterrathirdordermixer_t_kernel(tc, x_bytes, x_scale, mp, mq, mr, coef
             )
 
         def interleave_x_gpsimd(b):
-            nc.gpsimd.tensor_scalar(
-                out=x_words[b].rearrange("p (j g i t) -> p g j i t", j=4, g=16, i=8, t=4)[:, : BLOCKS],
-                in0=x_wide[b].rearrange("p t (g j i) -> p g j i t", g=16, j=4, i=8)[:, : BLOCKS],
-                scalar1=1.0,
-                scalar2=0.0,
-                op0=MULT,
-                op1=ADD,
+            nc.gpsimd.tensor_copy(
+                out=x_words[b].rearrange("p (j g i t) -> p g j t i", j=4, g=16, i=8, t=4)[:, :BLOCKS],
+                in_=x_wide[b].rearrange("p t (g j i) -> p g j t i", g=16, j=4, i=8)[:, :BLOCKS],
             )
 
         def turn_x(b):
@@ -478,7 +474,7 @@ def tile_volterrathirdordermixer_t_kernel(tc, x_bytes, x_scale, mp, mq, mr, coef
         quantize_z(LAST - 4)
         quantize_x(LAST)
         waiting.append(LAST - 4)
-        split = T * BLOCKS // 16
+        split = T * 13 // 16
         rows = pair_rows[:].rearrange("p b j t -> p b t j")
         words = pair_words[:].rearrange("p b (t j) -> p b t j", j=4)
         nc.gpsimd.tensor_scalar(

@@ -26,7 +26,7 @@ RUN = 4
 
 
 def scalar_share(b):
-    return {2: D, 3: 272}.get(b, 272)
+    return {2: D}.get(b, 368)
 
 
 def tile_volterrathirdordermixer_t_kernel(tc, x_bytes, x_scale, mp, mq, mr, coef, gain, wo, out):
@@ -274,14 +274,10 @@ def tile_volterrathirdordermixer_t_kernel(tc, x_bytes, x_scale, mp, mq, mr, coef
                 out=z_words[b][:, 4 * first * P :], in_=z_turned[b][:, first * P :, :].rearrange("p t j -> p (t j)")
             )
 
-        def interleave_z_gpsimd(b, times=T):
-            nc.gpsimd.tensor_scalar(
-                out=z_words[b].rearrange("p (t j) -> p t j", j=4)[:, :times],
-                in0=z_tile[b][:].rearrange("p j t -> p t j")[:, :times],
-                scalar1=1.0,
-                scalar2=0.0,
-                op0=MULT,
-                op1=ADD,
+        def interleave_z_gpsimd(b):
+            nc.gpsimd.tensor_copy(
+                out=z_words[b].rearrange("p (c i j) -> p c j i", i=8, j=4),
+                in_=z_tile[b][:].rearrange("p j (c i) -> p c j i", i=8),
             )
 
         def quantize_z(b, count=1):
@@ -405,9 +401,10 @@ def tile_volterrathirdordermixer_t_kernel(tc, x_bytes, x_scale, mp, mq, mr, coef
                     words = z_pool.tile([P, 4 * T], BF16, name="z_words", align_bytes=64)
                     z_words[b - 1] = words[:]
                 turn_z(b - 1)
-                fetch_z(b - 1)
             turn_x(b + 2)
             fetch_x(b + 2)
+            if 1 <= b < LAST - 2:
+                fetch_z(b - 1)
             for k in (n + 2, n + 3):
                 products(k, "R")
             for k in (n + 2, n + 3):
@@ -446,39 +443,45 @@ def tile_volterrathirdordermixer_t_kernel(tc, x_bytes, x_scale, mp, mq, mr, coef
             )
             half_words.append(words)
 
-        def project_half(c):
+        def project_half(c, banks):
             codes = zq_pool.tile([P, P], U32, name="half_q%d" % c, align_bytes=64)
             scales = zq_pool.tile([P, P], U8, name="half_qs%d" % c, align_bytes=64)
             nc.vector.quantize_mx(
                 out=codes[:].bitcast(X4), scales=scales[:], in_=half_words[c][:].rearrange("p t j -> p (t j)")
             )
-            half_ps = psum.tile([P, E], F32, name="half_ps", tag="Q" + "01"[c])
-            nc.tensor.matmul_mx(
-                out=half_ps[:],
-                lhsT=codes[:].bitcast(X4),
-                lhsT_scale=scales[:],
-                rhs=wo_codes[:].bitcast(X4),
-                rhs_scale=wo_scales[:],
-                start=True,
-                stop=True,
-            )
-            half_sums.append(half_ps)
+            width = E // len(banks)
+            parts = []
+            for k, bank in enumerate(banks):
+                cols = slice(k * width, (k + 1) * width)
+                half_ps = psum.tile([P, width], F32, name="half_ps", tag=bank)
+                nc.tensor.matmul_mx(
+                    out=half_ps[:],
+                    lhsT=codes[:].bitcast(X4),
+                    lhsT_scale=scales[:],
+                    rhs=wo_codes[:, cols].bitcast(X4),
+                    rhs_scale=wo_scales[:, cols],
+                    start=True,
+                    stop=True,
+                )
+                parts.append((cols, half_ps))
+            half_sums.append(parts)
 
-        def store_half(c, copy):
+        def store_half(c, copies):
             half_sb = out_pool.tile([P, E], F32, name="half_sb%d" % c, align_bytes=64)
-            copy(out=half_sb[:], in_=half_sums[c][:])
+            for copy, (cols, half_ps) in zip(copies, half_sums[c]):
+                copy(out=half_sb[:, cols], in_=half_ps[:])
             nc.sync.dma_start(out=out[LAST].rearrange("(p c) e -> p c e", c=2)[:, c, :], in_=half_sb[:])
 
         n = 2 * (LAST - 1)
-        emit("R1")
         quantize_z(LAST - 4)
         quantize_x(LAST)
         waiting.append(LAST - 4)
-        split = T * 13 // 16
+        split = T * 7 // 8
         rows = pair_rows[:].rearrange("p b j t -> p b t j")
         words = pair_words[:].rearrange("p b (t j) -> p b t j", j=4)
-        nc.gpsimd.tensor_scalar(
-            out=words[:, :, :split], in0=rows[:, :, :split], scalar1=1.0, scalar2=0.0, op0=MULT, op1=ADD
+        nc.gpsimd.tensor_copy(
+            out=words[:, :, :split].rearrange("p b (c i) j -> p b c j i", i=8),
+            in_=rows[:, :, :split].rearrange("p b (c i) j -> p b c j i", i=8),
         )
         pair_turned = psum.tile([P, 2, T - split, 4], BF16, name="pair_turned", tag="Z")
         for u in range(2):
@@ -500,10 +503,9 @@ def tile_volterrathirdordermixer_t_kernel(tc, x_bytes, x_scale, mp, mq, mr, coef
         times_q(n + 1)
         products(n + 3, "Q")
         emit("Z")
-        emit("O")
         times_p(n)
         products(n + 2, "P")
-        emit("R0")
+        emit("O")
         times_p(n + 1)
         z_words[LAST - 3] = pair_words[:].rearrange("p b w -> p (b w)")
         quantize_z(LAST - 3, 2)
@@ -512,8 +514,8 @@ def tile_volterrathirdordermixer_t_kernel(tc, x_bytes, x_scale, mp, mq, mr, coef
         z_words[LAST - 1] = late_words[:]
         products(n + 3, "P")
         interleave_z_gpsimd(LAST - 1)
-        emit("R1")
-        emit("Z")
+        for bank in ("R0", "R1", "Z", "O"):
+            emit(bank)
 
         n = 2 * LAST
         times_q(n)
@@ -525,7 +527,7 @@ def tile_volterrathirdordermixer_t_kernel(tc, x_bytes, x_scale, mp, mq, mr, coef
         times_p(n + 1)
         for c in range(2):
             interleave_half(c)
-        for c in range(2):
-            project_half(c)
-        store_half(0, nc.scalar.copy)
-        store_half(1, nc.vector.tensor_copy)
+        project_half(0, ("Q0",))
+        project_half(1, ("Q1", "P1"))
+        store_half(0, (nc.scalar.copy,))
+        store_half(1, (nc.scalar.copy, nc.vector.tensor_copy))

@@ -26,7 +26,7 @@ RUN = 4
 
 
 def scalar_share(b):
-    return {2: D}.get(b, 368)
+    return {2: D}.get(b, 400)
 
 
 def tile_volterrathirdordermixer_t_kernel(tc, x_bytes, x_scale, mp, mq, mr, coef, gain, wo, out):
@@ -140,9 +140,9 @@ def tile_volterrathirdordermixer_t_kernel(tc, x_bytes, x_scale, mp, mq, mr, coef
                 in_=x_wide[b].rearrange("p t (g j i) -> p g j t i", g=16, j=4, i=8)[:, :BLOCKS],
             )
 
-        def turn_x(b):
+        def turn_x(b, bank="O"):
             first = 32 * BLOCKS
-            turned = psum.tile([P, D - first, 4], BF16, name="x_turned", tag="O")
+            turned = psum.tile([P, D - first, 4], BF16, name="x_turned", tag=bank)
             for u in range(2):
                 nc.tensor.matmul(
                     turned[:, :, 2 * u : 2 * u + 2],
@@ -280,16 +280,11 @@ def tile_volterrathirdordermixer_t_kernel(tc, x_bytes, x_scale, mp, mq, mr, coef
                 in_=z_tile[b][:].rearrange("p j (c i) -> p c j i", i=8),
             )
 
-        def quantize_z(b, count=1):
-            codes = zq_pool.tile([P, count, T], U32, name="z_q%d" % b, align_bytes=64)
-            scales = zq_pool.tile([P, count, T], U8, name="z_qs%d" % b, align_bytes=64)
-            nc.vector.quantize_mx(
-                out=codes[:].rearrange("p k t -> p (k t)").bitcast(X4),
-                scales=scales[:].rearrange("p k t -> p (k t)"),
-                in_=z_words[b],
-            )
-            for k in range(count):
-                z_codes[b + k], z_scales[b + k] = codes[:, k, :], scales[:, k, :]
+        def quantize_z(b):
+            codes = zq_pool.tile([P, T], U32, name="z_q%d" % b, align_bytes=64)
+            scales = zq_pool.tile([P, T], U8, name="z_qs%d" % b, align_bytes=64)
+            nc.vector.quantize_mx(out=codes[:].bitcast(X4), scales=scales[:], in_=z_words[b])
+            z_codes[b], z_scales[b] = codes, scales
 
         def project(b, bank="O"):
             o_ps = psum.tile([P, 2, E], F32, name="o_ps", tag=bank)
@@ -401,8 +396,12 @@ def tile_volterrathirdordermixer_t_kernel(tc, x_bytes, x_scale, mp, mq, mr, coef
                     words = z_pool.tile([P, 4 * T], BF16, name="z_words", align_bytes=64)
                     z_words[b - 1] = words[:]
                 turn_z(b - 1)
-            turn_x(b + 2)
-            fetch_x(b + 2)
+            if b < LAST - 2:
+                turn_x(b + 2)
+                fetch_x(b + 2)
+            else:
+                turn_x(b + 2, "R1")
+                fetch_x(b + 2)
             if 1 <= b < LAST - 2:
                 fetch_z(b - 1)
             for k in (n + 2, n + 3):
@@ -410,6 +409,7 @@ def tile_volterrathirdordermixer_t_kernel(tc, x_bytes, x_scale, mp, mq, mr, coef
             for k in (n + 2, n + 3):
                 third_order(k)
             if b == LAST - 2:
+                emit("O")
                 emit("Z")
             for k in (n, n + 1):
                 times_q(k)
@@ -418,12 +418,13 @@ def tile_volterrathirdordermixer_t_kernel(tc, x_bytes, x_scale, mp, mq, mr, coef
                 z_tile["wo"], z_words["wo"] = wo_rows, wo_words[:].rearrange("p e j -> p (e j)")
                 turn_z("wo", bank="O")
                 fetch_z("wo")
-            elif b in (6, 9, 11):
+            elif 6 <= b < LAST - 3 and b % 3 == 1:
                 emit()
             elif b == LAST - 3:
+                emit("O")
                 emit("Z")
             elif b == LAST - 2:
-                emit("O")
+                emit("R1")
             if b + 4 < NB:
                 widen("scalar", b + 4, 0)
                 widen("scalar", b + 4, 2, 0, scalar_share(b + 4))
@@ -431,7 +432,7 @@ def tile_volterrathirdordermixer_t_kernel(tc, x_bytes, x_scale, mp, mq, mr, coef
                 times_p(k)
                 products(k + 2, "P")
                 if b == LAST - 2 and k == n:
-                    emit("R0")
+                    emit("O")
 
         half_words, half_sums = [], []
 
@@ -493,28 +494,28 @@ def tile_volterrathirdordermixer_t_kernel(tc, x_bytes, x_scale, mp, mq, mr, coef
                 stop=True,
             )
         nc.scalar.copy(out=words[:, :, split:], in_=pair_turned[:])
-        emit("O")
         products(n + 2, "R")
         products(n + 3, "R")
         third_order(n + 2)
         third_order(n + 3)
         times_q(n)
         products(n + 2, "Q")
+        emit("Z")
         times_q(n + 1)
         products(n + 3, "Q")
-        emit("Z")
+        emit("O")
         times_p(n)
         products(n + 2, "P")
-        emit("O")
+        emit("R0")
         times_p(n + 1)
-        z_words[LAST - 3] = pair_words[:].rearrange("p b w -> p (b w)")
-        quantize_z(LAST - 3, 2)
-        waiting.extend([LAST - 3, LAST - 2])
-        late_words = const.tile([P, 4 * T], BF16, name="late_words", align_bytes=64)
-        z_words[LAST - 1] = late_words[:]
-        products(n + 3, "P")
+        z_words[LAST - 3], z_words[LAST - 2] = pair_words[:, 0, :], pair_words[:, 1, :]
+        z_words[LAST - 1] = pair_words[:, 0, :]
+        quantize_z(LAST - 3)
         interleave_z_gpsimd(LAST - 1)
-        for bank in ("R0", "R1", "Z", "O"):
+        quantize_z(LAST - 2)
+        waiting.extend([LAST - 3, LAST - 2])
+        products(n + 3, "P")
+        for bank in ("R1", "Z", "O"):
             emit(bank)
 
         n = 2 * LAST

@@ -26,7 +26,7 @@ RUN = 4
 
 
 def scalar_share(b):
-    return {2: D}.get(b, 400)
+    return {2: D}.get(b, 432)
 
 
 def tile_volterrathirdordermixer_t_kernel(tc, x_bytes, x_scale, mp, mq, mr, coef, gain, wo, out):
@@ -81,8 +81,8 @@ def tile_volterrathirdordermixer_t_kernel(tc, x_bytes, x_scale, mp, mq, mr, coef
         load_vectors()
         load_m(0)
         load_m(1)
-        load_m(2)
         load_x(2, 1)
+        load_m(2)
         load_x(3, 1)
         load_x(SINGLE, 2)
         load_wo()
@@ -329,35 +329,36 @@ def tile_volterrathirdordermixer_t_kernel(tc, x_bytes, x_scale, mp, mq, mr, coef
         turn_m(2)
         for t in (0, 1, 2):
             widen("scalar", 1, t)
-        for i in range(3):
-            fetch_m(i)
+        fetch_m(0)
+        widen("scalar", 2, 0)
+        fetch_m(1)
+        widen("scalar", 2, 1)
+        fetch_m(2)
         new_x_words(0)
         interleave_x_vector(0, 0, 2)
         interleave_x_vector(0, 2, 4)
-        quantize_x(0, 0, 2)
-        quantize_x(0, 2, 4)
-        new_x_words(1)
-        interleave_x_vector(1, 0, 1)
-        quantize_m(0)
-        interleave_x_vector(1, 1, 4)
         nc.vector.tensor_tensor(
             out=vec_picked[:], in0=vec_ps[:], in1=pick[:].unsqueeze(1).to_broadcast([P, 12, 8]), op=MULT
         )
-        quantize_m(1)
+        quantize_x(0, 0, 2)
+        quantize_x(0, 2, 4)
         nc.vector.tensor_reduce(out=vec_cols[:], in_=vec_picked[:], axis=mybir.AxisListType.X, op=ADD)
-        products(0, "R")
-        products(1, "R")
-        products(0, "Q")
-        products(1, "Q")
-        widen("vector", 2, 2)
+        new_x_words(1)
+        interleave_x_vector(1, 0, 1)
         nc.vector.tensor_tensor(
             out=gain_coef[:].rearrange("p (v j) -> p v j", v=2),
             in0=vec_cols[:, 0:8].rearrange("p (v j) -> p v j", v=2),
             in1=vec_cols[:, 8:12].unsqueeze(1).to_broadcast([P, 2, 4]),
             op=MULT,
         )
-        widen("vector", 2, 0)
-        widen("scalar", 2, 1)
+        quantize_m(0)
+        interleave_x_vector(1, 1, 4)
+        quantize_m(1)
+        products(0, "R")
+        products(1, "R")
+        products(0, "Q")
+        products(1, "Q")
+        widen("vector", 2, 2)
         third_order(0)
         third_order(1)
         quantize_m(2)
@@ -368,14 +369,22 @@ def tile_volterrathirdordermixer_t_kernel(tc, x_bytes, x_scale, mp, mq, mr, coef
 
         waiting = []
 
-        def emit(bank="O"):
+        def emit(bank):
             project(waiting[0], bank)
             store(waiting.pop(0))
 
+        def step_q(n):
+            times_q(n)
+            products(n + 2, "Q")
+
+        def step_p(n):
+            times_p(n)
+            products(n + 2, "P")
+
         pair_words = const.tile([P, 2, 4 * T], BF16, name="pair_words", align_bytes=64)
         wo_words = const.tile([P, E, 4], BF16, name="wo_words", align_bytes=64)
-        for b in range(LAST - 1):
-            n = 2 * b
+
+        def port_work(b):
             if b == 5:
                 nc.vector.quantize_mx(
                     out=wo_codes[:].bitcast(X4), scales=wo_scales[:], in_=wo_words[:].rearrange("p e j -> p (e j)")
@@ -387,52 +396,42 @@ def tile_volterrathirdordermixer_t_kernel(tc, x_bytes, x_scale, mp, mq, mr, coef
             widen_rest(b + 2)
             quantize_x(b + 1)
             interleave_x_gpsimd(b + 2)
-            if b + 2 < LAST:
-                widen("scalar", b + 3, 1)
-            if 1 <= b < LAST - 2:
+
+        for b in range(LAST - 2):
+            n = 2 * b
+            port_work(b)
+            widen("scalar", b + 3, 1)
+            if b >= 1:
                 if b - 1 == LAST - 4:
                     z_words[b - 1] = pair_words[:, 0, :]
                 else:
                     words = z_pool.tile([P, 4 * T], BF16, name="z_words", align_bytes=64)
                     z_words[b - 1] = words[:]
                 turn_z(b - 1)
-            if b < LAST - 2:
-                turn_x(b + 2)
-                fetch_x(b + 2)
-            else:
-                turn_x(b + 2, "R1")
-                fetch_x(b + 2)
-            if 1 <= b < LAST - 2:
+            turn_x(b + 2)
+            fetch_x(b + 2)
+            if b >= 1:
                 fetch_z(b - 1)
             for k in (n + 2, n + 3):
                 products(k, "R")
             for k in (n + 2, n + 3):
                 third_order(k)
-            if b == LAST - 2:
-                emit("O")
-                emit("Z")
-            for k in (n, n + 1):
-                times_q(k)
-                products(k + 2, "Q")
+            step_q(n)
+            step_q(n + 1)
             if b == 3:
                 z_tile["wo"], z_words["wo"] = wo_rows, wo_words[:].rearrange("p e j -> p (e j)")
                 turn_z("wo", bank="O")
                 fetch_z("wo")
-            elif 6 <= b < LAST - 3 and b % 3 == 1:
-                emit()
-            elif b == LAST - 3:
+            elif b == LAST - 3 or (b >= 6 and b % 3 == 1):
                 emit("O")
-                emit("Z")
-            elif b == LAST - 2:
-                emit("R1")
             if b + 4 < NB:
                 widen("scalar", b + 4, 0)
                 widen("scalar", b + 4, 2, 0, scalar_share(b + 4))
-            for k in (n, n + 1):
-                times_p(k)
-                products(k + 2, "P")
-                if b == LAST - 2 and k == n:
-                    emit("O")
+            step_p(n)
+            if b == LAST - 3:
+                emit("R0")
+                emit("Z")
+            step_p(n + 1)
 
         half_words, half_sums = [], []
 
@@ -473,6 +472,22 @@ def tile_volterrathirdordermixer_t_kernel(tc, x_bytes, x_scale, mp, mq, mr, coef
                 copy(out=half_sb[:, cols], in_=half_ps[:])
             nc.sync.dma_start(out=out[LAST].rearrange("(p c) e -> p c e", c=2)[:, c, :], in_=half_sb[:])
 
+        n = 2 * (LAST - 2)
+        port_work(LAST - 2)
+        turn_x(LAST, "R1")
+        fetch_x(LAST)
+        emit("O")
+        products(n + 2, "R")
+        step_q(n)
+        products(n + 3, "R")
+        third_order(n + 2)
+        third_order(n + 3)
+        emit("Z")
+        step_q(n + 1)
+        emit("O")
+        step_p(n)
+        step_p(n + 1)
+
         n = 2 * (LAST - 1)
         quantize_z(LAST - 4)
         quantize_x(LAST)
@@ -484,6 +499,8 @@ def tile_volterrathirdordermixer_t_kernel(tc, x_bytes, x_scale, mp, mq, mr, coef
             out=words[:, :, :split].rearrange("p b (c i) j -> p b c j i", i=8),
             in_=rows[:, :, :split].rearrange("p b (c i) j -> p b c j i", i=8),
         )
+        products(n + 2, "R")
+        third_order(n + 2)
         pair_turned = psum.tile([P, 2, T - split, 4], BF16, name="pair_turned", tag="Z")
         for u in range(2):
             nc.tensor.matmul(
@@ -494,19 +511,15 @@ def tile_volterrathirdordermixer_t_kernel(tc, x_bytes, x_scale, mp, mq, mr, coef
                 stop=True,
             )
         nc.scalar.copy(out=words[:, :, split:], in_=pair_turned[:])
-        products(n + 2, "R")
         products(n + 3, "R")
-        third_order(n + 2)
         third_order(n + 3)
-        times_q(n)
-        products(n + 2, "Q")
-        emit("Z")
-        times_q(n + 1)
-        products(n + 3, "Q")
         emit("O")
-        times_p(n)
-        products(n + 2, "P")
+        step_q(n)
+        emit("Z")
+        step_q(n + 1)
+        step_p(n)
         emit("R0")
+        emit("R1")
         times_p(n + 1)
         z_words[LAST - 3], z_words[LAST - 2] = pair_words[:, 0, :], pair_words[:, 1, :]
         z_words[LAST - 1] = pair_words[:, 0, :]
@@ -515,7 +528,7 @@ def tile_volterrathirdordermixer_t_kernel(tc, x_bytes, x_scale, mp, mq, mr, coef
         quantize_z(LAST - 2)
         waiting.extend([LAST - 3, LAST - 2])
         products(n + 3, "P")
-        for bank in ("R1", "Z", "O"):
+        for bank in ("O", "Z"):
             emit(bank)
 
         n = 2 * LAST

from contextlib import ExitStack

import concourse.mybir as mybir
from concourse.masks import make_identity

NB, S, D, T, E = 16, 512, 512, 256, 256
P = 128
FLOPS = NB * (2 * 3 * T * S * D + 2 * T * D * E)

F32 = mybir.dt.float32
BF16 = mybir.dt.bfloat16
U32 = mybir.dt.uint32
U8 = mybir.dt.uint8
FP8 = mybir.dt.float8_e4m3fn
X4 = mybir.dt.float8_e4m3fn_x4
COPY = mybir.ActivationFunctionType.Copy
IDENTITY = mybir.ActivationFunctionType.Identity
ADD = mybir.AluOpType.add
MULT = mybir.AluOpType.mult

SINGLE = 4
LAST = NB - 1
PITCH = D + 24
BLOCKS = 15
RUN = 4


def scalar_share(b):
    return {2: D}.get(b, 432)


def tile_volterrathirdordermixer_t_kernel(tc, x_bytes, x_scale, mp, mq, mr, coef, gain, wo, out):
    nc = tc.nc
    with ExitStack() as ctx:
        const = ctx.enter_context(tc.tile_pool(name="const", bufs=1))
        bytes_pool = ctx.enter_context(tc.tile_pool(name="bytes_pool", bufs=8))
        wide_pool = ctx.enter_context(tc.tile_pool(name="wide_pool", bufs=4))
        xq_pool = ctx.enter_context(tc.tile_pool(name="xq_pool", bufs=5))
        poly = ctx.enter_context(tc.tile_pool(name="poly", bufs=4))
        z_pool = ctx.enter_context(tc.tile_pool(name="z_pool", bufs=4))
        zq_pool = ctx.enter_context(tc.tile_pool(name="zq_pool", bufs=1))
        out_pool = ctx.enter_context(tc.tile_pool(name="out_pool", bufs=8))
        psum = ctx.enter_context(tc.psum_pool(name="psum", bufs=1))
        ctx.enter_context(tc.manual_schedule())

        x_raw = {}

        def load_x(b, width):
            codes = bytes_pool.tile([P, width, 4 * D], U8, name="codes%d" % width, align_bytes=64)
            nc.sync.dma_start(out=codes[:], in_=x_bytes[b : b + width].rearrange("k (p t) d -> p k (t d)", t=4))
            for k in range(width):
                x_raw[b + k] = codes[:, k, :]

        scale = const.tile([P, 4], F32, name="scale", align_bytes=64)
        m_raw = {}

        def load_m(i):
            m_rows = const.tile([P, 2, S], BF16, name="m_rows%d" % i, align_bytes=64)
            nc.sync.dma_start(out=m_rows[:], in_=(mr, mq, mp)[i].rearrange("(p c) k -> p c k", c=2))
            m_raw[i] = m_rows

        vec_rows = const.tile([P, 3, 32], BF16, name="vec_rows", align_bytes=64)
        nc.vector.memset(vec_rows[:], 0.0)

        def load_vectors():
            nc.sync.dma_start(out=vec_rows[0:16, 0:2, :], in_=coef.rearrange("v (g c) -> g v c", c=32))
            nc.sync.dma_start(out=vec_rows[0:16, 2, :], in_=gain.rearrange("(g c) -> g c", c=32))

        wo_rows = const.tile([P, 4, E], BF16, name="wo_rows", align_bytes=64)

        def load_wo():
            for i in range(8):
                nc.sync.dma_start(out=wo_rows[i:P:8, :, :], in_=wo.rearrange("(g j i) e -> i g j e", j=4, i=8)[i])

        def load_scale():
            nc.sync.dma_start(out=scale[:], in_=x_scale.rearrange("o (p t) z -> p (o t z)", t=4))

        load_scale()
        load_x(0, 1)
        load_x(1, 1)
        load_vectors()
        load_m(0)
        load_m(1)
        load_x(2, 1)
        load_m(2)
        load_x(3, 1)
        load_x(SINGLE, 2)
        load_wo()
        for b in range(SINGLE + 2, NB, 2):
            load_x(b, 2)

        ident_f32 = const.tile([P, P], F32, name="ident_f32", align_bytes=64)
        make_identity(nc, ident_f32[:])
        ident_bf16 = const.tile([P, P], BF16, name="ident_bf16", align_bytes=64)
        nc.scalar.activation(out=ident_bf16[:], in_=ident_f32[:], func=COPY)
        spread = const.tile([P, 16, 8], BF16, name="spread", align_bytes=64)
        nc.vector.tensor_copy(out=spread[:], in_=ident_f32[:, 0:16].unsqueeze(2).to_broadcast([P, 16, 8]))
        pick = const.tile([P, 8], F32, name="pick", align_bytes=64)
        nc.vector.tensor_reduce(
            out=pick[:], in_=ident_f32[:].rearrange("p (g i) -> p i g", i=8), axis=mybir.AxisListType.X, op=ADD
        )

        x_wide, x_words, x_codes, x_scales, x_turned = {}, {}, {}, {}, {}
        word_buffers = []
        for k in range(2):
            buffer = const.tile([P, 4 * D], BF16, name="x_words%d" % k, align_bytes=64)
            word_buffers.append(buffer)

        def widen(engine, b, t, first=0, last=D):
            if b not in x_wide:
                wide = wide_pool.tile([P, 4, PITCH], BF16, name="wide", align_bytes=64)
                x_wide[b] = wide[:, :, :D]
            dst = x_wide[b][:, t, first:last]
            src = x_raw[b][:, t * D + first : t * D + last].bitcast(FP8)
            if engine == "scalar":
                nc.scalar.activation(out=dst, in_=src, func=COPY, scale=scale[:, t : t + 1])
            else:
                nc.vector.tensor_scalar(out=dst, in0=src, scalar1=scale[:, t : t + 1], scalar2=None, op0=MULT)

        def widen_rest(b):
            if scalar_share(b) < D:
                widen("vector", b, 2, scalar_share(b))
            widen("vector", b, 3, max(0, scalar_share(b) - D))

        def new_x_words(b):
            words = word_buffers[b % 2][:]
            codes = xq_pool.tile([P, D], U32, name="x_q", align_bytes=64)
            scales = xq_pool.tile([P, D], U8, name="x_qs", align_bytes=64)
            x_words[b], x_codes[b], x_scales[b] = words, codes, scales

        def interleave_x_vector(b, j0, j1):
            nc.vector.tensor_copy(
                out=x_words[b].rearrange("p (j g i t) -> p g j t i", j=4, g=16, i=8, t=4)[:, :, j0:j1],
                in_=x_wide[b].rearrange("p t (g j i) -> p g j t i", g=16, j=4, i=8)[:, :, j0:j1],
            )

        def interleave_x_gpsimd(b):
            nc.gpsimd.tensor_copy(
                out=x_words[b].rearrange("p (j g i t) -> p g j t i", j=4, g=16, i=8, t=4)[:, :BLOCKS],
                in_=x_wide[b].rearrange("p t (g j i) -> p g j t i", g=16, j=4, i=8)[:, :BLOCKS],
            )

        def turn_x(b, bank="O"):
            first = 32 * BLOCKS
            turned = psum.tile([P, D - first, 4], BF16, name="x_turned", tag=bank)
            for u in range(2):
                nc.tensor.matmul(
                    turned[:, :, 2 * u : 2 * u + 2],
                    lhsT=ident_bf16[:],
                    rhs=x_wide[b][:, 2 * u : 2 * u + 2, first:].rearrange("p t d -> p d t"),
                    start=True,
                    stop=True,
                )
            x_turned[b] = turned

        def fetch_x(b):
            nc.scalar.copy(
                out=x_words[b].rearrange("p (j g w) -> p g j w", j=4, g=16)[:, BLOCKS :],
                in_=x_turned[b][:].rearrange("p (g j i) t -> p g j (i t)", j=4, i=8),
            )

        def quantize_x(b, j0=0, j1=4):
            cols = slice(j0 * P, j1 * P)
            nc.vector.quantize_mx(
                out=x_codes[b][:, cols].bitcast(X4),
                scales=x_scales[b][:, cols],
                in_=x_words[b][:, 4 * j0 * P : 4 * j1 * P],
            )

        m_turned, m_words, m_codes, m_scales = [], [], [], []

        def turn_m(i):
            turned = psum.tile([P, 2, 2, P], F32, name="turned", tag="RQP"[i] + "1")
            for c in range(2):
                words = m_raw[i][:, c, :].bitcast(F32)
                for u in range(2):
                    nc.tensor.transpose(turned[:, c, u, :], words[:, u : S // 2 : 2], ident_f32[:])
            m_turned.append(turned)

        def fetch_m(i):
            turned = m_turned[i]
            grouped = const.tile([P, T, 4], BF16, name="m_words%d" % i, align_bytes=64)
            dst = grouped[:].rearrange("p n t -> p (n t)").bitcast(F32)
            nc.scalar.copy(
                out=dst.rearrange("p (c n u) -> p c n u", c=2, u=2), in_=turned[:].rearrange("p c u n -> p c n u")
            )
            m_words.append(grouped)

        def quantize_m(i):
            codes = const.tile([P, T], U32, name="m_q%d" % i, align_bytes=64)
            scales = const.tile([P, T], U8, name="m_qs%d" % i, align_bytes=64)
            nc.vector.quantize_mx(
                out=codes[:].bitcast(X4), scales=scales[:], in_=m_words[i][:].rearrange("p n t -> p (n t)")
            )
            m_codes.append(codes)
            m_scales.append(scales)

        sums, h_val, u_val, z_tile = {}, {}, {}, {}
        pair_rows = const.tile([P, 2, 4, T], BF16, name="pair_rows", align_bytes=64)

        def units(n):
            if n // 2 == LAST:
                c = n % 2
                return [(j, slice(c * P, (c + 1) * P), slice(j * P, (j + 1) * P)) for j in range(4)]
            return [(2 * (n % 2) + k, slice(0, T), slice(k * T, (k + 1) * T)) for k in range(2)]

        def products(n, name):
            b = n // 2
            i = "RQP".index(name)
            ps = psum.tile([P, 2 * T], F32, name="sum_ps", tag=name + "01"[n % 2])
            for j, times, bank in units(n):
                cols = slice(j * P, (j + 1) * P)
                nc.tensor.matmul_mx(
                    out=ps[:, bank],
                    lhsT=x_codes[b][:, cols].bitcast(X4),
                    lhsT_scale=x_scales[b][:, cols],
                    rhs=m_codes[i][:, times].bitcast(X4),
                    rhs_scale=m_scales[i][:, times],
                    start=True,
                    stop=True,
                )
            sums[name, n] = ps

        def third_order(n):
            h = poly.tile([P, 2 * T], F32, name="h", align_bytes=64)
            for j, times, bank in units(n):
                nc.scalar.activation(
                    out=h[:, bank],
                    in_=sums["R", n][:, bank],
                    func=IDENTITY,
                    bias=gain_coef[:, j : j + 1],
                    scale=gain_coef[:, 4 + j : 5 + j],
                )
            h_val[n] = h

        def times_q(n):
            u = poly.tile([P, 2 * T], F32, name="u", align_bytes=64)
            nc.vector.tensor_tensor(out=u[:], in0=h_val[n][:], in1=sums["Q", n][:], op=MULT)
            u_val[n] = u

        def times_p(n):
            b = n // 2
            if b in (LAST - 3, LAST - 2):
                z_tile[b] = pair_rows[:, b - (LAST - 3)]
            elif n % 2 == 0:
                z_rows = z_pool.tile([P, 4, T], BF16, name="z_rows", align_bytes=64)
                z_tile[b] = z_rows
            for j, times, bank in units(n):
                nc.vector.scalar_tensor_tensor(
                    out=z_tile[b][:, j, times],
                    in0=u_val[n][:, bank],
                    scalar=vec_cols[:, 8 + j : 9 + j],
                    in1=sums["P", n][:, bank],
                    op0=ADD,
                    op1=MULT,
                )

        z_turned, z_words, z_codes, z_scales, out_sum = {}, {}, {}, {}, {}

        def turn_z(b, first=0, bank="Z"):
            turned = psum.tile([P, T, 4], BF16, name="z_turned", tag=bank)
            for u in range(2):
                nc.tensor.matmul(
                    turned[:, first * P :, 2 * u : 2 * u + 2],
                    lhsT=ident_bf16[:],
                    rhs=z_tile[b][:, 2 * u : 2 * u + 2, first * P :].rearrange("p j t -> p t j"),
                    start=True,
                    stop=True,
                )
            z_turned[b] = turned

        def fetch_z(b, first=0):
            nc.scalar.copy(
                out=z_words[b][:, 4 * first * P :], in_=z_turned[b][:, first * P :, :].rearrange("p t j -> p (t j)")
            )

        def interleave_z_gpsimd(b):
            nc.gpsimd.tensor_copy(
                out=z_words[b].rearrange("p (c i j) -> p c j i", i=8, j=4),
                in_=z_tile[b][:].rearrange("p j (c i) -> p c j i", i=8),
            )

        def quantize_z(b):
            codes = zq_pool.tile([P, T], U32, name="z_q%d" % b, align_bytes=64)
            scales = zq_pool.tile([P, T], U8, name="z_qs%d" % b, align_bytes=64)
            nc.vector.quantize_mx(out=codes[:].bitcast(X4), scales=scales[:], in_=z_words[b])
            z_codes[b], z_scales[b] = codes, scales

        def project(b, bank="O"):
            o_ps = psum.tile([P, 2, E], F32, name="o_ps", tag=bank)
            for c in range(2):
                cols = slice(c * P, (c + 1) * P)
                nc.tensor.matmul_mx(
                    out=o_ps[:, c, :],
                    lhsT=z_codes[b][:, cols].bitcast(X4),
                    lhsT_scale=z_scales[b][:, cols],
                    rhs=wo_codes[:].bitcast(X4),
                    rhs_scale=wo_scales[:],
                    start=True,
                    stop=True,
                )
            out_sum[b] = o_ps

        def store(b):
            o_sb = out_pool.tile([P, 2, E], F32, name="o_sb", align_bytes=64)
            nc.scalar.copy(out=o_sb[:], in_=out_sum[b][:])
            nc.sync.dma_start(out=out[b].rearrange("(p c) e -> p c e", c=2), in_=o_sb[:])

        vec_cols = const.tile([P, 12], F32, name="vec_cols", align_bytes=64)
        gain_coef = const.tile([P, 8], F32, name="gain_coef", align_bytes=64)
        vec_ps = psum.tile([P, 12, 8], F32, name="vec_ps", tag="O")
        vec_picked = const.tile([P, 12, 8], F32, name="vec_picked", align_bytes=64)
        wo_codes = const.tile([P, E], U32, name="wo_q", align_bytes=64)
        wo_scales = const.tile([P, E], U8, name="wo_qs", align_bytes=64)
        widen("vector", 0, 0)
        widen("vector", 0, 1)
        widen("scalar", 0, 2)
        widen("vector", 0, 3)
        widen("vector", 1, 3)
        nc.tensor.matmul(
            vec_ps[:].rearrange("p w i -> p (w i)"),
            lhsT=spread[:].rearrange("p g i -> p (g i)"),
            rhs=vec_rows[:].rearrange("p v c -> p (v c)"),
            start=True,
            stop=True,
        )
        turn_m(0)
        turn_m(1)
        turn_m(2)
        for t in (0, 1, 2):
            widen("scalar", 1, t)
        fetch_m(0)
        widen("scalar", 2, 0)
        fetch_m(1)
        widen("scalar", 2, 1)
        fetch_m(2)
        new_x_words(0)
        interleave_x_vector(0, 0, 2)
        interleave_x_vector(0, 2, 4)
        nc.vector.tensor_tensor(
            out=vec_picked[:], in0=vec_ps[:], in1=pick[:].unsqueeze(1).to_broadcast([P, 12, 8]), op=MULT
        )
        quantize_x(0, 0, 2)
        quantize_x(0, 2, 4)
        nc.vector.tensor_reduce(out=vec_cols[:], in_=vec_picked[:], axis=mybir.AxisListType.X, op=ADD)
        new_x_words(1)
        interleave_x_vector(1, 0, 1)
        nc.vector.tensor_tensor(
            out=gain_coef[:].rearrange("p (v j) -> p v j", v=2),
            in0=vec_cols[:, 0:8].rearrange("p (v j) -> p v j", v=2),
            in1=vec_cols[:, 8:12].unsqueeze(1).to_broadcast([P, 2, 4]),
            op=MULT,
        )
        quantize_m(0)
        interleave_x_vector(1, 1, 4)
        quantize_m(1)
        products(0, "R")
        products(1, "R")
        products(0, "Q")
        products(1, "Q")
        widen("vector", 2, 2)
        third_order(0)
        third_order(1)
        quantize_m(2)
        products(0, "P")
        products(1, "P")
        widen("scalar", 3, 0)
        widen("scalar", 3, 2, 0, scalar_share(3))

        waiting = []

        def emit(bank):
            project(waiting[0], bank)
            store(waiting.pop(0))

        def step_q(n):
            times_q(n)
            products(n + 2, "Q")

        def step_p(n):
            times_p(n)
            products(n + 2, "P")

        pair_words = const.tile([P, 2, 4 * T], BF16, name="pair_words", align_bytes=64)
        wo_words = const.tile([P, E, 4], BF16, name="wo_words", align_bytes=64)

        def port_work(b):
            if b == 5:
                nc.vector.quantize_mx(
                    out=wo_codes[:].bitcast(X4), scales=wo_scales[:], in_=wo_words[:].rearrange("p e j -> p (e j)")
                )
            if b >= 3:
                quantize_z(b - 3)
                waiting.append(b - 3)
            new_x_words(b + 2)
            widen_rest(b + 2)
            quantize_x(b + 1)
            interleave_x_gpsimd(b + 2)

        for b in range(LAST - 2):
            n = 2 * b
            port_work(b)
            widen("scalar", b + 3, 1)
            if b >= 1:
                if b - 1 == LAST - 4:
                    z_words[b - 1] = pair_words[:, 0, :]
                else:
                    words = z_pool.tile([P, 4 * T], BF16, name="z_words", align_bytes=64)
                    z_words[b - 1] = words[:]
                turn_z(b - 1)
            turn_x(b + 2)
            fetch_x(b + 2)
            if b >= 1:
                fetch_z(b - 1)
            for k in (n + 2, n + 3):
                products(k, "R")
            for k in (n + 2, n + 3):
                third_order(k)
            step_q(n)
            step_q(n + 1)
            if b == 3:
                z_tile["wo"], z_words["wo"] = wo_rows, wo_words[:].rearrange("p e j -> p (e j)")
                turn_z("wo", bank="O")
                fetch_z("wo")
            elif b == LAST - 3 or (b >= 6 and b % 3 == 1):
                emit("O")
            if b + 4 < NB:
                widen("scalar", b + 4, 0)
                widen("scalar", b + 4, 2, 0, scalar_share(b + 4))
            step_p(n)
            if b == LAST - 3:
                emit("R0")
                emit("Z")
            step_p(n + 1)

        half_words, half_sums = [], []

        def interleave_half(c):
            words = zq_pool.tile([P, P, 4], BF16, name="half_words%d" % c, align_bytes=64)
            nc.vector.tensor_copy(
                out=words[:].rearrange("p (c i) j -> p c j i", i=RUN),
                in_=z_tile[LAST][:, :, c * P : (c + 1) * P].rearrange("p j (c i) -> p c j i", i=RUN),
            )
            half_words.append(words)

        def project_half(c, banks):
            codes = zq_pool.tile([P, P], U32, name="half_q%d" % c, align_bytes=64)
            scales = zq_pool.tile([P, P], U8, name="half_qs%d" % c, align_bytes=64)
            nc.vector.quantize_mx(
                out=codes[:].bitcast(X4), scales=scales[:], in_=half_words[c][:].rearrange("p t j -> p (t j)")
            )
            width = E // len(banks)
            parts = []
            for k, bank in enumerate(banks):
                cols = slice(k * width, (k + 1) * width)
                half_ps = psum.tile([P, width], F32, name="half_ps", tag=bank)
                nc.tensor.matmul_mx(
                    out=half_ps[:],
                    lhsT=codes[:].bitcast(X4),
                    lhsT_scale=scales[:],
                    rhs=wo_codes[:, cols].bitcast(X4),
                    rhs_scale=wo_scales[:, cols],
                    start=True,
                    stop=True,
                )
                parts.append((cols, half_ps))
            half_sums.append(parts)

        def store_half(c, copies):
            half_sb = out_pool.tile([P, E], F32, name="half_sb%d" % c, align_bytes=64)
            for copy, (cols, half_ps) in zip(copies, half_sums[c]):
                copy(out=half_sb[:, cols], in_=half_ps[:])
            nc.sync.dma_start(out=out[LAST].rearrange("(p c) e -> p c e", c=2)[:, c, :], in_=half_sb[:])

        n = 2 * (LAST - 2)
        port_work(LAST - 2)
        turn_x(LAST, "R1")
        fetch_x(LAST)
        emit("O")
        products(n + 2, "R")
        step_q(n)
        products(n + 3, "R")
        third_order(n + 2)
        third_order(n + 3)
        emit("Z")
        step_q(n + 1)
        emit("O")
        step_p(n)
        step_p(n + 1)

        n = 2 * (LAST - 1)
        quantize_z(LAST - 4)
        quantize_x(LAST)
        waiting.append(LAST - 4)
        split = T * 7 // 8
        rows = pair_rows[:].rearrange("p b j t -> p b t j")
        words = pair_words[:].rearrange("p b (t j) -> p b t j", j=4)
        nc.gpsimd.tensor_copy(
            out=words[:, :, :split].rearrange("p b (c i) j -> p b c j i", i=8),
            in_=rows[:, :, :split].rearrange("p b (c i) j -> p b c j i", i=8),
        )
        products(n + 2, "R")
        third_order(n + 2)
        pair_turned = psum.tile([P, 2, T - split, 4], BF16, name="pair_turned", tag="Z")
        for u in range(2):
            nc.tensor.matmul(
                pair_turned[:, :, :, 2 * u : 2 * u + 2],
                lhsT=ident_bf16[:],
                rhs=rows[:, :, split:, 2 * u : 2 * u + 2],
                start=True,
                stop=True,
            )
        nc.scalar.copy(out=words[:, :, split:], in_=pair_turned[:])
        products(n + 3, "R")
        third_order(n + 3)
        emit("O")
        step_q(n)
        emit("Z")
        step_q(n + 1)
        step_p(n)
        emit("R0")
        emit("R1")
        times_p(n + 1)
        z_words[LAST - 3], z_words[LAST - 2] = pair_words[:, 0, :], pair_words[:, 1, :]
        z_words[LAST - 1] = pair_words[:, 0, :]
        quantize_z(LAST - 3)
        interleave_z_gpsimd(LAST - 1)
        quantize_z(LAST - 2)
        waiting.extend([LAST - 3, LAST - 2])
        products(n + 3, "P")
        for bank in ("O", "Z"):
            emit(bank)

        n = 2 * LAST
        times_q(n)
        times_q(n + 1)
        times_p(n)
        quantize_z(LAST - 1)
        project(LAST - 1, "P0")
        store(LAST - 1)
        times_p(n + 1)
        for c in range(2):
            interleave_half(c)
        project_half(0, ("Q0",))
        project_half(1, ("Q1", "P1"))
        store_half(0, (nc.scalar.copy,))
        store_half(1, (nc.scalar.copy, nc.vector.tensor_copy))
